import numpy as np, ml_dtypes
CORES = [24,25,26,27,28,29,30,31]
N = 8
import mx_ref
BF = ml_dtypes.bfloat16
def gentries(a):
    return np.ascontiguousarray(a.reshape(8, 16, -1).transpose(0, 2, 1)).reshape(8, -1)
def gtable(e):
    e = np.asarray(e); return np.ascontiguousarray(e.reshape(8, -1, 16).transpose(0, 2, 1)).reshape(128, -1).astype(np.int32)
def gcols(t, e):
    v = np.concatenate([t.reshape(8, 16, -1, 4), np.zeros((8, 16, 1, 4), BF)], axis=2)
    return np.ascontiguousarray(np.stack([v[g][:, e[g]] for g in range(8)])).reshape(128, -1)
def tile(rs):
    return np.stack(rs, axis=2).reshape(128, -1).astype(BF)
def pick(q, e):
    c = np.concatenate([q[0].reshape(128, -1, 4), np.zeros((128, 1, 4), np.uint8)], axis=1); s = np.concatenate([q[1], np.ones((16, 1), np.uint8)], axis=1)
    return (np.ascontiguousarray(c[:, e].reshape(128, -1)), np.ascontiguousarray(s[:, e]))
def join(*qs):
    return (np.concatenate([q[0] for q in qs], axis=1), np.concatenate([q[1] for q in qs], axis=1))
def put(q, e, v):
    c, s = q[0].reshape(128, -1, 4).copy(), q[1].copy(); c[:, e] = v[0].reshape(128, -1, 4); s[:, e] = v[1]
    return (c.reshape(128, -1), s)
def pk(c, s):
    return (np.ascontiguousarray(c), mx_ref.live(s))
def emit(q):
    return q[0], q[1]
def packed(v, rng):
    q = [mx_ref.quantize(np.ascontiguousarray(v[r])) for r in range(N)]
    return np.stack([a for a, b in q]), np.stack([mx_ref.plane(b, rng) for a, b in q])
def values_of_codes():
    e, c = np.zeros((128, 128, 4), np.float32), np.zeros((128, 2, 4), np.uint8)
    e[np.arange(128), np.arange(128), 0] = 1
    c[:127, :, 0] = np.arange(256).reshape(2, 128).T[:127]
    return mx_ref.matmul(mx_ref.quantize(e.reshape(128, 512).astype(BF)), (c.reshape(128, 8), np.full((16, 2), 127, np.uint8))).T.reshape(-1).astype(np.float64)
CODE_VALUE, SCALE_VALUE = values_of_codes(), 2.0 ** (np.arange(256) - 127.0)
def decode(q):
    return (CODE_VALUE[q[0]].reshape(16, 8, -1, 4) * SCALE_VALUE[q[1]][:, None, :, None] + 0.0).reshape(128, -1).astype(np.float32)
def f(rng, *shape):
    return mx_ref.flush((rng.standard_normal(shape, dtype=np.float32) * np.exp2(rng.integers(-2, 3, shape[:-1] + (1,)))).astype(BF))
def wide(rng, *shape, cols=0):
    v = rng.standard_normal(shape, dtype=np.float32) * np.exp2(rng.integers(-12, 13, shape)).astype(np.float32)
    if cols: v *= np.repeat(np.exp2(rng.integers(-cols, cols + 1, shape[:-2] + (1, shape[-1] // 4))) * (rng.random(shape[:-2] + (1, shape[-1] // 4)) > 0.0625), 4, axis=-1).astype(np.float32)
    return mx_ref.flush(v.astype(BF))
C, H, R = 256, 96, 3
def numbers_of(rng):
    return {"x": np.array(f(rng, N, 128, 4 * C)), "u": np.array(f(rng, N, 128, 512)), "v": np.array(f(rng, N, 128, 512))}
def orders(rng):
    return np.argsort(rng.random((N, 8, C)), axis=2)
def bonds(e):
    return np.stack([gtable(e[r]) for r in range(N)])
def layers(rng, still=()):
    w = np.array(f(rng, N, 128, 2048)).reshape(N, 8, 16, 4, 8, 16, 4)
    for i in still:
        w[:, :, i] = 0
        w[:, :, :, :, :, i] = 0
    return w
def weights(rng, w):
    c, p = packed(np.ascontiguousarray(w).reshape(N, 128, 2048), rng)
    return {"wc": c, "ws": p}
def chosen(rng, n):
    k, a = np.arange(8 * n), np.zeros((8, C), bool)
    a[k % 8, k // 4] = True
    return a[:, rng.permutation(C)]
def crowd(rng):
    n, o = H + 1, rng.permutation(C)
    full, half, none, rest = o[:48], o[48:48 + n], o[48 + n:48 + 2 * n], o[48 + 2 * n:]
    a, e = np.zeros((8, C), bool), np.zeros((8, C), np.int64)
    a[:, full] = True
    for j in range(n): a[(j + 1 + rng.permutation(7)[:4]) % 8, half[j]] = True
    for g in range(8):
        b = np.concatenate([half[g::8], rng.permutation(np.delete(half, np.arange(g, n, 8)))])
        e[g, none] = rng.permutation(half)
        e[g, b[:48]] = rng.permutation(full)
        e[g, np.concatenate([b[48:], full])] = rng.permutation(none)
        e[g, rest] = rng.permutation(rest)
    return a, e
def faint():
    k = 2.0 ** -np.arange(4.0, 28.0)
    t = np.zeros((128, 24, 4), np.float32)
    t[0, :, 0] = 1.96875
    t[7, :, 0] = k
    once = decode(mx_ref.quantize(t.reshape(128, 96).astype(BF)))
    again = decode(mx_ref.quantize(once.astype(BF)))
    i = int(np.argmax((once[7, ::4] > 0) & (again[7, ::4] == 0)))
    assert once[7, 4 * i] == k[i] and again[7, 4 * i] == 0
    return k[i]
def plant(d, s):
    x = d["x"].reshape(N, 8, 16, C, 4)
    x[:, :, 0] = 0
    x[:, :, 0, :, 0] = s.astype(np.float32).astype(BF)
    u = d["u"].reshape(N, 128, 128, 4)
    u[:, :, ::16] = 0
    for h in range(0, 128, 16): u[:, h, h, 0] = 1
def setup_inputs(rng):
    return {**numbers_of(rng), "m": bonds(orders(rng)), **weights(rng, layers(rng))}
def setup_inputs_slots(rng):
    d = numbers_of(rng)
    e, s, c, h = orders(rng), np.zeros((N, 8, C)), int(rng.integers(4)), H // 2
    for r in range(N):
        k = (r + c) % 4
        if k == 0:
            a = chosen(rng, H)
            for g in rng.permutation(8)[:4]: a[g, rng.choice(np.flatnonzero(a[g]))] = False
        elif k == 1: a = chosen(rng, H + 1)
        elif k == 2:
            o = rng.permutation(C)
            a = np.zeros((8, C), bool)
            a[:, o[:h]] = True
            for g in range(8):
                e[r, g, o[h:2 * h]] = rng.permutation(o[:h])
                e[r, g, o[2 * h:3 * h]] = rng.permutation(o[h:2 * h])
                e[r, g, o[:h]] = rng.permutation(o[2 * h:3 * h])
                e[r, g, o[3 * h:]] = rng.permutation(o[3 * h:])
        else: a, e[r] = crowd(rng)
        s[r] = np.where(a, 1.0, -1.0 * rng.integers(0, 2, (8, C)))
    plant(d, s)
    x = d["x"].reshape(N, 8, 16, C, 4)
    x[:, :, 8:11] = 0
    x[:, :, 8, :, 0] = 1
    u = d["u"].reshape(N, 128, 128, 4)
    for i in range(0, 128, 16): u[:, i + 10, i, 0] = 1
    w, o = layers(rng, (0, 8, 9, 10)), rng.permutation(8)
    w[:, :, 8, 0, :, 9, 0] = 4
    for r in range(N):
        for j in range(8): w[r, :, 9, 0, o[(2 * r + j) % 8], 10, 0] = 512 if j < 4 else -512
    return {**d, "m": bonds(e), **weights(rng, w)}
def setup_inputs_near(rng):
    d = numbers_of(rng)
    x = d["x"].astype(np.float32).reshape(N, 8, 16, C, 4)
    x[:, :, :2] = 0
    x[:, :, 8:] = 0
    c = rng.choice([-1.0, 1.0], (N, 8, C))
    a = rng.choice([-1.0, 0.0, 1.0, 1.0], (3, N, 8, C))
    x[:, :, 0, :, 0] = c
    x[:, :, 1, :, 0] = -c
    x[:, :, 8, :, 0] = a[0] * 2.0 ** -30
    x[:, :, 9, :, 0] = a[1] * 2.0 ** -23
    x[:, :, 10, :, 0] = a[2] * 1.125 * 2.0 ** -30
    x[:, :, 11, :, 0] = a[2] * -1.0 * 2.0 ** -30
    u = d["u"].reshape(N, 128, 128, 4)
    u[:, :, ::16] = 0
    o = rng.permutation(N) % 3
    for r in range(N):
        if o[r] == 0:
            for g in rng.permutation(8)[:4]: x[r, g, 8, rng.integers(C), 0] = 2.0 ** 30 * rng.choice([-1.0, 1.0])
        for h in range(0, 128, 16):
            if o[r] == 0: u[r, h + 8, h, 0] = 2.0 ** -30
            elif o[r] == 1:
                u[r, h + 10, h, 0] = 1.125 * 2.0 ** -30
                u[r, h + 11, h, 0] = 1.25 * 2.0 ** -30
            else:
                for i in (0, 1, 9): u[r, h + i, h, 0] = 1
    return {"x": x.reshape(N, 128, 4 * C).astype(BF), "u": d["u"], "v": d["v"], "m": bonds(orders(rng)), **weights(rng, layers(rng, (0, 1, 8, 9, 10, 11, 12, 13, 14, 15)))}
def setup_inputs_late(rng):
    d = numbers_of(rng)
    k = np.argsort(rng.random((N, 8, C)), axis=1)
    known = k < 4 + (rng.permutation(N) % 2)[:, None, None]
    plant(d, np.where(k == 0, 0.0, np.where(known, 1.0, -1.0)))
    x = d["x"].reshape(N, 8, 16, C, 4)
    n = (N, 8, 8, C, 4)
    a = (1 + (2 * rng.integers(0, 64, n) + 1) * 2.0 ** -7) * np.exp2(rng.integers(-14, -7, n))
    a[:, :, 0, :, 0] = 1.96875
    x[:, :, 8:] = (a * (2.0 * rng.integers(0, 2, n) - 1.0)).astype(np.float32).astype(BF)
    x[:, :, 15, :, 0] = np.where(k == 0, faint(), 0.0).astype(np.float32).astype(BF)
    u = d["u"].reshape(N, 128, 128, 4)
    for h in range(0, 128, 16): u[:, h + 15, h, 0] = 1
    return {**d, "m": bonds(orders(rng)), **weights(rng, layers(rng))}
def setup_inputs_ends(rng):
    d = numbers_of(rng)
    x, e, c, i = np.zeros((N, 8, 16, C, 4)), orders(rng), int(rng.integers(4)), np.arange(128)
    u, v = d["u"].reshape(N, 128, 128, 4), d["v"]
    u[:, :, ::16] = 0
    w = np.zeros((N, 128, 4, 128, 4), np.float32)
    for r in range(N):
        k = (r + c) % 4
        a = (0.75 + 0.25 * rng.random((8, 16, C, 4))) * 2.0 ** 30
        for j in range(4): w[r, i, j, i, j] = 2.0 ** -30
        if k == 0:
            x[r] = a * rng.choice([-1.0, 1.0], C)[:, None]
            s = np.where(rng.permutation(8) < 5, 1.0, -1.0)
            for g in range(8): u[r, :, 16 * g] = s[g] * 2.0 ** 30
            e[r] = np.arange(C)[::-1]
            v[r] = (2.0 ** 30 * rng.choice([-1.0, 1.0], (128, 512))).astype(np.float32).astype(BF)
            n = i[i % 16 < 8]
            for j in range(4): w[r, n, j, n, j] = -1
        elif k == 1:
            x[r] = (1 + 0.25 * rng.integers(0, 4, (8, 16, C, 4))) * 2.0 ** -30
            x[r, :, :8] *= 2.0
            u[r, :, ::16] = 2.0 ** -30
            e[r] = np.arange(C)
            v[r] = (2.0 ** -30 * rng.choice([-1.0, 1.0], (128, 512))).astype(np.float32).astype(BF)
        elif k == 2:
            x[r] = -a
            u[r, :, ::16] = 2.0 ** 30
        else:
            x[r] = a * np.where(chosen(rng, H), 1.0, -1.0)[:, None, :, None]
            for g in range(8): u[r, 16 * g:16 * g + 16, 16 * g] = 2.0 ** 30
            e[r] = rng.permutation(C)
    return {"x": x.astype(np.float32).reshape(N, 128, 4 * C).astype(BF), "u": d["u"], "v": v, "m": bonds(e), **weights(rng, w.astype(BF))}
def setup_inputs_spread(rng):
    d = setup_inputs(rng)
    d["x"] = wide(rng, N, 128, 4 * C, cols=6)
    return d
def check_inputs(d):
    b = []
    for k in ("x", "u", "v"):
        a = np.abs(d[k].astype(np.float32))
        if not (np.isfinite(a).all() and ((a == 0) | (a >= 2.0 ** -30) & (a <= 2.0 ** 30)).all()): b.append("a value of " + k)
    none, least, most = [emit(mx_ref.quantize(np.full((128, 16), k, np.float32).astype(BF)))[1][0, 0] for k in (0.0, 2.0 ** -30, 2.0 ** 30)]
    for r in range(N):
        if (np.sort(gentries(d["m"][r]), axis=1) != np.arange(C)).any(): b.append("m: a list that is no permutation")
        if ((d["wc"][r] == 0x7F) | (d["wc"][r] == 0xFF)).any(): b.append("wc: a code that is no number")
        s = mx_ref.live(d["ws"][r])
        if ((s != none) & ((s < least) | (s > most))).any(): b.append("ws: a scale out of range")
    return b
def waves(s, to):
    w = np.where(s > 0, 1, 4)
    for t in (2, 3):
        licensed = np.count_nonzero(w < 4, axis=0) >= 5
        w = np.where((w == 4) & licensed[to], t, w)
    return w
def reference(x, u, v, m, wc, ws):
    qu = [mx_ref.quantize(u[r]) for r in range(N)]
    lay = [pk(wc[r], ws[r]) for r in range(N)]
    now = [x[r] for r in range(N)]
    lists = np.stack([gentries(m[r]) for r in range(N)])
    for t in range(R):
        to = np.roll(lists, -t, axis=1)
        own, wave, sent = [], [], []
        for r in range(N):
            q = mx_ref.quantize(now[r])
            own.append(decode(q).astype(BF))
            wave.append(waves(mx_ref.matmul(qu[r], q)[::16], to[r]))
            o = np.argsort(np.where(wave[r] < 4, 3 - wave[r], 3), axis=1, kind="stable")[:, :H]
            e = np.where(np.take_along_axis(wave[r], o, axis=1) < 4, o, -1)
            sent.append(mx_ref.quantize(gcols(own[r], e)))
        for r in range(N):
            guests = decode(sent[(r - 1) % N]).astype(BF)
            k = np.argsort(np.argsort(wave[r] < 4, axis=1, kind="stable"), axis=1)
            e = np.where(wave[r] == 1, np.arange(C), np.where(wave[r] < 4, to[r], C + k % H))
            z = gcols(np.concatenate([own[r], guests], axis=1), e)
            q = mx_ref.quantize(z)
            made = tile([mx_ref.matmul(pick(lay[r], np.arange(128 * b, 128 * b + 128)), q) * np.float32(0.03125) + z[:, b::4].astype(np.float32) for b in range(4)])
            now[r] = gcols(made, np.argsort(to[r], axis=1))
    y, wv = np.zeros((N, 128, C), np.float32), np.zeros((N, 8, C), np.float32)
    oc, osc = np.zeros((N, 128, 4 * C), np.uint8), np.zeros((N, 16, C), np.uint8)
    for r in range(N):
        q = mx_ref.quantize(now[r])
        y[r] = mx_ref.matmul(mx_ref.quantize(v[r]), q)
        wv[r] = wave[r]
        oc[r], osc[r] = emit(q)
    return {"y": y, "wv": wv, "oc": oc, "osc": osc}

@@ -1,0 +1,346 @@
+from concourse.mybir import dt, AluOpType, ActivationFunctionType
+
+R = 3
+BIG = 512.0
+
+
+def _scratch():
+    s = {}
+
+    def sb(d, w, names):
+        for n in names.split():
+            s[n] = ("sbuf", [128, w], d)
+
+    for w, names in ((128, "u u16 v ta tb ft"), (256, "x c p z f0 f1 f2 h0 h1 h2"), (512, "w e")):
+        for n in names.split():
+            s["q" + n] = ("sbuf", [128, w], "float8_e4m3fn_x4")
+            s["s" + n] = ("sbuf", [128, w], "uint8")
+    sb("bfloat16", 2048, "et")
+    sb("bfloat16", 1408, "fg")
+    sb("bfloat16", 1024, "x0 z xt ct pt")
+    sb("bfloat16", 512, "zero u0 v0 ta tb ft sl")
+    sb("bfloat16", 272, "hp0 hp1 hp2 hp3")
+    sb("bfloat16", 256, "row msk rsI rs lic1 lic2 tbm d wa wb iv z320 z321 z322 z323 tt0 tt1 tt2 tt3")
+    sb("bfloat16", 128, "ones neg ident nb nb2 rr rr2")
+    sb("uint16", 16, "mo0 mo1 mo2 inv0 inv1 inv2 pos off0 off1 off2 off3")
+    sb("uint16", 6, "slot0 slot1 slot2 land0 land1 land2")
+    sb("uint16", 8, "pick8")
+    sb("int32", 8, "pick8i")
+    sb("int32", 16, "mi0 mi1 mi2 ipI")
+    sb("float32", 16, "ic leg m16")
+    sb("float32", 32, "m32")
+    sb("float32", 48, "mf")
+    sb("float32", 64, "cum pp")
+    sb("float32", 192, "ll")
+    sb("float32", 256, "wrow yb")
+    for n in "k0 k1 k2 k3 b0 b1 b2 b3".split():
+        s[n] = ("psum", [128, 512], "float32")
+    return s
+
+
+SCRATCH = _scratch()
+LOADS = ["u", "xa", "xb", "v", "wc", "ws", "m0", "m1", "m2", "inv"]
+SEMAPHORES = ["sV", "sT", "sA", "sG", "loc", "st", "st2"] + ["ld_" + n for n in LOADS] + ["ah0", "ah1", "ah2", "al0", "al1", "al2"]
+
+
+def rank_program(g, core, T, topo):
+    rank = T.rank_of(core)
+    if rank is None:
+        return
+    A = AluOpType
+    COPY = ActivationFunctionType.Copy
+    nxt = T.cores[(rank + 1) % len(T.cores)]
+    rid, pid = topo.addr(nxt)[0], topo.addr(nxt)[1]
+    mask, neng = topo.mask(core, nxt), len(topo.engines(core, nxt))
+    queues = {"V": g.vector, "T": g.tensor, "A": g.scalar, "G": g, "S": g.sync}
+    known = {q: {} for q in queues}
+    count, writer, readers = {}, {}, {}
+
+    def order(q, need):
+        best = {}
+        for e in need:
+            if known[q].get(e[0], 0) < e[1] and (e[0] not in best or best[e[0]][1] < e[1]):
+                best[e[0]] = e
+        for s in list(best):
+            if any(o != s and best[o][2].get(s, 0) >= best[s][1] for o in best):
+                del best[s]
+        for s in best:
+            _, v, c = best[s]
+            queues[q].wait_ge(T.sem[s], v)
+            for k in c:
+                known[q][k] = max(known[q].get(k, 0), c[k])
+            known[q][s] = max(known[q].get(s, 0), v)
+
+    def op(q, fn, r=(), w=(), sem=None, inc=1):
+        need = []
+        for k in r:
+            if k in writer:
+                need.append(writer[k])
+        for k in w:
+            if k in writer:
+                need.append(writer[k])
+            need += [e for qq, e in readers.get(k, {}).items() if qq != q]
+        order(q, need)
+        i = fn()
+        s = sem or "s" + q
+        i.then_inc(T.sem[s], inc)
+        count[s] = count.get(s, 0) + inc
+        c = dict(known[q])
+        c[s] = count[s]
+        e = (s, count[s], c)
+        for k in r:
+            readers.setdefault(k, {})[q] = e
+        for k in w:
+            writer[k] = e
+            readers[k] = {}
+
+    def V(fn, r="", w=""):
+        op("V", fn, r.split(), w.split())
+
+    def act(out, in_, r, w, **kw):
+        op("A", lambda: g.scalar.activation(out, in_, COPY, **kw), r.split(), w.split())
+
+    def ts(out, in0, s1, s2, op0, op1=None):
+        if op1 is None:
+            return lambda: g.vector.tensor_scalar(out, in0, s1, None, op0)
+        return lambda: g.vector.tensor_scalar(out, in0, s1, s2, op0, op1)
+
+    def tt(out, a, b, o):
+        return lambda: g.vector.tensor_tensor(out, a, b, o)
+
+    def cp(out, a):
+        return lambda: g.vector.tensor_copy(out, a)
+
+    def fill(ap, v):
+        return lambda: g.vector.memset(ap, v)
+
+    def scan(out, a, b, init, o0, o1):
+        return lambda: g.vector.tensor_tensor_scan(out, a, b, init, o0, o1)
+
+    def quant(n, src, a, b, r, tok):
+        V(lambda: g.vector.quantize_mx(T["q" + n][:, a:b], T["s" + n][:, a:b], src), r, tok)
+
+    def mm(bank, ln, la, rn, ra, rb, r):
+        op("T", lambda: g.tensor.matmul_mx(T[bank][:, 0:rb - ra], T["q" + ln][:, la:la + 128], T["s" + ln][:, la:la + 128],
+                                           T["q" + rn][:, ra:rb], T["s" + rn][:, ra:rb], True, True), r.split(), [bank])
+
+    def dma(q, out, in_, sem, r="", w=""):
+        op(q, lambda: queues[q].dma_start(out, in_), r.split(), w.split(), sem, 16)
+
+    def own(src, n, tok, out="wa"):
+        V(scan(T[out][:, 0:n], src, T.msk[:, 0:n], BIG, A.min, A.max), tok + " msk", out)
+
+    def wrap(src, n, tok):
+        V(scan(T.wb[:, 0:n], T.rs[:, 0:n], src, BIG, A.max, A.min), tok + " rs", "wb")
+
+    def const(name, pat, base, ch, in_=None, cmp=None, fv=None):
+        out = T[name][:]
+        if in_ is None:
+            small = SCRATCH[name][2] != "int32"
+            op("G", lambda: g.iota(out, pat, base, ch, allow_small_or_imprecise_dtypes=small), [], [name])
+        else:
+            src = T[in_][:, 0:SCRATCH[name][1][1]]
+            op("G", lambda: g.affine_select(out, src, pat, cmp, fv, base, ch), [in_], [name])
+
+    dma("S", T.u0[:], T.u[:], "ld_u", "", "u0")
+    dma("A", T.x0[:, 0:512], T.x[:, 0:512], "ld_xa", "", "x0a")
+    dma("S", T.mi0[:], T.m[:], "ld_m0", "", "mi0")
+    dma("A", T.x0[:, 512:1024], T.x[:, 512:1024], "ld_xb", "", "x0b")
+    dma("S", T.qw[:].bitcast(dt.uint8), T.wc[:], "ld_wc", "", "qw")
+    dma("S", T.sw[:], T.ws[:], "ld_ws", "", "sw")
+    for t in (1, 2):
+        n = 16 * t
+        dma("S", T["mi%d" % t][0:128 - n, :], T.m[n:128, :], "ld_m%d" % t, "", "mi%da" % t)
+        dma("S", T["mi%d" % t][128 - n:128, :], T.m[0:n, :], "ld_m%d" % t, "", "mi%d" % t)
+    dma("S", T.v0[:], T.v[:], "ld_v", "", "v0")
+
+    V(fill(T.zero[:], 0.0), "", "zero")
+    V(fill(T.ones[:], 1.0), "", "ones")
+    V(fill(T.neg[:], -1.0), "", "neg")
+    const("pick8i", [[16, 8]], 0, 0)
+    const("ident", [[-1, 128]], 0, 1, "ones", A.is_equal, 0.0)
+    const("nb", [[-16, 8], [0, 16]], 0, 1, "neg", A.is_ge, 0.0)
+    const("nb2", [[16, 8], [0, 16]], 15, -1, "nb", A.is_ge, 0.0)
+    const("rr", [[-1, 128]], 0, 1, "nb2", A.is_gt, 0.0)
+    const("rr2", [[-1, 128]], 0, 1, "rr", A.not_equal, -1024.0)
+    const("ipI", [[0, 16]], 0, 1)
+    const("ic", [[16, 16]], 0, 0)
+    const("rsI", [[0, 16], [1, 16]], 0, 0)
+    const("rs", [[0, 16], [1, 16]], 0, 0, "zero", A.not_equal, BIG)
+    const("row", [[1, 256]], 0, 0)
+    for b in range(4):
+        act(T.et[:, 512 * b:512 * b + 512], T.zero[:], "zero", "et%d" % b)
+    V(fill(T.ct[:], 0.0), "", "ct")
+    V(fill(T.ct[:, 0:512:4], 0.0625), "", "ct")
+    V(fill(T.ct[:, 514:1024:4], 0.0625), "", "ct")
+    quant("c", T.ct[:], 0, 256, "ct", "qc")
+    V(cp(T.pick8[:], T.pick8i[:]), "pick8i", "pick8")
+    V(fill(T.ta[:], 0.0), "", "ta")
+    V(fill(T.tb[:], 0.0), "", "tb")
+    quant("u", T.u0[:], 0, 128, "u0", "qu")
+    V(cp(T.qu16[:, 0:128].bitcast(dt.uint32), T.qu[:, 0:128].bitcast(dt.uint32).indirect(T.pick8[:, 0:8])), "qu pick8", "qu16")
+    act(T.su16[:, 0:128], T.su[:, 0:128].indirect(T.pick8[:, 0:8]), "qu pick8", "su16")
+    for b in range(4):
+        act(T.et[:, 512 * b + b:512 * b + 512:4], T.ident[:], "ident", "et%d" % b)
+    for h in (0, 1):
+        act(T.pt[:, 512 * h:512 * h + 512], T.zero[:], "zero", "pt%d" % h)
+    act(T.pt[:, 0:512:4], T.rr2[:], "rr2", "pt0")
+    act(T.pt[:, 512:1024:4], T.nb2[:], "nb2", "pt1", scale=-1.0)
+
+    xs = ["xs%d%d" % (b, h) for h in (0, 1) for b in range(4)]
+    even = slice(0, 512, 2)
+    L = [T.ll[:, 16 * k:16 * k + 16] for k in range(12)]
+    F3, F2, F1, F4 = [T.ft[:, 64 * k:64 * k + 64:4] for k in range(4)]
+
+    def quant_x(h, src, r):
+        quant("x", src[:, 512 * h:512 * h + 512], 128 * h, 128 * h + 128, r, "qx%d" % h)
+
+    quant_x(0, T.x0, "x0a")
+    quant_x(1, T.x0, "x0b")
+    for t in range(R):
+        mo = T["mo%d" % t][:, 0:16]
+        mot = " mo%d" % t
+        mm("k0", "u16", 0, "x", 0, 128, "qu16 su16 qx0")
+        mm("k1", "u16", 0, "x", 128, 256, "qu16 su16 qx1")
+
+        def unpack(b):
+            mm("b%d" % b, "e", 128 * b, "x", 0, 256, "qe qx0 qx1")
+            act(T.fg[:, b:1024:4], T["b%d" % b][:, 0:256], "b%d" % b, "f%d" % b)
+        if t:
+            unpack(0)
+        for h in (0, 1):
+            V(ts(T.ta[:, 256 * h:256 * h + 256:2], T["k%d" % h][:, 0:128], 0.0, 1.25, A.is_gt, A.mult), "ta k%d" % h, "ta%d" % h)
+        quant("ta", T.ta[:], 0, 128, "ta ta0 ta1", "qta")
+        mm("k2", "c", 0, "ta", 0, 128, "qc qta")
+        mm("k3", "c", 128, "ta", 0, 128, "qc qta")
+        if t == 0:
+            V(cp(T.mo0[:], T.mi0[:]), "mi0", "mo0")
+            quant("e", T.et[:], 0, 512, "et0 et1 et2 et3", "qe")
+            unpack(0)
+        for b in (1, 2, 3):
+            unpack(b)
+        if t == 0:
+            act(T.ft[:], T.zero[:], "zero", "ft")
+            for b in range(4):
+                act(T["hp%d" % b][:, 256:272], T.zero[:, 0:16], "zero", "hz%d" % b)
+        V(fill(T.sl[:, 0:96], 256.0), "", "sl")
+        V(ts(T.lic1[:, 0:256:2], T.k2[:, 0:128], 5.5, 1.125, A.is_ge, A.mult), "k2", "lic1a")
+        V(ts(T.lic1[:, 1:256:2], T.k3[:, 0:128], 5.5, 1.125, A.is_ge, A.mult), "k3", "lic1b")
+        V(tt(T.tb[:, even], T.lic1[:, 0:256].indirect(mo), T.ta[:, even], A.max), "lic1a lic1b ta0 ta1 tb" + mot, "tbv")
+        quant("tb", T.tb[:], 0, 128, "tb tbv", "qtb")
+        mm("k2", "c", 0, "tb", 0, 128, "qc qtb")
+        mm("k3", "c", 128, "tb", 0, 128, "qc qtb")
+        if t == 0:
+            V(ts(T.ipI[:], T.ipI[:], 15, None, A.bitwise_and), "ipI", "ipI")
+            V(tt(T.leg[:], T.ipI[:], T.ic[:], A.add), "ipI ic", "leg")
+            V(ts(T.msk[:], T.rsI[:], T.leg[:, 0:1], BIG, A.not_equal, A.mult), "rsI leg", "msk")
+        own(T.tb[:, even], 256, "tbv", "tbm")
+        quant("f%d" % t, T.fg[:, 0:1024], 0, 256, "f0 f1 f2 f3", "qf")
+        order("G", [writer["qf"]])
+        g.remote_dma(T["qh%d" % t][:].bitcast(dt.uint8), T["qf%d" % t][:].bitcast(dt.uint8), T.sem["ah%d" % t], T.sem.loc, pid, rid, mask)
+        g.remote_dma(T["sh%d" % t][:], T["sf%d" % t][:], T.sem["ah%d" % t], T.sem.loc, pid, rid, mask)
+        V(ts(T.lic2[:, 0:256:2], T.k2[:, 0:128], 5.5, 0.875, A.is_ge, A.max), "k2", "lic2a")
+        V(ts(T.lic2[:, 1:256:2], T.k3[:, 0:128], 5.5, 0.875, A.is_ge, A.max), "k3", "lic2b")
+        V(tt(T.wa[:], T.lic2[:, 0:256].indirect(mo), T.tbm[:], A.max), "lic2a lic2b tbm" + mot, "wa")
+        wrap(T.wa[:], 256, "wa")
+        for k, code in enumerate((1.0, 1.125, 1.25, 0.875)):
+            V(ts(T.ft[:, 64 * k:64 * k + 64:4], T.wb[:, 15:256:16], code, None, A.is_equal), "wb ft", "ft%d" % k)
+        quant("ft", T.ft[:], 0, 128, "ft ft0 ft1 ft2 ft3", "qft")
+        if t == 0:
+            quant("p", T.pt[:], 0, 256, "pt0 pt1", "qp")
+            V(ts(T.pp[:, 48:64], T.leg[:], -767.0, None, A.add), "leg", "pc")
+            for k in range(R):
+                V(cp(T.mf[:, 16 * k:16 * k + 16], T["mi%d" % k][:]), "mi%d" % k, "mf%d" % k)
+        mm("k1", "p", 128, "ft", 0, 128, "qp qft")
+        mm("k0", "p", 0, "ft", 0, 128, "qp qft")
+        V(tt(L[0], F1, T.leg[:], A.mult), "ft2 leg", "l0")
+        V(tt(L[1], F2, F3, A.add), "ft0 ft1", "l1")
+        V(tt(L[2], L[1], T.mf[:, 16 * t:16 * t + 16], A.mult), "l1 mf%d" % t, "l2")
+        V(scan(T.cum[:], T.k1[:, 0:64], T.zero[:, 0:64], 0.0, A.add, A.add), "k1 zero", "cum")
+        V(tt(T.pp[:, 0:48], T.cum[:, 0:48], T.k0[:, 0:48], A.add), "cum k0", "pp")
+        V(tt(T.m32[:], T.pp[:, 0:32], T.pp[:, 32:64], A.min), "pp pc", "m32")
+        V(tt(T.m16[:], T.m32[:, 0:16], T.m32[:, 16:32], A.min), "m32", "m16")
+        V(ts(T.pos[:], T.m16[:], 1023.0, None, A.add), "m16", "pos")
+        V(cp(T.sl[:, 0:512].indirect(T.pos[:, 0:16]), T.row[:, 0:256]), "pos row", "sl")
+        own(T.sl[:, 0:96], 96, "sl")
+        wrap(T.wa[:, 0:96], 96, "wa")
+        V(cp(T["slot%d" % t][:, 0:6], T.wb[:, 15:96:16]), "wb", "slot")
+        order("G", [writer["slot"]])
+        g.remote_dma(T["land%d" % t][:], T["slot%d" % t][:], T.sem["al%d" % t], T.sem.loc, pid, rid, mask)
+        V(tt(L[3], T.cum[:, 48:64], T.k0[:, 48:64], A.add), "cum k0", "l3")
+        V(tt(L[5], L[0], L[2], A.add), "l0 l2", "l5")
+        V(ts(L[4], L[3], T.cum[:, 47:48], 1279.0, A.subtract, A.add), "l3 cum", "l4")
+        V(ts(L[6], L[4], 352.0, -96.0, A.is_ge, A.mult), "l4", "l6")
+        V(ts(L[7], L[4], 448.0, -96.0, A.is_ge, A.mult), "l4", "l7")
+        V(tt(L[8], L[4], L[6], A.add), "l4 l6", "l8")
+        V(tt(L[9], L[8], L[7], A.add), "l8 l7", "l9")
+        V(tt(L[10], L[9], F4, A.mult), "l9 ft3", "l10")
+        V(tt(L[11], L[5], L[10], A.add), "l5 l10", "l11")
+        for b in range(4):
+            V(ts(T["off%d" % b][:], L[11], 4.0, float(b), A.mult, A.add), "l11", "off%d" % b)
+        if t == 0:
+            V(cp(T.iv[:, 0:256].indirect(mo), T.row[:, 0:256]), "row" + mot, "iv")
+            own(T.iv[:], 256, "iv")
+            wrap(T.wa[:], 256, "wa")
+            V(cp(T.inv0[:, 0:16], T.wb[:, 15:256:16]), "wb", "inv0")
+            for k in (1, 2):
+                n = 16 * k
+                V(cp(T["mo%d" % k][:], T["mi%d" % k][:]), "mi%d" % k, "mo%d" % k)
+                dma("S", T["inv%d" % k][0:128 - n, :], T.inv0[n:128, :], "ld_inv", "inv0", "inv%da" % k)
+                dma("S", T["inv%d" % k][128 - n:128, :], T.inv0[0:n, :], "ld_inv", "inv0", "inv%d" % k)
+            writer["inv1"] = writer["inv2"]
+        elif t == 1:
+            quant("v", T.v0[:], 0, 128, "v0", "qv")
+        if t == R - 1:
+            V(tt(T.d[:], T.lic2[:, 0:256].indirect(mo), T.tb[:, even], A.max), "lic2a lic2b tbv" + mot, "d")
+        writer["hh"] = ("ah%d" % t, 2 * neng, {})
+        writer["land"] = ("al%d" % t, neng, {})
+        for b in range(4):
+            mm("b%d" % b, "e", 128 * b, "h%d" % t, 0, 256, "qe hh")
+            act(T["hp%d" % b][:, 0:256], T["b%d" % b][:, 0:256], "b%d" % b, "hp%d" % b)
+        if t == R - 1:
+            act(T.wrow[:], T.d[:], "d", "wrow", bias=11.0, scale=-8.0)
+            dma("S", T.wv[:], T.wrow[0:128:16, :], "st", "wrow")
+        for b in (0, 2, 1, 3):
+            src, out = T["hp%d" % b][:, 0:272].indirect(T["land%d" % t][:, 0:6]), T.fg[:, 1024 + b:1408:4]
+            r, w = "hp%d hz%d land" % (b, b), "g%d" % b
+            if b < 2:
+                V(cp(out, src), r, w)
+            else:
+                act(out, src, r, w)
+        for b in (0, 2, 1, 3):
+            src, out = T.fg[:, 0:1408].indirect(T["off%d" % b][:, 0:16]), T.z[:, b:1024:4]
+            r, w = "f0 f1 f2 f3 g0 g1 g2 g3 off%d" % b, "z%d" % b
+            if b < 2:
+                V(cp(out, src), r, w)
+            else:
+                act(out, src, r, w)
+        quant("z", T.z[:], 0, 256, "z0 z1 z2 z3", "qz")
+        for b in range(4):
+            mm("b%d" % b, "w", 128 * b, "z", 0, 256, "qw sw qz")
+        for b in (0, 1):
+            V(ts(T["z32%d" % b][:], T.z[:, b:1024:4], 32.0, None, A.mult), "z%d" % b, "z32%d" % b)
+        for b in (2, 3):
+            act(T["z32%d" % b][:], T.z[:, b:1024:4], "z%d" % b, "z32%d" % b, scale=32.0)
+        for b in range(4):
+            V(tt(T["tt%d" % b][:], T["b%d" % b][:, 0:256], T["z32%d" % b][:], A.add), "b%d z32%d" % (b, b), "tt%d" % b)
+        for h in (0, 1):
+            for b in range(4):
+                src = T["tt%d" % b][:, 0:256].indirect(T["inv%d" % t][:, 8 * h:8 * h + 8])
+                out, r, w = T.xt[:, 512 * h + b:512 * h + 512:4], "inv%d tt%d" % (t, b), "xs%d%d" % (b, h)
+                if b == 3:
+                    V(ts(out, src, 0.03125, None, A.mult), r, w)
+                else:
+                    act(out, src, r, w, scale=0.03125)
+            quant_x(h, T.xt, " ".join(xs[4 * h:4 * h + 4]))
+    for h in (0, 1):
+        dma("S", T.oc[:, 512 * h:512 * h + 512], T.qx[:, 128 * h:128 * h + 128].bitcast(dt.uint8), "st", "qx%d" % h)
+        mm("k%d" % h, "v", 0, "x", 128 * h, 128 * h + 128, "qv qx%d" % h)
+    for k in range(4):
+        dma("A", T.osc[4 * k:4 * k + 4, :], T.sx[32 * k:32 * k + 4, :], "st2", "qx0 qx1")
+    for h in (0, 1):
+        V(cp(T.yb[:, 128 * h:128 * h + 128], T["k%d" % h][:, 0:128]), "k%d" % h, "yb%d" % h)
+        dma("S", T.y[:, 128 * h:128 * h + 128], T.yb[:, 128 * h:128 * h + 128], "st", "yb%d" % h)
+    g.wait_ge(T.sem.loc, 3 * R * neng)
+    for s in sorted(count):
+        g.wait_ge(T.sem[s], count[s])

@@ -1,7 +1,10 @@
 from concourse.mybir import dt, AluOpType, ActivationFunctionType
 
 R = 3
-BIG = 512.0
+HUGE = 4096.0
+OWN = 1023.0
+NEVER = -1e29
+SMALL = "md md4 dump jn cum1 cum2 cum3 x1 pp2 pp3 t1 t2 m21 wm mn wr kk u1s a1 an t6 t7 sm gn ff".split()
 
 
 def _scratch():
@@ -11,35 +14,39 @@ def _scratch():
         for n in names.split():
             s[n] = ("sbuf", [128, w], d)
 
-    for w, names in ((128, "u u16 v ta tb ft"), (256, "x c p z f0 f1 f2 h0 h1 h2"), (512, "w e")):
+    for w, names in ((128, "u u16 v 1 2 3"), (256, "x z f0 f1 f2 h0 h1 h2"), (384, "c"), (512, "w e")):
         for n in names.split():
             s["q" + n] = ("sbuf", [128, w], "float8_e4m3fn_x4")
             s["s" + n] = ("sbuf", [128, w], "uint8")
-    sb("bfloat16", 2048, "et")
+    sb("bfloat16", 1536, "ct")
     sb("bfloat16", 1408, "fg")
-    sb("bfloat16", 1024, "x0 z xt ct pt")
-    sb("bfloat16", 512, "zero u0 v0 ta tb ft sl")
-    sb("bfloat16", 272, "hp0 hp1 hp2 hp3")
-    sb("bfloat16", 256, "row msk rsI rs lic1 lic2 tbm d wa wb iv z320 z321 z322 z323 tt0 tt1 tt2 tt3")
-    sb("bfloat16", 128, "ones neg ident nb nb2 rr rr2")
-    sb("uint16", 16, "mo0 mo1 mo2 inv0 inv1 inv2 pos off0 off1 off2 off3")
-    sb("uint16", 6, "slot0 slot1 slot2 land0 land1 land2")
+    sb("bfloat16", 1040, "hh")
+    sb("bfloat16", 1024, "x0 z z32 xt tu")
+    sb("bfloat16", 528, "eb zero")
+    sb("bfloat16", 512, "u0 v0 sl")
+    sb("bfloat16", 256, "row lam i4 i16 pat wr4 wr16 iv mrow thr0 thr1 thr2 tt0 tt1 tt2 tt3")
+    sb("bfloat16", 64, "d64 e0 wb0 wb1 wb quarter nl1 nl2")
+    sb("uint16", 32, "ls0 ls1 ls2")
+    sb("uint16", 16, "mo pos")
+    sb("uint16", 64, "off")
+    sb("uint16", 24, "slot0 slot1 slot2 land0 land1 land2")
     sb("uint16", 8, "pick8")
-    sb("int32", 8, "pick8i")
-    sb("int32", 16, "mi0 mi1 mi2 ipI")
-    sb("float32", 16, "ic leg m16")
-    sb("float32", 32, "m32")
-    sb("float32", 48, "mf")
-    sb("float32", 64, "cum pp")
-    sb("float32", 192, "ll")
-    sb("float32", 256, "wrow yb")
+    sb("int32", 8, "pick8i pi")
+    sb("int32", 16, "mi mq")
+    sb("float32", 8, "i8 gsel")
+    sb("float32", 16, "pc wc16")
+    sb("float32", 72, "nm")
+    sb("float32", 64, "n16 n4x dm0 dm1 dm2")
+    sb("float32", 64 * len(SMALL), "small")
+    sb("float32", 96, "ws96")
+    sb("float32", 256, "raw yb")
     for n in "k0 k1 k2 k3 b0 b1 b2 b3".split():
         s[n] = ("psum", [128, 512], "float32")
     return s
 
 
 SCRATCH = _scratch()
-LOADS = ["u", "xa", "xb", "v", "wc", "ws", "m0", "m1", "m2", "inv"]
+LOADS = ["u", "xa", "xb", "v", "wc", "ws", "m", "thr", "ls", "dm"]
 SEMAPHORES = ["sV", "sT", "sA", "sG", "loc", "st", "st2"] + ["ld_" + n for n in LOADS] + ["ah0", "ah1", "ah2", "al0", "al1", "al2"]
 
 
@@ -48,7 +55,7 @@ def rank_program(g, core, T, topo):
     if rank is None:
         return
     A = AluOpType
-    COPY = ActivationFunctionType.Copy
+    COPY, IDENT = ActivationFunctionType.Copy, ActivationFunctionType.Identity
     nxt = T.cores[(rank + 1) % len(T.cores)]
     rid, pid = topo.addr(nxt)[0], topo.addr(nxt)[1]
     mask, neng = topo.mask(core, nxt), len(topo.engines(core, nxt))
@@ -71,13 +78,10 @@ def rank_program(g, core, T, topo):
                 known[q][k] = max(known[q].get(k, 0), c[k])
             known[q][s] = max(known[q].get(s, 0), v)
 
-    def op(q, fn, r=(), w=(), sem=None, inc=1):
-        need = []
-        for k in r:
-            if k in writer:
-                need.append(writer[k])
+    def op(q, fn, r=(), w=(), sem=None, inc=1, chain=False):
+        need = [writer[k] for k in r]
         for k in w:
-            if k in writer:
+            if k in writer and not chain:
                 need.append(writer[k])
             need += [e for qq, e in readers.get(k, {}).items() if qq != q]
         order(q, need)
@@ -97,8 +101,8 @@ def rank_program(g, core, T, topo):
     def V(fn, r="", w=""):
         op("V", fn, r.split(), w.split())
 
-    def act(out, in_, r, w, **kw):
-        op("A", lambda: g.scalar.activation(out, in_, COPY, **kw), r.split(), w.split())
+    def act(out, in_, r, w, func=COPY, **kw):
+        op("A", lambda: g.scalar.activation(out, in_, func, **kw), r.split(), w.split())
 
     def ts(out, in0, s1, s2, op0, op1=None):
         if op1 is None:
@@ -120,77 +124,95 @@ def rank_program(g, core, T, topo):
     def quant(n, src, a, b, r, tok):
         V(lambda: g.vector.quantize_mx(T["q" + n][:, a:b], T["s" + n][:, a:b], src), r, tok)
 
-    def mm(bank, ln, la, rn, ra, rb, r):
+    def mm(bank, ln, la, rn, ra, rb, r, start=True, stop=True):
         op("T", lambda: g.tensor.matmul_mx(T[bank][:, 0:rb - ra], T["q" + ln][:, la:la + 128], T["s" + ln][:, la:la + 128],
-                                           T["q" + rn][:, ra:rb], T["s" + rn][:, ra:rb], True, True), r.split(), [bank])
+                                           T["q" + rn][:, ra:rb], T["s" + rn][:, ra:rb], start, stop), r.split(), [bank], chain=not start)
 
     def dma(q, out, in_, sem, r="", w=""):
         op(q, lambda: queues[q].dma_start(out, in_), r.split(), w.split(), sem, 16)
 
-    def own(src, n, tok, out="wa"):
-        V(scan(T[out][:, 0:n], src, T.msk[:, 0:n], BIG, A.min, A.max), tok + " msk", out)
+    def iota(name, pat, base, ch):
+        small = SCRATCH[name][2] != "int32"
+        op("G", lambda: g.iota(T[name][:], pat, base, ch, allow_small_or_imprecise_dtypes=small), [], [name])
 
-    def wrap(src, n, tok):
-        V(scan(T.wb[:, 0:n], T.rs[:, 0:n], src, BIG, A.max, A.min), tok + " rs", "wb")
+    def turn(name, sem, r):
+        for t in (1, 2):
+            n = 16 * t
+            dma("S", T[name + "%d" % t][0:128 - n, :], T[name + "0"][n:128, :], sem, r, name + "%da" % t)
+            dma("S", T[name + "%d" % t][128 - n:128, :], T[name + "0"][0:n, :], sem, r, name + "%d" % t)
+        writer[name + "1"] = writer[name + "2"]
 
-    def const(name, pat, base, ch, in_=None, cmp=None, fv=None):
-        out = T[name][:]
-        if in_ is None:
-            small = SCRATCH[name][2] != "int32"
-            op("G", lambda: g.iota(out, pat, base, ch, allow_small_or_imprecise_dtypes=small), [], [name])
-        else:
-            src = T[in_][:, 0:SCRATCH[name][1][1]]
-            op("G", lambda: g.affine_select(out, src, pat, cmp, fv, base, ch), [in_], [name])
+    def W(name, a=0, b=64, step=1):
+        k = 64 * SMALL.index(name)
+        return T.small[:, k + a:k + b:step]
 
-    dma("S", T.u0[:], T.u[:], "ld_u", "", "u0")
-    dma("A", T.x0[:, 0:512], T.x[:, 0:512], "ld_xa", "", "x0a")
-    dma("S", T.mi0[:], T.m[:], "ld_m0", "", "mi0")
+    def col(k):
+        return T.pc[:, k:k + 1]
+    RES, SUB, ELEM, GROUP, CA, INIT1, DUMP, OFFC, S0, SLOTC, CM, CI = range(12)
+
+    dma("S", T.mi[:], T.m[:], "ld_m", "", "mi")
+    dma("A", T.u0[:], T.u[:], "ld_u", "", "u0")
+    dma("S", T.x0[:, 0:512], T.x[:, 0:512], "ld_xa", "", "x0a")
     dma("A", T.x0[:, 512:1024], T.x[:, 512:1024], "ld_xb", "", "x0b")
-    dma("S", T.qw[:].bitcast(dt.uint8), T.wc[:], "ld_wc", "", "qw")
+    dma("S", T.qw[:].bitcast(dt.uint8), T.wc[:], "ld_wc", "x0a x0b", "qw")
     dma("S", T.sw[:], T.ws[:], "ld_ws", "", "sw")
-    for t in (1, 2):
-        n = 16 * t
-        dma("S", T["mi%d" % t][0:128 - n, :], T.m[n:128, :], "ld_m%d" % t, "", "mi%da" % t)
-        dma("S", T["mi%d" % t][128 - n:128, :], T.m[0:n, :], "ld_m%d" % t, "", "mi%d" % t)
     dma("S", T.v0[:], T.v[:], "ld_v", "", "v0")
 
+    op("G", lambda: g.iota(T.pi[:, 4:5], [[0, 1]], 0, 1), [], ["pi4"])
+    iota("d64", [[-1, 4], [0, 4], [1, 4]], 0, 0)
+    iota("i8", [[1, 8]], 0, 0)
     V(fill(T.zero[:], 0.0), "", "zero")
-    V(fill(T.ones[:], 1.0), "", "ones")
-    V(fill(T.neg[:], -1.0), "", "neg")
-    const("pick8i", [[16, 8]], 0, 0)
-    const("ident", [[-1, 128]], 0, 1, "ones", A.is_equal, 0.0)
-    const("nb", [[-16, 8], [0, 16]], 0, 1, "neg", A.is_ge, 0.0)
-    const("nb2", [[16, 8], [0, 16]], 15, -1, "nb", A.is_ge, 0.0)
-    const("rr", [[-1, 128]], 0, 1, "nb2", A.is_gt, 0.0)
-    const("rr2", [[-1, 128]], 0, 1, "rr", A.not_equal, -1024.0)
-    const("ipI", [[0, 16]], 0, 1)
-    const("ic", [[16, 16]], 0, 0)
-    const("rsI", [[0, 16], [1, 16]], 0, 0)
-    const("rs", [[0, 16], [1, 16]], 0, 0, "zero", A.not_equal, BIG)
-    const("row", [[1, 256]], 0, 0)
+    op("G", lambda: g.affine_select(T.eb[:], T.zero[:], [[-1, 528]], A.not_equal, 1.0, 3, 4), ["zero"], ["eb"])
+    iota("pick8i", [[16, 8]], 0, 0)
+    iota("row", [[1, 256]], 0, 0)
+    iota("i16", [[0, 16], [1, 16]], 0, 0)
+    iota("n16", [[16, 16], [0, 4]], 0, 0)
+    iota("n4x", [[-4, 64]], -100, 0)
+    iota("lam", [[16, 16], [1, 4], [4, 4]], 0, 0)
+    V(ts(T.pi[:, 0:1], T.pi[:, 4:5], 15, None, A.bitwise_and), "pi4", "pi0")
+    V(ts(T.pi[:, 1:2], T.pi[:, 4:5], 2, 3, A.logical_shift_right, A.bitwise_and), "pi4", "pi1")
+    V(ts(T.pi[:, 2:3], T.pi[:, 4:5], 3, None, A.bitwise_and), "pi4", "pi2")
+    V(ts(T.pi[:, 3:4], T.pi[:, 4:5], 4, None, A.logical_shift_right), "pi4", "pi3")
+    V(ts(T.e0[:], T.d64[:], 0.0, 0.25, A.is_equal, A.mult), "d64", "e0")
+    V(cp(T.pc[:, 0:4], T.pi[:, 0:4]), "pi0 pi1 pi2 pi3", "pc")
+    V(ts(T.wb0[:], T.d64[:], 0.0, -0.25, A.is_gt, A.mult), "d64", "wb0")
+    V(ts(T.wb1[:], T.d64[:], 0.0, -256.0, A.is_equal, A.mult), "d64", "wb1")
+    V(ts(T.gsel[:], T.i8[:], col(GROUP), None, A.is_equal), "i8 pc", "gsel")
+    V(fill(T.quarter[:], 0.25), "", "quarter")
+    V(tt(T.wb[:], T.wb0[:], T.wb1[:], A.add), "wb0 wb1", "wb")
+    for k in range(4):
+        V(fill(T.i4[:, k:256:4], float(k)), "", "i4%d" % k)
+    V(fill(T.nm[:, 0:1], 0.0), "", "nm0")
+    V(ts(T.pat[:], T.i4[:], col(SUB), NEVER, A.not_equal, A.mult), "i40 i41 i42 i43 pc", "pat")
+    V(ts(T.nm[:, 1:65], T.i4[:, 0:64], col(ELEM), -HUGE, A.not_equal, A.mult), "i40 i41 i42 i43 pc", "nm")
+    for j, src in enumerate(("e0", "quarter", "wb")):
+        for k in range(8):
+            kw = {"scale": T.gsel[:, k:k + 1]} if j else {}
+            act(T.ct[:, 512 * j + 64 * k:512 * j + 64 * k + 64], T[src][:], src + (" gsel" if j else ""), "c%d%d" % (j, k), **kw)
+    V(fill(T.tu[:, 256:1024], 0.0), "", "tz")
+    V(tt(W("md"), T.nm[:, 0:64], T.nm[:, 1:65], A.subtract), "nm0 nm", "md")
     for b in range(4):
-        act(T.et[:, 512 * b:512 * b + 512], T.zero[:], "zero", "et%d" % b)
-    V(fill(T.ct[:], 0.0), "", "ct")
-    V(fill(T.ct[:, 0:512:4], 0.0625), "", "ct")
-    V(fill(T.ct[:, 514:1024:4], 0.0625), "", "ct")
-    quant("c", T.ct[:], 0, 256, "ct", "qc")
+        quant("e", T.eb[:, 3 - b:515 - b], 128 * b, 128 * b + 128, "eb", "qe%d" % b)
     V(cp(T.pick8[:], T.pick8i[:]), "pick8i", "pick8")
-    V(fill(T.ta[:], 0.0), "", "ta")
-    V(fill(T.tb[:], 0.0), "", "tb")
+    act(col(CA), col(SUB), "pc", "ca", scale=-1.0, bias=1027.0)
+    act(col(DUMP), col(RES), "pc", "cdump", bias=256.0 - OWN)
+    act(W("md4"), W("md"), "md", "md4", bias=4.0)
+    act(col(INIT1), T.nm[:, 64:65], "nm ca", "init1", IDENT, scale=-1.0, bias=col(CA))
+    V(cp(T.mo[:], T.mi[:]), "mi", "mo")
+    V(ts(T.mq[:], T.mi[:], 2, None, A.logical_shift_right), "mi", "mq")
+    act(T.thr0[:], T.pat[:, 0:256].indirect(T.mo[:, 0:16]), "pat mo", "thr0")
+    V(cp(T.iv[:, 0:256].indirect(T.mo[:, 0:16]), T.row[:, 0:256]), "row mo", "iv")
     quant("u", T.u0[:], 0, 128, "u0", "qu")
+    V(cp(T.ls0[:, 16:32], T.mq[:]), "mq", "ls0")
     V(cp(T.qu16[:, 0:128].bitcast(dt.uint32), T.qu[:, 0:128].bitcast(dt.uint32).indirect(T.pick8[:, 0:8])), "qu pick8", "qu16")
+    act(W("dump"), T.nm[:, 1:65], "nm cdump", "dump", IDENT, scale=2.0, bias=col(DUMP))
+    act(col(CI), col(RES), "pc", "ci", scale=-256.0, bias=3840.0)
     act(T.su16[:, 0:128], T.su[:, 0:128].indirect(T.pick8[:, 0:8]), "qu pick8", "su16")
-    for b in range(4):
-        act(T.et[:, 512 * b + b:512 * b + 512:4], T.ident[:], "ident", "et%d" % b)
-    for h in (0, 1):
-        act(T.pt[:, 512 * h:512 * h + 512], T.zero[:], "zero", "pt%d" % h)
-    act(T.pt[:, 0:512:4], T.rr2[:], "rr2", "pt0")
-    act(T.pt[:, 512:1024:4], T.nb2[:], "nb2", "pt1", scale=-1.0)
+    turn("thr", "ld_thr", "thr0")
 
     xs = ["xs%d%d" % (b, h) for h in (0, 1) for b in range(4)]
-    even = slice(0, 512, 2)
-    L = [T.ll[:, 16 * k:16 * k + 16] for k in range(12)]
-    F3, F2, F1, F4 = [T.ft[:, 64 * k:64 * k + 64:4] for k in range(4)]
+    fs = "f0 f1 f2 f3"
+    q64 = slice(0, 64)
 
     def quant_x(h, src, r):
         quant("x", src[:, 512 * h:512 * h + 512], 128 * h, 128 * h + 128, r, "qx%d" % h)
@@ -198,136 +220,144 @@ def rank_program(g, core, T, topo):
     quant_x(0, T.x0, "x0a")
     quant_x(1, T.x0, "x0b")
     for t in range(R):
-        mo = T["mo%d" % t][:, 0:16]
-        mot = " mo%d" % t
+        moq = T["ls%d" % t][:, 16:32]
+        lst = " ls%d" % t
         mm("k0", "u16", 0, "x", 0, 128, "qu16 su16 qx0")
         mm("k1", "u16", 0, "x", 128, 256, "qu16 su16 qx1")
 
         def unpack(b):
-            mm("b%d" % b, "e", 128 * b, "x", 0, 256, "qe qx0 qx1")
-            act(T.fg[:, b:1024:4], T["b%d" % b][:, 0:256], "b%d" % b, "f%d" % b)
-        if t:
-            unpack(0)
+            mm("b%d" % b, "e", 128 * b, "x", 0, 256, "qe%d qx0 qx1" % b)
+            act(T.fg[:, 384 + b:1408:4], T["b%d" % b][:, 0:256], "b%d" % b, "f%d" % b)
+        unpack(0)
+        unpack(1)
+        if t == 0:
+            quant("c", T.ct[:, 0:512], 0, 128, " ".join("c0%d" % k for k in range(8)), "qc0")
         for h in (0, 1):
-            V(ts(T.ta[:, 256 * h:256 * h + 256:2], T["k%d" % h][:, 0:128], 0.0, 1.25, A.is_gt, A.mult), "ta k%d" % h, "ta%d" % h)
-        quant("ta", T.ta[:], 0, 128, "ta ta0 ta1", "qta")
-        mm("k2", "c", 0, "ta", 0, 128, "qc qta")
-        mm("k3", "c", 128, "ta", 0, 128, "qc qta")
-        if t == 0:
-            V(cp(T.mo0[:], T.mi0[:]), "mi0", "mo0")
-            quant("e", T.et[:], 0, 512, "et0 et1 et2 et3", "qe")
-            unpack(0)
-        for b in (1, 2, 3):
-            unpack(b)
-        if t == 0:
-            act(T.ft[:], T.zero[:], "zero", "ft")
-            for b in range(4):
-                act(T["hp%d" % b][:, 256:272], T.zero[:, 0:16], "zero", "hz%d" % b)
+            V(tt(T.tu[:, 128 * h:128 * h + 128], T["k%d" % h][:, 0:128], T["thr%d" % t][:, 128 * h:128 * h + 128], A.is_le),
+              "k%d thr%d" % (h, t), "u1%d" % h)
         V(fill(T.sl[:, 0:96], 256.0), "", "sl")
-        V(ts(T.lic1[:, 0:256:2], T.k2[:, 0:128], 5.5, 1.125, A.is_ge, A.mult), "k2", "lic1a")
-        V(ts(T.lic1[:, 1:256:2], T.k3[:, 0:128], 5.5, 1.125, A.is_ge, A.mult), "k3", "lic1b")
-        V(tt(T.tb[:, even], T.lic1[:, 0:256].indirect(mo), T.ta[:, even], A.max), "lic1a lic1b ta0 ta1 tb" + mot, "tbv")
-        quant("tb", T.tb[:], 0, 128, "tb tbv", "qtb")
-        mm("k2", "c", 0, "tb", 0, 128, "qc qtb")
-        mm("k3", "c", 128, "tb", 0, 128, "qc qtb")
+        quant("1", T.tu[:, 0:512], 0, 128, "u10 u11 tz", "q1")
+        mm("k2", "c", 0, "1", 0, 128, "qc0 q1")
         if t == 0:
-            V(ts(T.ipI[:], T.ipI[:], 15, None, A.bitwise_and), "ipI", "ipI")
-            V(tt(T.leg[:], T.ipI[:], T.ic[:], A.add), "ipI ic", "leg")
-            V(ts(T.msk[:], T.rsI[:], T.leg[:, 0:1], BIG, A.not_equal, A.mult), "rsI leg", "msk")
-        own(T.tb[:, even], 256, "tbv", "tbm")
-        quant("f%d" % t, T.fg[:, 0:1024], 0, 256, "f0 f1 f2 f3", "qf")
+            quant("c", T.ct[:, 512:1536], 128, 384, " ".join("c%d%d" % (j, k) for j in (1, 2) for k in range(8)), "qc1")
+        unpack(2)
+        unpack(3)
+        mm("k0", "c", 128, "1", 0, 128, "qc1 q1")
+        mm("k1", "c", 256, "1", 0, 128, "qc1 q1")
+        mm("k3", "c", 128, "1", 0, 128, "qc1 q1", True, False)
+        mm("b0", "c", 256, "1", 0, 128, "qc1 q1", True, False)
+        V(ts(T.nl1[:], T.k2[:, q64], 3.5, -1.0, A.is_ge, A.mult), "k2", "nl1")
+        if t == 0:
+            V(tt(W("dump"), W("dump"), T.n16[:], A.add), "dump n16", "dump")
+        V(tt(T.tu[:, 256:512], T.nl1[:, q64].indirect(moq), T.tu[:, 0:256], A.mult), "nl1 u10 u11" + lst, "u2")
+        V(scan(W("cum1"), T.k0[:, q64], W("md4"), col(INIT1), A.add, A.subtract), "k0 md4 init1", "cum1")
+        quant("2", T.tu[:, 256:768], 0, 128, "u2", "q2")
+        mm("k2", "c", 0, "2", 0, 128, "qc0 q2")
+        mm("k3", "c", 128, "2", 0, 128, "q2", False, True)
+        mm("b0", "c", 256, "2", 0, 128, "q2", False, True)
+        mm("b1", "c", 128, "2", 0, 128, "q2", True, False)
+        mm("b2", "c", 256, "2", 0, 128, "q2", True, False)
+        quant("f%d" % t, T.fg[:, 384:1408], 0, 256, fs, "qf")
         order("G", [writer["qf"]])
         g.remote_dma(T["qh%d" % t][:].bitcast(dt.uint8), T["qf%d" % t][:].bitcast(dt.uint8), T.sem["ah%d" % t], T.sem.loc, pid, rid, mask)
         g.remote_dma(T["sh%d" % t][:], T["sf%d" % t][:], T.sem["ah%d" % t], T.sem.loc, pid, rid, mask)
-        V(ts(T.lic2[:, 0:256:2], T.k2[:, 0:128], 5.5, 0.875, A.is_ge, A.max), "k2", "lic2a")
-        V(ts(T.lic2[:, 1:256:2], T.k3[:, 0:128], 5.5, 0.875, A.is_ge, A.max), "k3", "lic2b")
-        V(tt(T.wa[:], T.lic2[:, 0:256].indirect(mo), T.tbm[:], A.max), "lic2a lic2b tbm" + mot, "wa")
-        wrap(T.wa[:], 256, "wa")
-        for k, code in enumerate((1.0, 1.125, 1.25, 0.875)):
-            V(ts(T.ft[:, 64 * k:64 * k + 64:4], T.wb[:, 15:256:16], code, None, A.is_equal), "wb ft", "ft%d" % k)
-        quant("ft", T.ft[:], 0, 128, "ft ft0 ft1 ft2 ft3", "qft")
+        V(ts(T.nl2[:], T.k2[:, q64], -3.5, -1.0, A.is_gt, A.mult), "k2", "nl2")
+        V(scan(W("cum2"), T.k3[:, q64], W("md"), T.nm[:, 64:65], A.add, A.add), "k3 md nm", "cum2")
+        V(tt(T.tu[:, 512:768], T.nl2[:, q64].indirect(moq), T.tu[:, 256:512], A.mult), "nl2 u2" + lst, "u3")
+        V(tt(W("x1"), T.k1[:, q64], W("cum1"), A.add), "k1 cum1", "x1")
+        quant("3", T.tu[:, 512:1024], 0, 128, "u3", "q3")
+        mm("k2", "c", 128, "3", 0, 128, "q3")
+        mm("k0", "c", 256, "3", 0, 128, "q3")
+        mm("b1", "c", 128, "3", 0, 128, "q3", False, True)
+        mm("b2", "c", 256, "3", 0, 128, "q3", False, True)
+        act(W("t1"), W("x1"), "x1 cum2", "t1", IDENT, scale=-1.0, bias=W("cum2", 63))
         if t == 0:
-            quant("p", T.pt[:], 0, 256, "pt0 pt1", "qp")
-            V(ts(T.pp[:, 48:64], T.leg[:], -767.0, None, A.add), "leg", "pc")
-            for k in range(R):
-                V(cp(T.mf[:, 16 * k:16 * k + 16], T["mi%d" % k][:]), "mi%d" % k, "mf%d" % k)
-        mm("k1", "p", 128, "ft", 0, 128, "qp qft")
-        mm("k0", "p", 0, "ft", 0, 128, "qp qft")
-        V(tt(L[0], F1, T.leg[:], A.mult), "ft2 leg", "l0")
-        V(tt(L[1], F2, F3, A.add), "ft0 ft1", "l1")
-        V(tt(L[2], L[1], T.mf[:, 16 * t:16 * t + 16], A.mult), "l1 mf%d" % t, "l2")
-        V(scan(T.cum[:], T.k1[:, 0:64], T.zero[:, 0:64], 0.0, A.add, A.add), "k1 zero", "cum")
-        V(tt(T.pp[:, 0:48], T.cum[:, 0:48], T.k0[:, 0:48], A.add), "cum k0", "pp")
-        V(tt(T.m32[:], T.pp[:, 0:32], T.pp[:, 32:64], A.min), "pp pc", "m32")
-        V(tt(T.m16[:], T.m32[:, 0:16], T.m32[:, 16:32], A.min), "m32", "m16")
-        V(ts(T.pos[:], T.m16[:], 1023.0, None, A.add), "m16", "pos")
-        V(cp(T.sl[:, 0:512].indirect(T.pos[:, 0:16]), T.row[:, 0:256]), "pos row", "sl")
-        own(T.sl[:, 0:96], 96, "sl")
-        wrap(T.wa[:, 0:96], 96, "wa")
-        V(cp(T["slot%d" % t][:, 0:6], T.wb[:, 15:96:16]), "wb", "slot")
+            act(T.wr4[:], T.pat[:], "pat", "wr4", ActivationFunctionType.Relu, bias=1280.0)
+        V(tt(W("pp2"), T.b0[:, q64], W("cum2"), A.add), "b0 cum2", "pp2")
+        V(tt(W("m21"), W("pp2"), W("t1"), A.min), "pp2 t1", "m21")
+        V(scan(W("cum3"), T.k2[:, q64], W("md"), 0.0, A.add, A.add), "k2 md", "cum3")
+        V(scan(W("wm"), W("dump"), W("m21"), -HUGE, A.max, A.min), "dump m21", "wm")
+        V(tt(W("pp3"), T.k0[:, q64], W("cum3"), A.add), "k0 cum3", "pp3")
+        V(ts(W("t2", 0, 16), W("wm", 3, 64, 4), W("cum3", 63), None, A.add), "wm cum3", "t2")
+        V(scan(W("wr"), W("dump"), W("pp3"), -HUGE, A.max, A.min), "dump pp3", "wr")
+        V(tt(W("mn", 0, 16), W("wr", 3, 64, 4), W("t2", 0, 16), A.min), "wr t2", "mn")
+        V(ts(T.pos[:], W("mn", 0, 16), OWN, None, A.add), "mn", "pos")
+        if t == 0:
+            act(col(S0), col(ELEM), "pc", "s0", bias=3072.0)
+            act(col(OFFC), col(ELEM), "pc", "offc", bias=4092.0)
+            act(T.wr4[:], T.wr4[:], "wr4", "wr4", bias=-256.0)
+            act(col(SLOTC), col(SUB), "pc s0", "slotc", IDENT, scale=-1024.0, bias=col(S0))
+            act(col(CM), col(SUB), "pc", "cm", scale=256.0, bias=159.0)
+            act(W("jn"), T.n4x[:], "n4x ca", "jn", IDENT, bias=col(CA))
+            act(T.mrow[:], T.row[:, 0:256].indirect(T.mo[:, 0:16]), "row mo", "mrow")
+        V(cp(T.sl[:, 0:512].indirect(T.pos[:, 0:16]), T.lam[:, 0:256]), "pos lam", "sl")
+        V(scan(T.ws96[:], T.wr4[:, 0:96], T.sl[:, 0:96], 0.0, A.add, A.min), "wr4 sl", "ws96")
+        V(ts(T["slot%d" % t][:], T.ws96[:, 3:96:4], 4.0, col(SLOTC), A.mult, A.add), "ws96 slotc", "slot")
         order("G", [writer["slot"]])
         g.remote_dma(T["land%d" % t][:], T["slot%d" % t][:], T.sem["al%d" % t], T.sem.loc, pid, rid, mask)
-        V(tt(L[3], T.cum[:, 48:64], T.k0[:, 48:64], A.add), "cum k0", "l3")
-        V(tt(L[5], L[0], L[2], A.add), "l0 l2", "l5")
-        V(ts(L[4], L[3], T.cum[:, 47:48], 1279.0, A.subtract, A.add), "l3 cum", "l4")
-        V(ts(L[6], L[4], 352.0, -96.0, A.is_ge, A.mult), "l4", "l6")
-        V(ts(L[7], L[4], 448.0, -96.0, A.is_ge, A.mult), "l4", "l7")
-        V(tt(L[8], L[4], L[6], A.add), "l4 l6", "l8")
-        V(tt(L[9], L[8], L[7], A.add), "l8 l7", "l9")
-        V(tt(L[10], L[9], F4, A.mult), "l9 ft3", "l10")
-        V(tt(L[11], L[5], L[10], A.add), "l5 l10", "l11")
-        for b in range(4):
-            V(ts(T["off%d" % b][:], L[11], 4.0, float(b), A.mult, A.add), "l11", "off%d" % b)
+        writer["hq"] = ("ah%d" % t, 2 * neng, {})
+        writer["land"] = ("al%d" % t, neng, {})
+        for b, bank in enumerate(("b3", "k3", "b0", "k2")):
+            mm(bank, "e", 128 * b, "h%d" % t, 0, 256, "hq")
+            act(T.hh[:, b:1024:4], T[bank][:, 0:256], bank, "h%d" % b)
+        V(scan(W("cum1"), T.b1[:, q64], T.zero[:, q64], 0.0, A.add, A.add), "b1 zero", "cum1")
         if t == 0:
-            V(cp(T.iv[:, 0:256].indirect(mo), T.row[:, 0:256]), "row" + mot, "iv")
-            own(T.iv[:], 256, "iv")
-            wrap(T.wa[:], 256, "wa")
-            V(cp(T.inv0[:, 0:16], T.wb[:, 15:256:16]), "wb", "inv0")
-            for k in (1, 2):
-                n = 16 * k
-                V(cp(T["mo%d" % k][:], T["mi%d" % k][:]), "mi%d" % k, "mo%d" % k)
-                dma("S", T["inv%d" % k][0:128 - n, :], T.inv0[n:128, :], "ld_inv", "inv0", "inv%da" % k)
-                dma("S", T["inv%d" % k][128 - n:128, :], T.inv0[0:n, :], "ld_inv", "inv0", "inv%d" % k)
-            writer["inv1"] = writer["inv2"]
+            V(scan(T.raw[:], T.wr4[:], T.mrow[:], 0.0, A.add, A.min), "wr4 mrow", "raw")
+        V(tt(W("kk"), T.b2[:, q64], W("cum1"), A.add), "b2 cum1", "kk")
+        if t == 0:
+            V(tt(W("a1"), T.raw[:, 3:256:4], W("jn"), A.add), "raw jn", "a1")
+            V(ts(T.wr16[:], T.i16[:], col(RES), 4352.0, A.is_equal, A.mult), "i16 pc", "wr16")
+            V(ts(T.dm0[:], W("a1"), -1.0, col(CM), A.mult, A.add), "a1 cm", "dm0")
+            V(ts(T.wr16[:], T.wr16[:], -256.0, None, A.add), "wr16", "wr16")
+            turn("dm", "ld_dm", "dm0")
+        V(ts(W("u1s"), T.k1[:, q64], -512.0, None, A.is_le), "k1", "u1s")
+        V(ts(W("t6"), W("kk"), OWN - 96.0, 96.0, A.is_le, A.mult), "kk", "t6")
+        V(tt(W("a1"), W("u1s"), T["dm%d" % t][:], A.mult), "u1s dm%d" % t, "a1")
+        V(ts(W("t7"), W("kk"), OWN - 192.0, 96.0, A.is_le, A.mult), "kk", "t7")
+        V(tt(W("sm"), W("kk"), W("t6"), A.add), "kk t6", "sm")
+        V(tt(W("an"), W("a1"), W("jn"), A.add), "a1 jn", "an")
+        V(tt(W("gn"), W("sm"), W("t7"), A.add), "sm t7", "gn")
+        if t == 0:
+            V(scan(T.raw[:], T.wr16[:], T.iv[:], 0.0, A.add, A.min), "wr16 iv", "raw")
+        V(tt(W("ff"), W("gn"), W("an"), A.max), "gn an", "ff")
+        if t == 0:
+            V(ts(T.ls0[:, 0:16], T.raw[:, 15:256:16], col(CI), None, A.add), "raw ci ls0", "ls0")
+            turn("ls", "ld_ls", "ls0")
+        V(ts(T.off[:], W("ff"), -4.0, col(OFFC), A.mult, A.add), "ff offc", "off")
+        if t == 0:
+            V(fill(T.hh[:, 1024:1040], 0.0), "", "hz")
         elif t == 1:
             quant("v", T.v0[:], 0, 128, "v0", "qv")
-        if t == R - 1:
-            V(tt(T.d[:], T.lic2[:, 0:256].indirect(mo), T.tb[:, even], A.max), "lic2a lic2b tbv" + mot, "d")
-        writer["hh"] = ("ah%d" % t, 2 * neng, {})
-        writer["land"] = ("al%d" % t, neng, {})
+        else:
+            V(ts(W("t6"), T.k0[:, q64], -512.0, 1.0, A.is_le, A.add), "k0", "t6")
+            V(ts(W("t7"), W("kk"), 512.0, 2.0, A.is_ge, A.mult), "kk", "t7")
+            V(tt(W("sm"), W("t6"), W("u1s"), A.add), "t6 u1s", "sm")
+            V(tt(W("an"), W("sm"), W("t7"), A.add), "sm t7", "an")
+            V(lambda: g.vector.transpose(W("gn"), W("an")), "an", "gn")
+            act(T.wc16[:], W("gn", 0, 64, 4), "gn", "wc16")
+            for k in range(4):
+                dma("S", T.wv[k % 2:8:2, 128 * (k // 2):128 * (k // 2) + 128], T.wc16[:, 4 * k:4 * k + 4], "st", "wc16")
+        r = "h0 h1 h2 h3 hz land"
+        V(cp(T.fg[:, 0:192], T.hh[:, 0:1040].indirect(T["land%d" % t][:, 0:12])), r, "g0")
+        act(T.fg[:, 192:384], T.hh[:, 0:1040].indirect(T["land%d" % t][:, 12:24]), r, "g1")
+        r = fs + " g0 g1 off"
+        V(cp(T.z[:, 0:512], T.fg[:, 0:1408].indirect(T.off[:, 0:32])), r, "z0")
+        act(T.z[:, 512:1024], T.fg[:, 0:1408].indirect(T.off[:, 32:64]), r, "z1")
+        for h in (0, 1):
+            quant("z", T.z[:, 512 * h:512 * h + 512], 128 * h, 128 * h + 128, "z%d" % h, "qz%d" % h)
+        for b, h in ((0, 0), (1, 0), (0, 1), (1, 1), (2, 0), (2, 1), (3, 0), (3, 1)):
+            mm("bk"[h] + "%d" % b, "w", 128 * b, "z", 128 * h, 128 * h + 128, "qw sw qz%d" % h)
+        for b in (0, 1, 3):
+            act(T.z32[:, 256 * b:256 * b + 256], T.z[:, b:1024:4], "z0 z1", "y%d" % b, scale=32.0)
+        V(ts(T.z32[:, 512:768], T.z[:, 2:1024:4], 32.0, None, A.mult), "z0 z1", "y2")
         for b in range(4):
-            mm("b%d" % b, "e", 128 * b, "h%d" % t, 0, 256, "qe hh")
-            act(T["hp%d" % b][:, 0:256], T["b%d" % b][:, 0:256], "b%d" % b, "hp%d" % b)
-        if t == R - 1:
-            act(T.wrow[:], T.d[:], "d", "wrow", bias=11.0, scale=-8.0)
-            dma("S", T.wv[:], T.wrow[0:128:16, :], "st", "wrow")
-        for b in (0, 2, 1, 3):
-            src, out = T["hp%d" % b][:, 0:272].indirect(T["land%d" % t][:, 0:6]), T.fg[:, 1024 + b:1408:4]
-            r, w = "hp%d hz%d land" % (b, b), "g%d" % b
-            if b < 2:
-                V(cp(out, src), r, w)
-            else:
-                act(out, src, r, w)
-        for b in (0, 2, 1, 3):
-            src, out = T.fg[:, 0:1408].indirect(T["off%d" % b][:, 0:16]), T.z[:, b:1024:4]
-            r, w = "f0 f1 f2 f3 g0 g1 g2 g3 off%d" % b, "z%d" % b
-            if b < 2:
-                V(cp(out, src), r, w)
-            else:
-                act(out, src, r, w)
-        quant("z", T.z[:], 0, 256, "z0 z1 z2 z3", "qz")
-        for b in range(4):
-            mm("b%d" % b, "w", 128 * b, "z", 0, 256, "qw sw qz")
-        for b in (0, 1):
-            V(ts(T["z32%d" % b][:], T.z[:, b:1024:4], 32.0, None, A.mult), "z%d" % b, "z32%d" % b)
-        for b in (2, 3):
-            act(T["z32%d" % b][:], T.z[:, b:1024:4], "z%d" % b, "z32%d" % b, scale=32.0)
-        for b in range(4):
-            V(tt(T["tt%d" % b][:], T["b%d" % b][:, 0:256], T["z32%d" % b][:], A.add), "b%d z32%d" % (b, b), "tt%d" % b)
+            for h in (0, 1):
+                bank, a = "bk"[h] + "%d" % b, 256 * b + 128 * h
+                V(tt(T["tt%d" % b][:, 128 * h:128 * h + 128], T[bank][:, 0:128], T.z32[:, a:a + 128], A.add), bank + " y%d" % b, "tt%d%d" % (b, h))
         for h in (0, 1):
             for b in range(4):
-                src = T["tt%d" % b][:, 0:256].indirect(T["inv%d" % t][:, 8 * h:8 * h + 8])
-                out, r, w = T.xt[:, 512 * h + b:512 * h + 512:4], "inv%d tt%d" % (t, b), "xs%d%d" % (b, h)
+                src = T["tt%d" % b][:, 0:256].indirect(T["ls%d" % t][:, 8 * h:8 * h + 8])
+                out, r, w = T.xt[:, 512 * h + b:512 * h + 512:4], "tt%d0 tt%d1" % (b, b) + lst, "xs%d%d" % (b, h)
                 if b == 3:
                     V(ts(out, src, 0.03125, None, A.mult), r, w)
                 else:

@@ -5,6 +5,11 @@ HUGE = 4096.0
 OWN = 1023.0
 NEVER = -1e29
 SMALL = "md md4 dump jn cum1 cum2 cum3 x1 pp2 pp3 t1 t2 m21 wm mn wr kk u1s a1 an t6 t7 sm gn ff".split()
+SHARES = (("A", 0, 0, 8), ("A", 1, 0, 8), ("V", 2, 0, 8), ("V", 3, 0, 8), ("A", 0, 8, 16), ("A", 1, 8, 16), ("A", 2, 8, 16),
+          ("V", 3, 8, 12), ("Q", 0, 0, 8), ("V", 3, 12, 16), ("Q", 1, 8, 16))
+SCALE = (("A", 0, 0), ("A", 1, 0), ("V", 2, 0), ("V", 3, 0), ("A", 0, 1), ("A", 1, 1), ("A", 2, 1), ("A", 3, 1))
+SUMS = ((0, 0), (1, 0), (2, 0), (0, 1), (3, 0), (1, 1), (2, 1), (3, 1))
+FILL = ((0, 16, 32), (32, 44, 64))
 
 
 def _scratch():
@@ -189,7 +194,7 @@ def rank_program(g, core, T, topo):
         for k in range(8):
             kw = {"scale": T.gsel[:, k:k + 1]} if j else {}
             act(T.ct[:, 512 * j + 64 * k:512 * j + 64 * k + 64], T[src][:], src + (" gsel" if j else ""), "c%d%d" % (j, k), **kw)
-    V(fill(T.tu[:, 256:1024], 0.0), "", "tz")
+    op("G", lambda: g.iota(T.tu[:, 512:1024], [[0, 512]], 0, 0, allow_small_or_imprecise_dtypes=True), [], ["tz2"])
     V(tt(W("md"), T.nm[:, 0:64], T.nm[:, 1:65], A.subtract), "nm0 nm", "md")
     for b in range(4):
         quant("e", T.eb[:, 3 - b:515 - b], 128 * b, 128 * b + 128, "eb", "qe%d" % b)
@@ -198,81 +203,126 @@ def rank_program(g, core, T, topo):
     act(col(DUMP), col(RES), "pc", "cdump", bias=256.0 - OWN)
     act(W("md4"), W("md"), "md", "md4", bias=4.0)
     act(col(INIT1), T.nm[:, 64:65], "nm ca", "init1", IDENT, scale=-1.0, bias=col(CA))
+    act(T.tu[:, 256:512], T.zero[:, 0:256], "zero", "tz")
     V(cp(T.mo[:], T.mi[:]), "mi", "mo")
     V(ts(T.mq[:], T.mi[:], 2, None, A.logical_shift_right), "mi", "mq")
     act(T.thr0[:], T.pat[:, 0:256].indirect(T.mo[:, 0:16]), "pat mo", "thr0")
-    V(cp(T.iv[:, 0:256].indirect(T.mo[:, 0:16]), T.row[:, 0:256]), "row mo", "iv")
-    quant("u", T.u0[:], 0, 128, "u0", "qu")
+    quant("c", T.ct[:, 0:512], 0, 128, " ".join("c0%d" % k for k in range(8)), "qc0")
     V(cp(T.ls0[:, 16:32], T.mq[:]), "mq", "ls0")
-    V(cp(T.qu16[:, 0:128].bitcast(dt.uint32), T.qu[:, 0:128].bitcast(dt.uint32).indirect(T.pick8[:, 0:8])), "qu pick8", "qu16")
-    act(W("dump"), T.nm[:, 1:65], "nm cdump", "dump", IDENT, scale=2.0, bias=col(DUMP))
-    act(col(CI), col(RES), "pc", "ci", scale=-256.0, bias=3840.0)
-    act(T.su16[:, 0:128], T.su[:, 0:128].indirect(T.pick8[:, 0:8]), "qu pick8", "su16")
-    turn("thr", "ld_thr", "thr0")
-
-    xs = ["xs%d%d" % (b, h) for h in (0, 1) for b in range(4)]
-    fs = "f0 f1 f2 f3"
-    q64 = slice(0, 64)
 
     def quant_x(h, src, r):
         quant("x", src[:, 512 * h:512 * h + 512], 128 * h, 128 * h + 128, r, "qx%d" % h)
 
+    quant("u", T.u0[:], 0, 128, "u0", "qu")
     quant_x(0, T.x0, "x0a")
+    V(cp(T.qu16[:, 0:128].bitcast(dt.uint32), T.qu[:, 0:128].bitcast(dt.uint32).indirect(T.pick8[:, 0:8])), "qu pick8", "qu16")
     quant_x(1, T.x0, "x0b")
+    act(T.su16[:, 0:128], T.su[:, 0:128].indirect(T.pick8[:, 0:8]), "qu pick8", "su16")
+    act(T.wr4[:], T.pat[:], "pat", "wr4", ActivationFunctionType.Relu, bias=1280.0)
+    act(W("dump"), T.nm[:, 1:65], "nm cdump", "dump", IDENT, scale=2.0, bias=col(DUMP))
+    act(T.wr4[:], T.wr4[:], "wr4", "wr4", bias=-256.0)
+    turn("thr", "ld_thr", "thr0")
+
+    def late_constants():
+        act(T.mrow[:], T.row[:, 0:256].indirect(T.mo[:, 0:16]), "row mo", "mrow")
+        act(T.wr16[:], T.i16[:], "i16 pc", "wr16", ActivationFunctionType.Abs, scale=-1.0, bias=col(RES))
+        act(col(S0), col(ELEM), "pc", "s0", bias=3072.0)
+        act(W("jn"), T.n4x[:], "n4x ca", "jn", IDENT, bias=col(CA))
+        act(T.wr16[:], T.wr16[:], "wr16", "wr16", ActivationFunctionType.Relu, scale=-4352.0, bias=4352.0)
+        act(col(SLOTC), col(SUB), "pc s0", "slotc", IDENT, scale=-1024.0, bias=col(S0))
+        act(col(CM), col(SUB), "pc", "cm", scale=256.0, bias=159.0)
+        act(T.wr16[:], T.wr16[:], "wr16", "wr16", bias=-256.0)
+        act(col(OFFC), col(ELEM), "pc", "offc", bias=4092.0)
+        act(col(CI), col(RES), "pc", "ci", scale=-256.0, bias=3840.0)
+
+    def unwrap(src, steps, h, r):
+        V(scan(T.raw[:, 128 * h:128 * h + 128], T[steps][:, 0:128], T[src][:, 128 * h:128 * h + 128], 0.0, A.add, A.min), r, "raw%d" % h)
+
+    def partners():
+        V(ts(T.dm0[:], W("a1"), -1.0, col(CM), A.mult, A.add), "a1 cm", "dm0")
+        turn("dm", "ld_dm", "dm0")
+
+    def inverse():
+        V(ts(T.ls0[:, 0:16], T.raw[:, 15:256:16], col(CI), None, A.add), "raw0 raw1 ci ls0", "ls0")
+        turn("ls", "ld_ls", "ls0")
+
+    once = {
+        "count": lambda: quant("c", T.ct[:, 512:1536], 128, 384, " ".join("c%d%d" % (j, k) for j in (1, 2) for k in range(8)), "qc1"),
+        "licence": lambda: V(tt(W("dump"), W("dump"), T.n16[:], A.add), "dump n16", "dump"),
+        "unpacked": late_constants,
+        "place": lambda: unwrap("mrow", "wr4", 0, "wr4 mrow"),
+        "least": lambda: unwrap("mrow", "wr4", 1, "wr4 mrow"),
+        "offsets": lambda: V(tt(W("a1"), T.raw[:, 3:256:4], W("jn"), A.add), "raw0 raw1 jn", "a1"),
+        "scatter": partners,
+        "slots": lambda: V(fill(T.hh[:, 1024:1040], 0.0), "", "hz"),
+        "travel": lambda: V(cp(T.iv[:, 0:256].indirect(T.mo[:, 0:16]), T.row[:, 0:256]), "row mo", "iv"),
+        "guests": lambda: unwrap("iv", "wr16", 0, "wr16 iv"),
+        "fill0": lambda: unwrap("iv", "wr16", 1, "wr16 iv"),
+        "fill1": inverse,
+    }
+
+    fs = ["f0%d f1%d f2%d f3%d" % (h, h, h, h) for h in (0, 1)]
+    q64 = slice(0, 64)
+
+    def unpack(b, h, bank):
+        mm(bank, "e", 128 * b, "x", 128 * h, 128 * h + 128, "qe%d qx%d" % (b, h))
+        act(T.fg[:, 384 + 512 * h + b:896 + 512 * h:4], T[bank][:, 0:128], bank, "f%d%d" % (b, h))
+
+    def send(out, in_, sem, tok):
+        order("G", [writer[tok]])
+        g.remote_dma(out, in_, T.sem[sem], T.sem.loc, pid, rid, mask)
+
     for t in range(R):
         moq = T["ls%d" % t][:, 16:32]
         lst = " ls%d" % t
-        mm("k0", "u16", 0, "x", 0, 128, "qu16 su16 qx0")
-        mm("k1", "u16", 0, "x", 128, 256, "qu16 su16 qx1")
 
-        def unpack(b):
-            mm("b%d" % b, "e", 128 * b, "x", 0, 256, "qe%d qx0 qx1" % b)
-            act(T.fg[:, 384 + b:1408:4], T["b%d" % b][:, 0:256], "b%d" % b, "f%d" % b)
-        unpack(0)
-        unpack(1)
-        if t == 0:
-            quant("c", T.ct[:, 0:512], 0, 128, " ".join("c0%d" % k for k in range(8)), "qc0")
+        def at(place):
+            if t == 0:
+                once[place]()
+        mm("k0", "u16", 0, "x", 0, 128, "qu16 su16 qx0")
+        for b in range(2 if t else 0):
+            unpack(b, 0, "b%d" % b)
+        mm("k1", "u16", 0, "x", 128, 256, "qu16 su16 qx1")
+        for b in range(2 if t else 0, 4):
+            unpack(b, 0, "b%d" % b)
+        if t:
+            unpack(0, 1, "k3")
         for h in (0, 1):
             V(tt(T.tu[:, 128 * h:128 * h + 128], T["k%d" % h][:, 0:128], T["thr%d" % t][:, 128 * h:128 * h + 128], A.is_le),
               "k%d thr%d" % (h, t), "u1%d" % h)
         V(fill(T.sl[:, 0:96], 256.0), "", "sl")
         quant("1", T.tu[:, 0:512], 0, 128, "u10 u11 tz", "q1")
         mm("k2", "c", 0, "1", 0, 128, "qc0 q1")
-        if t == 0:
-            quant("c", T.ct[:, 512:1536], 128, 384, " ".join("c%d%d" % (j, k) for j in (1, 2) for k in range(8)), "qc1")
-        unpack(2)
-        unpack(3)
+        at("count")
+        for b in range(1 if t else 0, 4):
+            unpack(b, 1, ("k3", "b0", "b1", "b2")[b])
+        at("unpacked")
         mm("k0", "c", 128, "1", 0, 128, "qc1 q1")
         mm("k1", "c", 256, "1", 0, 128, "qc1 q1")
-        mm("k3", "c", 128, "1", 0, 128, "qc1 q1", True, False)
-        mm("b0", "c", 256, "1", 0, 128, "qc1 q1", True, False)
         V(ts(T.nl1[:], T.k2[:, q64], 3.5, -1.0, A.is_ge, A.mult), "k2", "nl1")
-        if t == 0:
-            V(tt(W("dump"), W("dump"), T.n16[:], A.add), "dump n16", "dump")
+        at("licence")
         V(tt(T.tu[:, 256:512], T.nl1[:, q64].indirect(moq), T.tu[:, 0:256], A.mult), "nl1 u10 u11" + lst, "u2")
         V(scan(W("cum1"), T.k0[:, q64], W("md4"), col(INIT1), A.add, A.subtract), "k0 md4 init1", "cum1")
-        quant("2", T.tu[:, 256:768], 0, 128, "u2", "q2")
+        quant("2", T.tu[:, 256:768], 0, 128, "u2 tz2", "q2")
         mm("k2", "c", 0, "2", 0, 128, "qc0 q2")
-        mm("k3", "c", 128, "2", 0, 128, "q2", False, True)
-        mm("b0", "c", 256, "2", 0, 128, "q2", False, True)
+        for bank, a in (("k3", 128), ("b0", 256)):
+            mm(bank, "c", a, "1", 0, 128, "q1", True, False)
+            mm(bank, "c", a, "2", 0, 128, "q2", False, True)
         mm("b1", "c", 128, "2", 0, 128, "q2", True, False)
         mm("b2", "c", 256, "2", 0, 128, "q2", True, False)
-        quant("f%d" % t, T.fg[:, 384:1408], 0, 256, fs, "qf")
-        order("G", [writer["qf"]])
-        g.remote_dma(T["qh%d" % t][:].bitcast(dt.uint8), T["qf%d" % t][:].bitcast(dt.uint8), T.sem["ah%d" % t], T.sem.loc, pid, rid, mask)
-        g.remote_dma(T["sh%d" % t][:], T["sf%d" % t][:], T.sem["ah%d" % t], T.sem.loc, pid, rid, mask)
+        quant("f%d" % t, T.fg[:, 384:1408], 0, 256, " ".join(fs), "qf")
+        send(T["qh%d" % t][:].bitcast(dt.uint8), T["qf%d" % t][:].bitcast(dt.uint8), "ah%d" % t, "qf")
+        send(T["sh%d" % t][:], T["sf%d" % t][:], "ah%d" % t, "qf")
         V(ts(T.nl2[:], T.k2[:, q64], -3.5, -1.0, A.is_gt, A.mult), "k2", "nl2")
-        V(scan(W("cum2"), T.k3[:, q64], W("md"), T.nm[:, 64:65], A.add, A.add), "k3 md nm", "cum2")
-        V(tt(T.tu[:, 512:768], T.nl2[:, q64].indirect(moq), T.tu[:, 256:512], A.mult), "nl2 u2" + lst, "u3")
         V(tt(W("x1"), T.k1[:, q64], W("cum1"), A.add), "k1 cum1", "x1")
+        V(tt(T.tu[:, 512:768], T.nl2[:, q64].indirect(moq), T.tu[:, 256:512], A.mult), "nl2 u2" + lst, "u3")
+        V(scan(W("cum2"), T.k3[:, q64], W("md"), T.nm[:, 64:65], A.add, A.add), "k3 md nm", "cum2")
         quant("3", T.tu[:, 512:1024], 0, 128, "u3", "q3")
+        act(W("t1"), W("x1"), "x1 cum2", "t1", IDENT, scale=-1.0, bias=W("cum2", 63))
         mm("k2", "c", 128, "3", 0, 128, "q3")
         mm("k0", "c", 256, "3", 0, 128, "q3")
         mm("b1", "c", 128, "3", 0, 128, "q3", False, True)
         mm("b2", "c", 256, "3", 0, 128, "q3", False, True)
-        act(W("t1"), W("x1"), "x1 cum2", "t1", IDENT, scale=-1.0, bias=W("cum2", 63))
-        if t == 0:
-            act(T.wr4[:], T.pat[:], "pat", "wr4", ActivationFunctionType.Relu, bias=1280.0)
         V(tt(W("pp2"), T.b0[:, q64], W("cum2"), A.add), "b0 cum2", "pp2")
         V(tt(W("m21"), W("pp2"), W("t1"), A.min), "pp2 t1", "m21")
         V(scan(W("cum3"), T.k2[:, q64], W("md"), 0.0, A.add, A.add), "k2 md", "cum3")
@@ -280,89 +330,82 @@ def rank_program(g, core, T, topo):
         V(tt(W("pp3"), T.k0[:, q64], W("cum3"), A.add), "k0 cum3", "pp3")
         V(ts(W("t2", 0, 16), W("wm", 3, 64, 4), W("cum3", 63), None, A.add), "wm cum3", "t2")
         V(scan(W("wr"), W("dump"), W("pp3"), -HUGE, A.max, A.min), "dump pp3", "wr")
+        at("place")
         V(tt(W("mn", 0, 16), W("wr", 3, 64, 4), W("t2", 0, 16), A.min), "wr t2", "mn")
+        at("least")
         V(ts(T.pos[:], W("mn", 0, 16), OWN, None, A.add), "mn", "pos")
-        if t == 0:
-            act(col(S0), col(ELEM), "pc", "s0", bias=3072.0)
-            act(col(OFFC), col(ELEM), "pc", "offc", bias=4092.0)
-            act(T.wr4[:], T.wr4[:], "wr4", "wr4", bias=-256.0)
-            act(col(SLOTC), col(SUB), "pc s0", "slotc", IDENT, scale=-1024.0, bias=col(S0))
-            act(col(CM), col(SUB), "pc", "cm", scale=256.0, bias=159.0)
-            act(W("jn"), T.n4x[:], "n4x ca", "jn", IDENT, bias=col(CA))
-            act(T.mrow[:], T.row[:, 0:256].indirect(T.mo[:, 0:16]), "row mo", "mrow")
+        at("offsets")
         V(cp(T.sl[:, 0:512].indirect(T.pos[:, 0:16]), T.lam[:, 0:256]), "pos lam", "sl")
+        at("scatter")
         V(scan(T.ws96[:], T.wr4[:, 0:96], T.sl[:, 0:96], 0.0, A.add, A.min), "wr4 sl", "ws96")
+        at("slots")
         V(ts(T["slot%d" % t][:], T.ws96[:, 3:96:4], 4.0, col(SLOTC), A.mult, A.add), "ws96 slotc", "slot")
-        order("G", [writer["slot"]])
-        g.remote_dma(T["land%d" % t][:], T["slot%d" % t][:], T.sem["al%d" % t], T.sem.loc, pid, rid, mask)
+        send(T["land%d" % t][:], T["slot%d" % t][:], "al%d" % t, "slot")
         writer["hq"] = ("ah%d" % t, 2 * neng, {})
         writer["land"] = ("al%d" % t, neng, {})
         for b, bank in enumerate(("b3", "k3", "b0", "k2")):
             mm(bank, "e", 128 * b, "h%d" % t, 0, 256, "hq")
             act(T.hh[:, b:1024:4], T[bank][:, 0:256], bank, "h%d" % b)
         V(scan(W("cum1"), T.b1[:, q64], T.zero[:, q64], 0.0, A.add, A.add), "b1 zero", "cum1")
-        if t == 0:
-            V(scan(T.raw[:], T.wr4[:], T.mrow[:], 0.0, A.add, A.min), "wr4 mrow", "raw")
-        V(tt(W("kk"), T.b2[:, q64], W("cum1"), A.add), "b2 cum1", "kk")
-        if t == 0:
-            V(tt(W("a1"), T.raw[:, 3:256:4], W("jn"), A.add), "raw jn", "a1")
-            V(ts(T.wr16[:], T.i16[:], col(RES), 4352.0, A.is_equal, A.mult), "i16 pc", "wr16")
-            V(ts(T.dm0[:], W("a1"), -1.0, col(CM), A.mult, A.add), "a1 cm", "dm0")
-            V(ts(T.wr16[:], T.wr16[:], -256.0, None, A.add), "wr16", "wr16")
-            turn("dm", "ld_dm", "dm0")
         V(ts(W("u1s"), T.k1[:, q64], -512.0, None, A.is_le), "k1", "u1s")
-        V(ts(W("t6"), W("kk"), OWN - 96.0, 96.0, A.is_le, A.mult), "kk", "t6")
+        V(tt(W("kk"), T.b2[:, q64], W("cum1"), A.add), "b2 cum1", "kk")
         V(tt(W("a1"), W("u1s"), T["dm%d" % t][:], A.mult), "u1s dm%d" % t, "a1")
+        V(ts(W("t6"), W("kk"), OWN - 96.0, 96.0, A.is_le, A.mult), "kk", "t6")
         V(ts(W("t7"), W("kk"), OWN - 192.0, 96.0, A.is_le, A.mult), "kk", "t7")
-        V(tt(W("sm"), W("kk"), W("t6"), A.add), "kk t6", "sm")
         V(tt(W("an"), W("a1"), W("jn"), A.add), "a1 jn", "an")
+        V(tt(W("sm"), W("kk"), W("t6"), A.add), "kk t6", "sm")
+        last = t == R - 1
+        at("travel")
+        if last:
+            V(ts(W("t1"), T.k0[:, q64], -512.0, 1.0, A.is_le, A.add), "k0", "t1")
+            V(ts(W("t2"), W("kk"), 512.0, 2.0, A.is_ge, A.mult), "kk", "t2")
         V(tt(W("gn"), W("sm"), W("t7"), A.add), "sm t7", "gn")
-        if t == 0:
-            V(scan(T.raw[:], T.wr16[:], T.iv[:], 0.0, A.add, A.min), "wr16 iv", "raw")
+        if last:
+            V(tt(W("pp2"), W("t1"), W("u1s"), A.add), "t1 u1s", "pp2")
         V(tt(W("ff"), W("gn"), W("an"), A.max), "gn an", "ff")
-        if t == 0:
-            V(ts(T.ls0[:, 0:16], T.raw[:, 15:256:16], col(CI), None, A.add), "raw ci ls0", "ls0")
-            turn("ls", "ld_ls", "ls0")
+        if last:
+            V(tt(W("pp3"), W("pp2"), W("t2"), A.add), "pp2 t2", "pp3")
         V(ts(T.off[:], W("ff"), -4.0, col(OFFC), A.mult, A.add), "ff offc", "off")
-        if t == 0:
-            V(fill(T.hh[:, 1024:1040], 0.0), "", "hz")
-        elif t == 1:
-            quant("v", T.v0[:], 0, 128, "v0", "qv")
-        else:
-            V(ts(W("t6"), T.k0[:, q64], -512.0, 1.0, A.is_le, A.add), "k0", "t6")
-            V(ts(W("t7"), W("kk"), 512.0, 2.0, A.is_ge, A.mult), "kk", "t7")
-            V(tt(W("sm"), W("t6"), W("u1s"), A.add), "t6 u1s", "sm")
-            V(tt(W("an"), W("sm"), W("t7"), A.add), "sm t7", "an")
-            V(lambda: g.vector.transpose(W("gn"), W("an")), "an", "gn")
-            act(T.wc16[:], W("gn", 0, 64, 4), "gn", "wc16")
+        if last:
+            V(lambda: g.vector.transpose(W("m21"), W("pp3")), "pp3", "m21")
+            V(cp(T.wc16[:], W("m21", 0, 64, 4)), "m21", "wc16")
             for k in range(4):
                 dma("S", T.wv[k % 2:8:2, 128 * (k // 2):128 * (k // 2) + 128], T.wc16[:, 4 * k:4 * k + 4], "st", "wc16")
+        if t == 1:
+            quant("v", T.v0[:], 0, 128, "v0", "qv")
         r = "h0 h1 h2 h3 hz land"
         V(cp(T.fg[:, 0:192], T.hh[:, 0:1040].indirect(T["land%d" % t][:, 0:12])), r, "g0")
         act(T.fg[:, 192:384], T.hh[:, 0:1040].indirect(T["land%d" % t][:, 12:24]), r, "g1")
-        r = fs + " g0 g1 off"
-        V(cp(T.z[:, 0:512], T.fg[:, 0:1408].indirect(T.off[:, 0:32])), r, "z0")
-        act(T.z[:, 512:1024], T.fg[:, 0:1408].indirect(T.off[:, 32:64]), r, "z1")
+        at("guests")
+        r = " ".join(fs) + " g0 g1 off"
         for h in (0, 1):
-            quant("z", T.z[:, 512 * h:512 * h + 512], 128 * h, 128 * h + 128, "z%d" % h, "qz%d" % h)
-        for b, h in ((0, 0), (1, 0), (0, 1), (1, 1), (2, 0), (2, 1), (3, 0), (3, 1)):
-            mm("bk"[h] + "%d" % b, "w", 128 * b, "z", 128 * h, 128 * h + 128, "qw sw qz%d" % h)
-        for b in (0, 1, 3):
-            act(T.z32[:, 256 * b:256 * b + 256], T.z[:, b:1024:4], "z0 z1", "y%d" % b, scale=32.0)
-        V(ts(T.z32[:, 512:768], T.z[:, 2:1024:4], 32.0, None, A.mult), "z0 z1", "y2")
-        for b in range(4):
-            for h in (0, 1):
-                bank, a = "bk"[h] + "%d" % b, 256 * b + 128 * h
-                V(tt(T["tt%d" % b][:, 128 * h:128 * h + 128], T[bank][:, 0:128], T.z32[:, a:a + 128], A.add), bank + " y%d" % b, "tt%d%d" % (b, h))
-        for h in (0, 1):
+            a, m, e = FILL[h]
+            V(cp(T.z[:, 16 * a:16 * m], T.fg[:, 0:1408].indirect(T.off[:, a:m])), r, "zv%d" % h)
+            act(T.z[:, 16 * m:16 * e], T.fg[:, 0:1408].indirect(T.off[:, m:e]), r, "za%d" % h)
+            at("fill%d" % h)
+            quant("z", T.z[:, 512 * h:512 * h + 512], 128 * h, 128 * h + 128, "zv%d za%d" % (h, h), "qz%d" % h)
             for b in range(4):
-                src = T["tt%d" % b][:, 0:256].indirect(T["ls%d" % t][:, 8 * h:8 * h + 8])
-                out, r, w = T.xt[:, 512 * h + b:512 * h + 512:4], "tt%d0 tt%d1" % (b, b) + lst, "xs%d%d" % (b, h)
-                if b == 3:
-                    V(ts(out, src, 0.03125, None, A.mult), r, w)
-                else:
-                    act(out, src, r, w, scale=0.03125)
-            quant_x(h, T.xt, " ".join(xs[4 * h:4 * h + 4]))
+                mm("bk"[h] + "%d" % b, "w", 128 * b, "z", 128 * h, 128 * h + 128, "qw sw qz%d" % h)
+        for q, b, h in SCALE:
+            a = 512 * h + 128 * b
+            out, src, r, w = T.z32[:, a:a + 128], T.z[:, 512 * h + b:512 * h + 512:4], "zv%d za%d" % (h, h), "y%d%d" % (b, h)
+            if q == "V":
+                V(ts(out, src, 32.0, None, A.mult), r, w)
+            else:
+                act(out, src, r, w, scale=32.0)
+        for b, h in SUMS:
+            bank, a = "bk"[h] + "%d" % b, 512 * h + 128 * b
+            V(tt(T["tt%d" % b][:, 128 * h:128 * h + 128], T[bank][:, 0:128], T.z32[:, a:a + 128], A.add), bank + " y%d%d" % (b, h), "tt%d%d" % (b, h))
+        for q, b, a, e in SHARES:
+            if q == "Q":
+                quant_x(b, T.xt, " ".join("xs%d%d" % (k[1], k[2]) for k in SHARES if k[0] != "Q" and k[2] < e and k[3] > a))
+                continue
+            src = T["tt%d" % b][:, 0:256].indirect(T["ls%d" % t][:, a:e])
+            out, r, w = T.xt[:, 64 * a + b:64 * e:4], "tt%d0 tt%d1" % (b, b) + lst, "xs%d%d" % (b, a)
+            if q == "V":
+                V(ts(out, src, 0.03125, None, A.mult), r, w)
+            else:
+                act(out, src, r, w, scale=0.03125)
     for h in (0, 1):
         dma("S", T.oc[:, 512 * h:512 * h + 512], T.qx[:, 128 * h:128 * h + 128].bitcast(dt.uint8), "st", "qx%d" % h)
         mm("k%d" % h, "v", 0, "x", 128 * h, 128 * h + 128, "qv qx%d" % h)

@@ -7,7 +7,8 @@ NEVER = -1e29
 SMALL = "md md4 dump jn cum1 cum2 cum3 x1 pp2 pp3 t1 t2 m21 wm mn wr kk u1s a1 an t6 t7 sm gn ff".split()
 SHARES = (("A", 0, 0, 8), ("A", 1, 0, 8), ("V", 2, 0, 8), ("V", 3, 0, 8), ("A", 0, 8, 16), ("A", 1, 8, 16), ("A", 2, 8, 16),
           ("V", 3, 8, 12), ("Q", 0, 0, 8), ("V", 3, 12, 16), ("Q", 1, 8, 16))
-SCALE = (("A", 0, 0), ("A", 1, 0), ("V", 2, 0), ("V", 3, 0), ("A", 0, 1), ("A", 1, 1), ("A", 2, 1), ("A", 3, 1))
+SCALE = (("V", 0, 0), ("V", 1, 0), ("A", 2, 0), ("A", 0, 1), ("A", 3, 0), ("A", 1, 1), ("A", 2, 1), ("A", 3, 1))
+EARLY = 2
 SUMS = ((0, 0), (1, 0), (2, 0), (0, 1), (3, 0), (1, 1), (2, 1), (3, 1))
 FILL = ((0, 16, 32), (32, 44, 64))
 
@@ -170,9 +171,10 @@ def rank_program(g, core, T, topo):
     op("G", lambda: g.affine_select(T.eb[:], T.zero[:], [[-1, 528]], A.not_equal, 1.0, 3, 4), ["zero"], ["eb"])
     iota("pick8i", [[16, 8]], 0, 0)
     iota("row", [[1, 256]], 0, 0)
-    iota("i16", [[0, 16], [1, 16]], 0, 0)
-    iota("n16", [[16, 16], [0, 4]], 0, 0)
     iota("n4x", [[-4, 64]], -100, 0)
+    iota("n16", [[16, 16], [0, 4]], 0, 0)
+    op("G", lambda: g.iota(T.tu[:, 512:1024], [[0, 512]], 0, 0, allow_small_or_imprecise_dtypes=True), [], ["tz2"])
+    iota("i16", [[0, 16], [1, 16]], 0, 0)
     iota("lam", [[16, 16], [1, 4], [4, 4]], 0, 0)
     V(ts(T.pi[:, 0:1], T.pi[:, 4:5], 15, None, A.bitwise_and), "pi4", "pi0")
     V(ts(T.pi[:, 1:2], T.pi[:, 4:5], 2, 3, A.logical_shift_right, A.bitwise_and), "pi4", "pi1")
@@ -194,7 +196,6 @@ def rank_program(g, core, T, topo):
         for k in range(8):
             kw = {"scale": T.gsel[:, k:k + 1]} if j else {}
             act(T.ct[:, 512 * j + 64 * k:512 * j + 64 * k + 64], T[src][:], src + (" gsel" if j else ""), "c%d%d" % (j, k), **kw)
-    op("G", lambda: g.iota(T.tu[:, 512:1024], [[0, 512]], 0, 0, allow_small_or_imprecise_dtypes=True), [], ["tz2"])
     V(tt(W("md"), T.nm[:, 0:64], T.nm[:, 1:65], A.subtract), "nm0 nm", "md")
     for b in range(4):
         quant("e", T.eb[:, 3 - b:515 - b], 128 * b, 128 * b + 128, "eb", "qe%d" % b)
@@ -203,12 +204,13 @@ def rank_program(g, core, T, topo):
     act(col(DUMP), col(RES), "pc", "cdump", bias=256.0 - OWN)
     act(W("md4"), W("md"), "md", "md4", bias=4.0)
     act(col(INIT1), T.nm[:, 64:65], "nm ca", "init1", IDENT, scale=-1.0, bias=col(CA))
-    act(T.tu[:, 256:512], T.zero[:, 0:256], "zero", "tz")
     V(cp(T.mo[:], T.mi[:]), "mi", "mo")
     V(ts(T.mq[:], T.mi[:], 2, None, A.logical_shift_right), "mi", "mq")
     act(T.thr0[:], T.pat[:, 0:256].indirect(T.mo[:, 0:16]), "pat mo", "thr0")
     quant("c", T.ct[:, 0:512], 0, 128, " ".join("c0%d" % k for k in range(8)), "qc0")
     V(cp(T.ls0[:, 16:32], T.mq[:]), "mq", "ls0")
+    V(fill(T.tu[:, 256:512], 0.0), "", "tz")
+    V(ts(T.wr4[:], T.pat[:], 1024.0, -256.0, A.add, A.max), "pat", "wr4")
 
     def quant_x(h, src, r):
         quant("x", src[:, 512 * h:512 * h + 512], 128 * h, 128 * h + 128, r, "qx%d" % h)
@@ -218,43 +220,38 @@ def rank_program(g, core, T, topo):
     V(cp(T.qu16[:, 0:128].bitcast(dt.uint32), T.qu[:, 0:128].bitcast(dt.uint32).indirect(T.pick8[:, 0:8])), "qu pick8", "qu16")
     quant_x(1, T.x0, "x0b")
     act(T.su16[:, 0:128], T.su[:, 0:128].indirect(T.pick8[:, 0:8]), "qu pick8", "su16")
-    act(T.wr4[:], T.pat[:], "pat", "wr4", ActivationFunctionType.Relu, bias=1280.0)
-    act(W("dump"), T.nm[:, 1:65], "nm cdump", "dump", IDENT, scale=2.0, bias=col(DUMP))
-    act(T.wr4[:], T.wr4[:], "wr4", "wr4", bias=-256.0)
+    act(T.mrow[:], T.row[:, 0:256].indirect(T.mo[:, 0:16]), "row mo", "mrow")
+    act(W("jn"), T.n4x[:], "n4x ca", "jn", IDENT, bias=col(CA))
+    act(col(CM), col(SUB), "pc", "cm", scale=256.0, bias=159.0)
     turn("thr", "ld_thr", "thr0")
+    quant("c", T.ct[:, 512:1536], 128, 384, " ".join("c%d%d" % (j, k) for j in (1, 2) for k in range(8)), "qc1")
 
     def late_constants():
-        act(T.mrow[:], T.row[:, 0:256].indirect(T.mo[:, 0:16]), "row mo", "mrow")
         act(T.wr16[:], T.i16[:], "i16 pc", "wr16", ActivationFunctionType.Abs, scale=-1.0, bias=col(RES))
         act(col(S0), col(ELEM), "pc", "s0", bias=3072.0)
-        act(W("jn"), T.n4x[:], "n4x ca", "jn", IDENT, bias=col(CA))
         act(T.wr16[:], T.wr16[:], "wr16", "wr16", ActivationFunctionType.Relu, scale=-4352.0, bias=4352.0)
         act(col(SLOTC), col(SUB), "pc s0", "slotc", IDENT, scale=-1024.0, bias=col(S0))
-        act(col(CM), col(SUB), "pc", "cm", scale=256.0, bias=159.0)
         act(T.wr16[:], T.wr16[:], "wr16", "wr16", bias=-256.0)
         act(col(OFFC), col(ELEM), "pc", "offc", bias=4092.0)
         act(col(CI), col(RES), "pc", "ci", scale=-256.0, bias=3840.0)
 
+        act(T.hh[:, 1024:1040], T.zero[:, 0:16], "zero", "hz")
+
     def unwrap(src, steps, h, r):
         V(scan(T.raw[:, 128 * h:128 * h + 128], T[steps][:, 0:128], T[src][:, 128 * h:128 * h + 128], 0.0, A.add, A.min), r, "raw%d" % h)
-
-    def partners():
-        V(ts(T.dm0[:], W("a1"), -1.0, col(CM), A.mult, A.add), "a1 cm", "dm0")
-        turn("dm", "ld_dm", "dm0")
 
     def inverse():
         V(ts(T.ls0[:, 0:16], T.raw[:, 15:256:16], col(CI), None, A.add), "raw0 raw1 ci ls0", "ls0")
         turn("ls", "ld_ls", "ls0")
+        turn("dm", "ld_dm", "dm0")
 
     once = {
-        "count": lambda: quant("c", T.ct[:, 512:1536], 128, 384, " ".join("c%d%d" % (j, k) for j in (1, 2) for k in range(8)), "qc1"),
-        "licence": lambda: V(tt(W("dump"), W("dump"), T.n16[:], A.add), "dump n16", "dump"),
-        "unpacked": late_constants,
-        "place": lambda: unwrap("mrow", "wr4", 0, "wr4 mrow"),
-        "least": lambda: unwrap("mrow", "wr4", 1, "wr4 mrow"),
-        "offsets": lambda: V(tt(W("a1"), T.raw[:, 3:256:4], W("jn"), A.add), "raw0 raw1 jn", "a1"),
-        "scatter": partners,
-        "slots": lambda: V(fill(T.hh[:, 1024:1040], 0.0), "", "hz"),
+        "count": lambda: V(scan(T.raw[:], T.wr4[:], T.mrow[:], 0.0, A.add, A.min), "wr4 mrow", "raw0 raw1"),
+        "licence": lambda: V(tt(W("a1"), T.raw[:, 3:256:4], W("jn"), A.add), "raw0 raw1 jn", "a1"),
+        "unpacked": lambda: act(W("dump"), T.nm[:, 1:65], "nm cdump", "dump", IDENT, scale=2.0, bias=col(DUMP)),
+        "sent": lambda: V(tt(W("dump"), W("dump"), T.n16[:], A.add), "dump n16", "dump"),
+        "order": late_constants,
+        "slots": lambda: V(ts(T.dm0[:], W("a1"), -1.0, col(CM), A.mult, A.add), "a1 cm", "dm0"),
         "travel": lambda: V(cp(T.iv[:, 0:256].indirect(T.mo[:, 0:16]), T.row[:, 0:256]), "row mo", "iv"),
         "guests": lambda: unwrap("iv", "wr16", 0, "wr16 iv"),
         "fill0": lambda: unwrap("iv", "wr16", 1, "wr16 iv"),
@@ -268,6 +265,22 @@ def rank_program(g, core, T, topo):
         mm(bank, "e", 128 * b, "x", 128 * h, 128 * h + 128, "qe%d qx%d" % (b, h))
         act(T.fg[:, 384 + 512 * h + b:896 + 512 * h:4], T[bank][:, 0:128], bank, "f%d%d" % (b, h))
 
+    def scale_z(parts):
+        for q, b, h in parts:
+            a = 512 * h + 128 * b
+            out, src, r, w = T.z32[:, a:a + 128], T.z[:, 512 * h + b:512 * h + 512:4], "zv%d za%d" % (h, h), "y%d%d" % (b, h)
+            if q == "V":
+                V(ts(out, src, 32.0, None, A.mult), r, w)
+            else:
+                act(out, src, r, w, scale=32.0)
+
+    def store_y(h):
+        if h:
+            V(cp(T.yb[:, 128:256], T.k1[:, 0:128]), "k1", "yb1")
+        else:
+            act(T.yb[:, 0:128], T.k0[:, 0:128], "k0", "yb0")
+        dma("S", T.y[:, 128 * h:128 * h + 128], T.yb[:, 128 * h:128 * h + 128], "st", "yb%d" % h)
+
     def send(out, in_, sem, tok):
         order("G", [writer[tok]])
         g.remote_dma(out, in_, T.sem[sem], T.sem.loc, pid, rid, mask)
@@ -280,13 +293,11 @@ def rank_program(g, core, T, topo):
             if t == 0:
                 once[place]()
         mm("k0", "u16", 0, "x", 0, 128, "qu16 su16 qx0")
-        for b in range(2 if t else 0):
+        for b in range(1 if t else 0):
             unpack(b, 0, "b%d" % b)
         mm("k1", "u16", 0, "x", 128, 256, "qu16 su16 qx1")
-        for b in range(2 if t else 0, 4):
+        for b in range(1 if t else 0, 4):
             unpack(b, 0, "b%d" % b)
-        if t:
-            unpack(0, 1, "k3")
         for h in (0, 1):
             V(tt(T.tu[:, 128 * h:128 * h + 128], T["k%d" % h][:, 0:128], T["thr%d" % t][:, 128 * h:128 * h + 128], A.is_le),
               "k%d thr%d" % (h, t), "u1%d" % h)
@@ -294,10 +305,11 @@ def rank_program(g, core, T, topo):
         quant("1", T.tu[:, 0:512], 0, 128, "u10 u11 tz", "q1")
         mm("k2", "c", 0, "1", 0, 128, "qc0 q1")
         at("count")
-        for b in range(1 if t else 0, 4):
-            unpack(b, 1, ("k3", "b0", "b1", "b2")[b])
-        at("unpacked")
+        for b in range(3):
+            unpack(b, 1, ("k3", "b0", "b1")[b])
         mm("k0", "c", 128, "1", 0, 128, "qc1 q1")
+        unpack(3, 1, "b2")
+        at("unpacked")
         mm("k1", "c", 256, "1", 0, 128, "qc1 q1")
         V(ts(T.nl1[:], T.k2[:, q64], 3.5, -1.0, A.is_ge, A.mult), "k2", "nl1")
         at("licence")
@@ -313,12 +325,14 @@ def rank_program(g, core, T, topo):
         quant("f%d" % t, T.fg[:, 384:1408], 0, 256, " ".join(fs), "qf")
         send(T["qh%d" % t][:].bitcast(dt.uint8), T["qf%d" % t][:].bitcast(dt.uint8), "ah%d" % t, "qf")
         send(T["sh%d" % t][:], T["sf%d" % t][:], "ah%d" % t, "qf")
+        at("sent")
         V(ts(T.nl2[:], T.k2[:, q64], -3.5, -1.0, A.is_gt, A.mult), "k2", "nl2")
         V(tt(W("x1"), T.k1[:, q64], W("cum1"), A.add), "k1 cum1", "x1")
         V(tt(T.tu[:, 512:768], T.nl2[:, q64].indirect(moq), T.tu[:, 256:512], A.mult), "nl2 u2" + lst, "u3")
         V(scan(W("cum2"), T.k3[:, q64], W("md"), T.nm[:, 64:65], A.add, A.add), "k3 md nm", "cum2")
         quant("3", T.tu[:, 512:1024], 0, 128, "u3", "q3")
         act(W("t1"), W("x1"), "x1 cum2", "t1", IDENT, scale=-1.0, bias=W("cum2", 63))
+        at("order")
         mm("k2", "c", 128, "3", 0, 128, "q3")
         mm("k0", "c", 256, "3", 0, 128, "q3")
         mm("b1", "c", 128, "3", 0, 128, "q3", False, True)
@@ -330,13 +344,13 @@ def rank_program(g, core, T, topo):
         V(tt(W("pp3"), T.k0[:, q64], W("cum3"), A.add), "k0 cum3", "pp3")
         V(ts(W("t2", 0, 16), W("wm", 3, 64, 4), W("cum3", 63), None, A.add), "wm cum3", "t2")
         V(scan(W("wr"), W("dump"), W("pp3"), -HUGE, A.max, A.min), "dump pp3", "wr")
-        at("place")
+        V(ts(W("u1s"), T.k1[:, q64], -512.0, None, A.is_le), "k1", "u1s")
         V(tt(W("mn", 0, 16), W("wr", 3, 64, 4), W("t2", 0, 16), A.min), "wr t2", "mn")
-        at("least")
+        V(scan(W("cum1"), T.b1[:, q64], T.zero[:, q64], 0.0, A.add, A.add), "b1 zero", "cum1")
         V(ts(T.pos[:], W("mn", 0, 16), OWN, None, A.add), "mn", "pos")
-        at("offsets")
+        V(tt(W("kk"), T.b2[:, q64], W("cum1"), A.add), "b2 cum1", "kk")
         V(cp(T.sl[:, 0:512].indirect(T.pos[:, 0:16]), T.lam[:, 0:256]), "pos lam", "sl")
-        at("scatter")
+        V(ts(W("t6"), W("kk"), OWN - 96.0, 96.0, A.is_le, A.mult), "kk", "t6")
         V(scan(T.ws96[:], T.wr4[:, 0:96], T.sl[:, 0:96], 0.0, A.add, A.min), "wr4 sl", "ws96")
         at("slots")
         V(ts(T["slot%d" % t][:], T.ws96[:, 3:96:4], 4.0, col(SLOTC), A.mult, A.add), "ws96 slotc", "slot")
@@ -346,14 +360,10 @@ def rank_program(g, core, T, topo):
         for b, bank in enumerate(("b3", "k3", "b0", "k2")):
             mm(bank, "e", 128 * b, "h%d" % t, 0, 256, "hq")
             act(T.hh[:, b:1024:4], T[bank][:, 0:256], bank, "h%d" % b)
-        V(scan(W("cum1"), T.b1[:, q64], T.zero[:, q64], 0.0, A.add, A.add), "b1 zero", "cum1")
-        V(ts(W("u1s"), T.k1[:, q64], -512.0, None, A.is_le), "k1", "u1s")
-        V(tt(W("kk"), T.b2[:, q64], W("cum1"), A.add), "b2 cum1", "kk")
         V(tt(W("a1"), W("u1s"), T["dm%d" % t][:], A.mult), "u1s dm%d" % t, "a1")
-        V(ts(W("t6"), W("kk"), OWN - 96.0, 96.0, A.is_le, A.mult), "kk", "t6")
+        V(tt(W("sm"), W("kk"), W("t6"), A.add), "kk t6", "sm")
         V(ts(W("t7"), W("kk"), OWN - 192.0, 96.0, A.is_le, A.mult), "kk", "t7")
         V(tt(W("an"), W("a1"), W("jn"), A.add), "a1 jn", "an")
-        V(tt(W("sm"), W("kk"), W("t6"), A.add), "kk t6", "sm")
         last = t == R - 1
         at("travel")
         if last:
@@ -383,22 +393,23 @@ def rank_program(g, core, T, topo):
             V(cp(T.z[:, 16 * a:16 * m], T.fg[:, 0:1408].indirect(T.off[:, a:m])), r, "zv%d" % h)
             act(T.z[:, 16 * m:16 * e], T.fg[:, 0:1408].indirect(T.off[:, m:e]), r, "za%d" % h)
             at("fill%d" % h)
+            if h:
+                scale_z(SCALE[:EARLY])
             quant("z", T.z[:, 512 * h:512 * h + 512], 128 * h, 128 * h + 128, "zv%d za%d" % (h, h), "qz%d" % h)
             for b in range(4):
                 mm("bk"[h] + "%d" % b, "w", 128 * b, "z", 128 * h, 128 * h + 128, "qw sw qz%d" % h)
-        for q, b, h in SCALE:
-            a = 512 * h + 128 * b
-            out, src, r, w = T.z32[:, a:a + 128], T.z[:, 512 * h + b:512 * h + 512:4], "zv%d za%d" % (h, h), "y%d%d" % (b, h)
-            if q == "V":
-                V(ts(out, src, 32.0, None, A.mult), r, w)
-            else:
-                act(out, src, r, w, scale=32.0)
+        scale_z(SCALE[EARLY:])
         for b, h in SUMS:
             bank, a = "bk"[h] + "%d" % b, 512 * h + 128 * b
             V(tt(T["tt%d" % b][:, 128 * h:128 * h + 128], T[bank][:, 0:128], T.z32[:, a:a + 128], A.add), bank + " y%d%d" % (b, h), "tt%d%d" % (b, h))
         for q, b, a, e in SHARES:
             if q == "Q":
+                if last and b:
+                    store_y(0)
                 quant_x(b, T.xt, " ".join("xs%d%d" % (k[1], k[2]) for k in SHARES if k[0] != "Q" and k[2] < e and k[3] > a))
+                if last:
+                    dma("S", T.oc[:, 512 * b:512 * b + 512], T.qx[:, 128 * b:128 * b + 128].bitcast(dt.uint8), "st", "qx%d" % b)
+                    mm("k%d" % b, "v", 0, "x", 128 * b, 128 * b + 128, "qv qx%d" % b)
                 continue
             src = T["tt%d" % b][:, 0:256].indirect(T["ls%d" % t][:, a:e])
             out, r, w = T.xt[:, 64 * a + b:64 * e:4], "tt%d0 tt%d1" % (b, b) + lst, "xs%d%d" % (b, a)
@@ -406,14 +417,9 @@ def rank_program(g, core, T, topo):
                 V(ts(out, src, 0.03125, None, A.mult), r, w)
             else:
                 act(out, src, r, w, scale=0.03125)
-    for h in (0, 1):
-        dma("S", T.oc[:, 512 * h:512 * h + 512], T.qx[:, 128 * h:128 * h + 128].bitcast(dt.uint8), "st", "qx%d" % h)
-        mm("k%d" % h, "v", 0, "x", 128 * h, 128 * h + 128, "qv qx%d" % h)
     for k in range(4):
         dma("A", T.osc[4 * k:4 * k + 4, :], T.sx[32 * k:32 * k + 4, :], "st2", "qx0 qx1")
-    for h in (0, 1):
-        V(cp(T.yb[:, 128 * h:128 * h + 128], T["k%d" % h][:, 0:128]), "k%d" % h, "yb%d" % h)
-        dma("S", T.y[:, 128 * h:128 * h + 128], T.yb[:, 128 * h:128 * h + 128], "st", "yb%d" % h)
+    store_y(1)
     g.wait_ge(T.sem.loc, 3 * R * neng)
     for s in sorted(count):
         g.wait_ge(T.sem[s], count[s])

@@ -4,13 +4,16 @@ R = 3
 HUGE = 4096.0
 OWN = 1023.0
 NEVER = -1e29
-SMALL = "md md4 dump jn cum1 cum2 cum3 x1 pp2 pp3 t1 t2 m21 wm mn wr kk u1s a1 an t6 t7 sm gn ff".split()
-SHARES = (("A", 0, 0, 8), ("A", 1, 0, 8), ("V", 2, 0, 8), ("V", 3, 0, 8), ("A", 0, 8, 16), ("A", 1, 8, 16), ("A", 2, 8, 16),
-          ("V", 3, 8, 12), ("Q", 0, 0, 8), ("V", 3, 12, 16), ("Q", 1, 8, 16))
-SCALE = (("V", 0, 0), ("V", 1, 0), ("A", 2, 0), ("A", 0, 1), ("A", 3, 0), ("A", 1, 1), ("A", 2, 1), ("A", 3, 1))
+SMALL = "md md4 jn cum1 cum2 cum3 x1 pp2 pp3 t1 t2 m21 kk u1s a1 an t6 t7 sm gn ff".split()
+SHARES = (("A", 0, 0, 16), ("A", 1, 0, 16), ("A", 2, 8, 16),
+          ("V", 2, 0, 8), ("V", 3, 0, 8), ("V", 3, 8, 16), ("Q", 0, 0, 8), ("Q", 1, 8, 16))
+SCALE = (("V", 2, 0), ("V", 1, 0), ("A", 0, 0), ("A", 0, 1), ("A", 2, 1), ("A", 1, 1), ("A", 3, 1), ("A", 3, 0))
 EARLY = 2
-SUMS = ((0, 0), (1, 0), (2, 0), (0, 1), (3, 0), (1, 1), (2, 1), (3, 1))
-FILL = ((0, 16, 32), (32, 44, 64))
+LOOK = 16
+FIRST = 3
+UNPACK = ((0, 4, 7), (0, 4, 8))
+SUMS = ((2, 0), (1, 0), (0, 0), (0, 1), (2, 1), (1, 1), (3, 1), (3, 0))
+FILL = ((0, 18, 32), (38, 42, 64))
 
 
 def _scratch():
@@ -30,9 +33,9 @@ def _scratch():
     sb("bfloat16", 1024, "x0 z z32 xt tu")
     sb("bfloat16", 528, "eb zero")
     sb("bfloat16", 512, "u0 v0 sl")
-    sb("bfloat16", 256, "row lam i4 i16 pat wr4 wr16 iv mrow thr0 thr1 thr2 tt0 tt1 tt2 tt3")
+    sb("bfloat16", 256, "far row lam i4 i16 pat wr4 wr16 iv mrow thr0 thr1 thr2 tt0 tt1 tt2 tt3")
     sb("bfloat16", 64, "d64 e0 wb0 wb1 wb quarter nl1 nl2")
-    sb("uint16", 32, "ls0 ls1 ls2")
+    sb("uint16", 16, "ls0 ls1 ls2 inv0 inv1 inv2")
     sb("uint16", 16, "mo pos")
     sb("uint16", 64, "off")
     sb("uint16", 24, "slot0 slot1 slot2 land0 land1 land2")
@@ -44,7 +47,8 @@ def _scratch():
     sb("float32", 72, "nm")
     sb("float32", 64, "n16 n4x dm0 dm1 dm2")
     sb("float32", 64 * len(SMALL), "small")
-    sb("float32", 96, "ws96")
+    sb("float16", 96, "ws96")
+    sb("float32", 128, "dump pair least")
     sb("float32", 256, "raw yb")
     for n in "k0 k1 k2 k3 b0 b1 b2 b3".split():
         s[n] = ("psum", [128, 512], "float32")
@@ -52,7 +56,7 @@ def _scratch():
 
 
 SCRATCH = _scratch()
-LOADS = ["u", "xa", "xb", "v", "wc", "ws", "m", "thr", "ls", "dm"]
+LOADS = ["u", "xa", "xb", "v", "wc", "ws", "m", "thr", "ls", "inv", "dm"]
 SEMAPHORES = ["sV", "sT", "sA", "sG", "loc", "st", "st2"] + ["ld_" + n for n in LOADS] + ["ah0", "ah1", "ah2", "al0", "al1", "al2"]
 
 
@@ -158,112 +162,136 @@ def rank_program(g, core, T, topo):
 
     dma("S", T.mi[:], T.m[:], "ld_m", "", "mi")
     dma("A", T.u0[:], T.u[:], "ld_u", "", "u0")
-    dma("S", T.x0[:, 0:512], T.x[:, 0:512], "ld_xa", "", "x0a")
-    dma("A", T.x0[:, 512:1024], T.x[:, 512:1024], "ld_xb", "", "x0b")
-    dma("S", T.qw[:].bitcast(dt.uint8), T.wc[:], "ld_wc", "x0a x0b", "qw")
-    dma("S", T.sw[:], T.ws[:], "ld_ws", "", "sw")
-    dma("S", T.v0[:], T.v[:], "ld_v", "", "v0")
 
     op("G", lambda: g.iota(T.pi[:, 4:5], [[0, 1]], 0, 1), [], ["pi4"])
     iota("d64", [[-1, 4], [0, 4], [1, 4]], 0, 0)
     iota("i8", [[1, 8]], 0, 0)
+    iota("pick8i", [[16, 8]], 0, 0)
     V(fill(T.zero[:], 0.0), "", "zero")
     op("G", lambda: g.affine_select(T.eb[:], T.zero[:], [[-1, 528]], A.not_equal, 1.0, 3, 4), ["zero"], ["eb"])
-    iota("pick8i", [[16, 8]], 0, 0)
     iota("row", [[1, 256]], 0, 0)
-    iota("n4x", [[-4, 64]], -100, 0)
     iota("n16", [[16, 16], [0, 4]], 0, 0)
-    op("G", lambda: g.iota(T.tu[:, 512:1024], [[0, 512]], 0, 0, allow_small_or_imprecise_dtypes=True), [], ["tz2"])
-    iota("i16", [[0, 16], [1, 16]], 0, 0)
+    iota("n4x", [[-4, 64]], -100, 0)
     iota("lam", [[16, 16], [1, 4], [4, 4]], 0, 0)
+    iota("i16", [[0, 16], [1, 16]], 0, 0)
     V(ts(T.pi[:, 0:1], T.pi[:, 4:5], 15, None, A.bitwise_and), "pi4", "pi0")
     V(ts(T.pi[:, 1:2], T.pi[:, 4:5], 2, 3, A.logical_shift_right, A.bitwise_and), "pi4", "pi1")
     V(ts(T.pi[:, 2:3], T.pi[:, 4:5], 3, None, A.bitwise_and), "pi4", "pi2")
     V(ts(T.pi[:, 3:4], T.pi[:, 4:5], 4, None, A.logical_shift_right), "pi4", "pi3")
     V(ts(T.e0[:], T.d64[:], 0.0, 0.25, A.is_equal, A.mult), "d64", "e0")
+    dma("S", T.x0[:, 0:512], T.x[:, 0:512], "ld_xa", "pi3", "x0a")
+    dma("S", T.x0[:, 512:1024], T.x[:, 512:1024], "ld_xb", "", "x0b")
+    dma("S", T.qw[:].bitcast(dt.uint8), T.wc[:], "ld_wc", "x0a x0b", "qw")
+    dma("S", T.sw[:], T.ws[:], "ld_ws", "", "sw")
     V(cp(T.pc[:, 0:4], T.pi[:, 0:4]), "pi0 pi1 pi2 pi3", "pc")
-    V(ts(T.wb0[:], T.d64[:], 0.0, -0.25, A.is_gt, A.mult), "d64", "wb0")
-    V(ts(T.wb1[:], T.d64[:], 0.0, -256.0, A.is_equal, A.mult), "d64", "wb1")
-    V(ts(T.gsel[:], T.i8[:], col(GROUP), None, A.is_equal), "i8 pc", "gsel")
     V(fill(T.quarter[:], 0.25), "", "quarter")
-    V(tt(T.wb[:], T.wb0[:], T.wb1[:], A.add), "wb0 wb1", "wb")
+    V(ts(T.wb0[:], T.d64[:], 0.0, -0.25, A.is_gt, A.mult), "d64", "wb0")
+    V(ts(T.gsel[:], T.i8[:], col(GROUP), None, A.is_equal), "i8 pc", "gsel")
+    V(ts(T.wb1[:], T.d64[:], 0.0, -256.0, A.is_equal, A.mult), "d64", "wb1")
     for k in range(4):
         V(fill(T.i4[:, k:256:4], float(k)), "", "i4%d" % k)
-    V(fill(T.nm[:, 0:1], 0.0), "", "nm0")
+    V(tt(T.wb[:], T.wb0[:], T.wb1[:], A.add), "wb0 wb1", "wb")
     V(ts(T.pat[:], T.i4[:], col(SUB), NEVER, A.not_equal, A.mult), "i40 i41 i42 i43 pc", "pat")
-    V(ts(T.nm[:, 1:65], T.i4[:, 0:64], col(ELEM), -HUGE, A.not_equal, A.mult), "i40 i41 i42 i43 pc", "nm")
-    for j, src in enumerate(("e0", "quarter", "wb")):
+    V(cp(T.pick8[:], T.pick8i[:]), "pick8i", "pick8")
+
+    def tile_of_constants(j, src):
         for k in range(8):
             kw = {"scale": T.gsel[:, k:k + 1]} if j else {}
             act(T.ct[:, 512 * j + 64 * k:512 * j + 64 * k + 64], T[src][:], src + (" gsel" if j else ""), "c%d%d" % (j, k), **kw)
-    V(tt(W("md"), T.nm[:, 0:64], T.nm[:, 1:65], A.subtract), "nm0 nm", "md")
-    for b in range(4):
+
+    def quant_e(b):
         quant("e", T.eb[:, 3 - b:515 - b], 128 * b, 128 * b + 128, "eb", "qe%d" % b)
-    V(cp(T.pick8[:], T.pick8i[:]), "pick8i", "pick8")
-    act(col(CA), col(SUB), "pc", "ca", scale=-1.0, bias=1027.0)
-    act(col(DUMP), col(RES), "pc", "cdump", bias=256.0 - OWN)
-    act(W("md4"), W("md"), "md", "md4", bias=4.0)
-    act(col(INIT1), T.nm[:, 64:65], "nm ca", "init1", IDENT, scale=-1.0, bias=col(CA))
-    V(cp(T.mo[:], T.mi[:]), "mi", "mo")
-    V(ts(T.mq[:], T.mi[:], 2, None, A.logical_shift_right), "mi", "mq")
-    act(T.thr0[:], T.pat[:, 0:256].indirect(T.mo[:, 0:16]), "pat mo", "thr0")
-    quant("c", T.ct[:, 0:512], 0, 128, " ".join("c0%d" % k for k in range(8)), "qc0")
-    V(cp(T.ls0[:, 16:32], T.mq[:]), "mq", "ls0")
-    V(fill(T.tu[:, 256:512], 0.0), "", "tz")
-    V(ts(T.wr4[:], T.pat[:], 1024.0, -256.0, A.add, A.max), "pat", "wr4")
 
     def quant_x(h, src, r):
         quant("x", src[:, 512 * h:512 * h + 512], 128 * h, 128 * h + 128, r, "qx%d" % h)
 
+    tile_of_constants(0, "e0")
+    tile_of_constants(1, "quarter")
+    tile_of_constants(2, "wb")
+    V(fill(T.tu[:, 0:256], 0.0), "", "tz")
+    V(fill(T.nm[:, 0:1], 0.0), "", "nm0")
+    V(ts(T.nm[:, 1:65], T.i4[:, 0:64], col(ELEM), -HUGE, A.not_equal, A.mult), "i40 i41 i42 i43 pc", "nm")
+    V(ts(T.wr4[:], T.pat[:], 1024.0, -256.0, A.add, A.max), "pat", "wr4")
+    V(tt(W("md"), T.nm[:, 0:64], T.nm[:, 1:65], A.subtract), "nm0 nm", "md")
+    V(cp(T.mo[:], T.mi[:]), "mi", "mo")
+    V(ts(T.mq[:], T.mi[:], 2, None, A.logical_shift_right), "mi", "mq")
+    act(T.thr0[:], T.pat[:, 0:256].indirect(T.mo[:, 0:16]), "pat mo", "thr0")
+    quant("c", T.ct[:, 0:512], 0, 128, " ".join("c0%d" % k for k in range(8)), "qc0")
+    V(cp(T.ls0[:], T.mq[:]), "mq", "ls0")
+    quant_e(0)
+    quant_e(1)
+    turn("thr", "ld_thr", "thr0")
+    turn("ls", "ld_ls", "ls0")
     quant("u", T.u0[:], 0, 128, "u0", "qu")
-    quant_x(0, T.x0, "x0a")
+    quant_e(2)
     V(cp(T.qu16[:, 0:128].bitcast(dt.uint32), T.qu[:, 0:128].bitcast(dt.uint32).indirect(T.pick8[:, 0:8])), "qu pick8", "qu16")
+    quant_x(0, T.x0, "x0a")
     quant_x(1, T.x0, "x0b")
     act(T.su16[:, 0:128], T.su[:, 0:128].indirect(T.pick8[:, 0:8]), "qu pick8", "su16")
+    act(col(CA), col(SUB), "pc", "ca", scale=-1.0, bias=1027.0)
     act(T.mrow[:], T.row[:, 0:256].indirect(T.mo[:, 0:16]), "row mo", "mrow")
     act(W("jn"), T.n4x[:], "n4x ca", "jn", IDENT, bias=col(CA))
-    act(col(CM), col(SUB), "pc", "cm", scale=256.0, bias=159.0)
-    turn("thr", "ld_thr", "thr0")
+    quant_e(3)
     quant("c", T.ct[:, 512:1536], 128, 384, " ".join("c%d%d" % (j, k) for j in (1, 2) for k in range(8)), "qc1")
 
-    def late_constants():
-        act(T.wr16[:], T.i16[:], "i16 pc", "wr16", ActivationFunctionType.Abs, scale=-1.0, bias=col(RES))
-        act(col(S0), col(ELEM), "pc", "s0", bias=3072.0)
-        act(T.wr16[:], T.wr16[:], "wr16", "wr16", ActivationFunctionType.Relu, scale=-4352.0, bias=4352.0)
-        act(col(SLOTC), col(SUB), "pc s0", "slotc", IDENT, scale=-1024.0, bias=col(S0))
-        act(T.wr16[:], T.wr16[:], "wr16", "wr16", bias=-256.0)
-        act(col(OFFC), col(ELEM), "pc", "offc", bias=4092.0)
-        act(col(CI), col(RES), "pc", "ci", scale=-256.0, bias=3840.0)
+    act(W("md4"), W("md"), "md", "md4", bias=4.0)
+    act(col(INIT1), T.nm[:, 64:65], "nm ca", "init1", IDENT, scale=-1.0, bias=col(CA))
 
+    def masks():
+        act(col(DUMP), col(RES), "pc", "cdump", bias=256.0 - OWN)
+        act(col(CM), col(SUB), "pc", "cm", scale=256.0, bias=159.0)
+        act(W("t2"), T.nm[:, 1:65], "nm cdump", "t2", IDENT, scale=2.0, bias=col(DUMP))
+        act(T.dump[:, 1:128:2], T.zero[:, 0:64], "zero", "dump1", bias=-HUGE)
+        V(tt(W("a1"), T.raw[:, 3:256:4], W("jn"), A.add), "raw0 raw1 jn", "a1")
+
+    def invert(h):
+        V(cp(T.iv[:, 0:256].indirect(T.mo[:, 8 * h:8 * h + 8]), T.row[:, 128 * h:128 * h + 128]), "row mo", "iv")
+
+    def late_constants():
+        act(col(S0), col(ELEM), "pc", "s0", bias=3072.0)
+        act(T.wr16[:], T.i16[:], "i16 pc", "wr16", ActivationFunctionType.Abs, scale=-1.0, bias=col(RES))
+        act(col(SLOTC), col(SUB), "pc s0", "slotc", IDENT, scale=-1024.0, bias=col(S0))
+        act(T.wr16[:], T.wr16[:], "wr16", "wr16", ActivationFunctionType.Relu, scale=-4352.0, bias=4352.0)
+        act(col(OFFC), col(ELEM), "pc", "offc", bias=4092.0)
+        act(T.wr16[:], T.wr16[:], "wr16", "wr16", bias=-256.0)
+        act(col(CI), col(RES), "pc", "ci", scale=-256.0, bias=3840.0)
         act(T.hh[:, 1024:1040], T.zero[:, 0:16], "zero", "hz")
 
-    def unwrap(src, steps, h, r):
-        V(scan(T.raw[:, 128 * h:128 * h + 128], T[steps][:, 0:128], T[src][:, 128 * h:128 * h + 128], 0.0, A.add, A.min), r, "raw%d" % h)
-
     def inverse():
-        V(ts(T.ls0[:, 0:16], T.raw[:, 15:256:16], col(CI), None, A.add), "raw0 raw1 ci ls0", "ls0")
-        turn("ls", "ld_ls", "ls0")
+        V(ts(T.inv0[:], T.raw[:, 15:256:16], col(CI), None, A.add), "raw0 raw1 ci", "inv0")
+        turn("inv", "ld_inv", "inv0")
         turn("dm", "ld_dm", "dm0")
+        dma("S", T.v0[:], T.v[:], "ld_v", "", "v0")
 
     once = {
         "count": lambda: V(scan(T.raw[:], T.wr4[:], T.mrow[:], 0.0, A.add, A.min), "wr4 mrow", "raw0 raw1"),
-        "licence": lambda: V(tt(W("a1"), T.raw[:, 3:256:4], W("jn"), A.add), "raw0 raw1 jn", "a1"),
-        "unpacked": lambda: act(W("dump"), T.nm[:, 1:65], "nm cdump", "dump", IDENT, scale=2.0, bias=col(DUMP)),
-        "sent": lambda: V(tt(W("dump"), W("dump"), T.n16[:], A.add), "dump n16", "dump"),
+        "again": masks,
+        "waves": lambda: V(ts(T.dm0[:], W("a1"), -1.0, col(CM), A.mult, A.add), "a1 cm", "dm0"),
+        "counted": lambda: V(tt(T.dump[:, 0:128:2], W("t2"), T.n16[:], A.add), "t2 n16", "dump"),
         "order": late_constants,
-        "slots": lambda: V(ts(T.dm0[:], W("a1"), -1.0, col(CM), A.mult, A.add), "a1 cm", "dm0"),
-        "travel": lambda: V(cp(T.iv[:, 0:256].indirect(T.mo[:, 0:16]), T.row[:, 0:256]), "row mo", "iv"),
-        "guests": lambda: unwrap("iv", "wr16", 0, "wr16 iv"),
-        "fill0": lambda: unwrap("iv", "wr16", 1, "wr16 iv"),
-        "fill1": inverse,
+        "travel0": lambda: invert(0),
+        "travel1": lambda: invert(1),
+        "travel2": lambda: V(scan(T.raw[:], T.wr16[:], T.iv[:], 0.0, A.add, A.min), "wr16 iv", "raw0 raw1"),
+        "guests": inverse,
     }
 
     fs = ["f0%d f1%d f2%d f3%d" % (h, h, h, h) for h in (0, 1)]
-    q64 = slice(0, 64)
+    q64 = slice(64, 128)
 
-    def unpack(b, h, bank):
-        mm(bank, "e", 128 * b, "x", 128 * h, 128 * h + 128, "qe%d qx%d" % (b, h))
-        act(T.fg[:, 384 + 512 * h + b:896 + 512 * h:4], T[bank][:, 0:128], bank, "f%d%d" % (b, h))
+    def unpack(b, h, bank, half="TA"):
+        if "T" in half:
+            mm(bank, "e", 128 * b, "x", 128 * h, 128 * h + 128, "qe%d qx%d" % (b, h))
+        if "A" in half:
+            act(T.fg[:, 384 + 512 * h + b:896 + 512 * h:4], T[bank][:, 0:128], bank, "f%d%d" % (b, h))
+
+    def look_up(t, win, a, r, w, keep):
+        n, lists = 16 * LOOK, T["ls%d" % t]
+        if LOOK == 16:
+            V(tt(T.tu[:, a + 256:a + 512], T[win][:, 0:64].indirect(lists[:, 0:16]), T.tu[:, a:a + 256], A.mult), win + " ls%d " % t + r, w)
+            return
+        act(T.far[:, n:256], T[win][:, 0:64].indirect(lists[:, LOOK:16]), win + " ls%d" % t, "far")
+        V(tt(T.tu[:, a + 256:a + 256 + n], T[win][:, 0:64].indirect(lists[:, 0:LOOK]), T.tu[:, a:a + n], A.mult), win + " ls%d " % t + r, w + "a")
+        V(scan(T.tu[:, a + 256 + n:a + 512], T.tu[:, a + n:a + 256], T.far[:, n:256], 0.0, keep, A.mult), "far " + r, w)
 
     def scale_z(parts):
         for q, b, h in parts:
@@ -279,80 +307,81 @@ def rank_program(g, core, T, topo):
             V(cp(T.yb[:, 128:256], T.k1[:, 0:128]), "k1", "yb1")
         else:
             act(T.yb[:, 0:128], T.k0[:, 0:128], "k0", "yb0")
-        dma("S", T.y[:, 128 * h:128 * h + 128], T.yb[:, 128 * h:128 * h + 128], "st", "yb%d" % h)
+        dma("AS"[h], T.y[:, 128 * h:128 * h + 128], T.yb[:, 128 * h:128 * h + 128], ("st2", "st")[h], "yb%d" % h)
 
     def send(out, in_, sem, tok):
         order("G", [writer[tok]])
         g.remote_dma(out, in_, T.sem[sem], T.sem.loc, pid, rid, mask)
 
     for t in range(R):
-        moq = T["ls%d" % t][:, 16:32]
-        lst = " ls%d" % t
-
         def at(place):
             if t == 0:
                 once[place]()
         mm("k0", "u16", 0, "x", 0, 128, "qu16 su16 qx0")
-        for b in range(1 if t else 0):
-            unpack(b, 0, "b%d" % b)
+        parts = [(b, 0, "b%d" % b) for b in range(4)] + [(b, 1, ("k3", "b0", "b1", "b2")[b]) for b in range(4)]
+        n0, n1, n2 = UNPACK[min(t, 1)]
+        for part in parts[:n0]:
+            unpack(*part)
         mm("k1", "u16", 0, "x", 128, 256, "qu16 su16 qx1")
-        for b in range(1 if t else 0, 4):
-            unpack(b, 0, "b%d" % b)
+        for part in parts[n0:n1]:
+            unpack(*part)
         for h in (0, 1):
-            V(tt(T.tu[:, 128 * h:128 * h + 128], T["k%d" % h][:, 0:128], T["thr%d" % t][:, 128 * h:128 * h + 128], A.is_le),
+            V(tt(T.tu[:, 256 + 128 * h:384 + 128 * h], T["k%d" % h][:, 0:128], T["thr%d" % t][:, 128 * h:128 * h + 128], A.is_le),
               "k%d thr%d" % (h, t), "u1%d" % h)
         V(fill(T.sl[:, 0:96], 256.0), "", "sl")
         quant("1", T.tu[:, 0:512], 0, 128, "u10 u11 tz", "q1")
         mm("k2", "c", 0, "1", 0, 128, "qc0 q1")
         at("count")
-        for b in range(3):
-            unpack(b, 1, ("k3", "b0", "b1")[b])
+        for part in parts[n1:n2]:
+            unpack(*part, half="T")
         mm("k0", "c", 128, "1", 0, 128, "qc1 q1")
-        unpack(3, 1, "b2")
-        at("unpacked")
-        mm("k1", "c", 256, "1", 0, 128, "qc1 q1")
         V(ts(T.nl1[:], T.k2[:, q64], 3.5, -1.0, A.is_ge, A.mult), "k2", "nl1")
-        at("licence")
-        V(tt(T.tu[:, 256:512], T.nl1[:, q64].indirect(moq), T.tu[:, 0:256], A.mult), "nl1 u10 u11" + lst, "u2")
-        V(scan(W("cum1"), T.k0[:, q64], W("md4"), col(INIT1), A.add, A.subtract), "k0 md4 init1", "cum1")
-        quant("2", T.tu[:, 256:768], 0, 128, "u2 tz2", "q2")
+        quant("f%d" % t, T.fg[:, 384:896], 0, 128, fs[0], "qf")
+        look_up(t, "nl1", 256, "u10 u11", "u2", A.max)
+        for part in parts[n1:n2]:
+            unpack(*part, half="A")
+        for part in parts[n2:]:
+            unpack(*part)
+        mm("k1", "c", 256, "1", 0, 128, "qc1 q1")
+        quant("2", T.tu[:, 256:768], 0, 128, "u2", "q2")
+        at("again")
         mm("k2", "c", 0, "2", 0, 128, "qc0 q2")
         for bank, a in (("k3", 128), ("b0", 256)):
             mm(bank, "c", a, "1", 0, 128, "q1", True, False)
             mm(bank, "c", a, "2", 0, 128, "q2", False, True)
         mm("b1", "c", 128, "2", 0, 128, "q2", True, False)
         mm("b2", "c", 256, "2", 0, 128, "q2", True, False)
-        quant("f%d" % t, T.fg[:, 384:1408], 0, 256, " ".join(fs), "qf")
+        V(scan(W("cum1"), T.k0[:, q64], W("md4"), col(INIT1), A.add, A.subtract), "k0 md4 init1", "cum1")
+        quant("f%d" % t, T.fg[:, 896:1408], 128, 256, fs[1], "qf")
         send(T["qh%d" % t][:].bitcast(dt.uint8), T["qf%d" % t][:].bitcast(dt.uint8), "ah%d" % t, "qf")
         send(T["sh%d" % t][:], T["sf%d" % t][:], "ah%d" % t, "qf")
-        at("sent")
         V(ts(T.nl2[:], T.k2[:, q64], -3.5, -1.0, A.is_gt, A.mult), "k2", "nl2")
         V(tt(W("x1"), T.k1[:, q64], W("cum1"), A.add), "k1 cum1", "x1")
-        V(tt(T.tu[:, 512:768], T.nl2[:, q64].indirect(moq), T.tu[:, 256:512], A.mult), "nl2 u2" + lst, "u3")
+        look_up(t, "nl2", 512, "u2", "u3", A.min)
         V(scan(W("cum2"), T.k3[:, q64], W("md"), T.nm[:, 64:65], A.add, A.add), "k3 md nm", "cum2")
         quant("3", T.tu[:, 512:1024], 0, 128, "u3", "q3")
         act(W("t1"), W("x1"), "x1 cum2", "t1", IDENT, scale=-1.0, bias=W("cum2", 63))
-        at("order")
         mm("k2", "c", 128, "3", 0, 128, "q3")
         mm("k0", "c", 256, "3", 0, 128, "q3")
         mm("b1", "c", 128, "3", 0, 128, "q3", False, True)
         mm("b2", "c", 256, "3", 0, 128, "q3", False, True)
         V(tt(W("pp2"), T.b0[:, q64], W("cum2"), A.add), "b0 cum2", "pp2")
+        at("waves")
         V(tt(W("m21"), W("pp2"), W("t1"), A.min), "pp2 t1", "m21")
         V(scan(W("cum3"), T.k2[:, q64], W("md"), 0.0, A.add, A.add), "k2 md", "cum3")
-        V(scan(W("wm"), W("dump"), W("m21"), -HUGE, A.max, A.min), "dump m21", "wm")
-        V(tt(W("pp3"), T.k0[:, q64], W("cum3"), A.add), "k0 cum3", "pp3")
-        V(ts(W("t2", 0, 16), W("wm", 3, 64, 4), W("cum3", 63), None, A.add), "wm cum3", "t2")
-        V(scan(W("wr"), W("dump"), W("pp3"), -HUGE, A.max, A.min), "dump pp3", "wr")
+        at("counted")
+        V(tt(T.pair[:, 0:128:2], T.k0[:, q64], W("cum3"), A.add), "k0 cum3", "pp3")
+        act(T.pair[:, 1:128:2], W("m21"), "m21 cum3", "known", IDENT, bias=W("cum3", 63))
+        at("order")
         V(ts(W("u1s"), T.k1[:, q64], -512.0, None, A.is_le), "k1", "u1s")
-        V(tt(W("mn", 0, 16), W("wr", 3, 64, 4), W("t2", 0, 16), A.min), "wr t2", "mn")
-        V(scan(W("cum1"), T.b1[:, q64], T.zero[:, q64], 0.0, A.add, A.add), "b1 zero", "cum1")
-        V(ts(T.pos[:], W("mn", 0, 16), OWN, None, A.add), "mn", "pos")
+        V(scan(T.least[:], T.dump[:], T.pair[:], -HUGE, A.max, A.min), "dump dump1 pp3 known", "least")
+        V(scan(W("cum1"), T.b1[:, q64], T.zero[:, 0:64], 0.0, A.add, A.add), "b1 zero", "cum1")
+        V(ts(T.pos[:], T.least[:, 7:128:8], OWN, None, A.add), "least", "pos")
         V(tt(W("kk"), T.b2[:, q64], W("cum1"), A.add), "b2 cum1", "kk")
         V(cp(T.sl[:, 0:512].indirect(T.pos[:, 0:16]), T.lam[:, 0:256]), "pos lam", "sl")
         V(ts(W("t6"), W("kk"), OWN - 96.0, 96.0, A.is_le, A.mult), "kk", "t6")
         V(scan(T.ws96[:], T.wr4[:, 0:96], T.sl[:, 0:96], 0.0, A.add, A.min), "wr4 sl", "ws96")
-        at("slots")
+        V(ts(W("t7"), W("kk"), OWN - 192.0, 96.0, A.is_le, A.mult), "kk", "t7")
         V(ts(T["slot%d" % t][:], T.ws96[:, 3:96:4], 4.0, col(SLOTC), A.mult, A.add), "ws96 slotc", "slot")
         send(T["land%d" % t][:], T["slot%d" % t][:], "al%d" % t, "slot")
         writer["hq"] = ("ah%d" % t, 2 * neng, {})
@@ -360,22 +389,22 @@ def rank_program(g, core, T, topo):
         for b, bank in enumerate(("b3", "k3", "b0", "k2")):
             mm(bank, "e", 128 * b, "h%d" % t, 0, 256, "hq")
             act(T.hh[:, b:1024:4], T[bank][:, 0:256], bank, "h%d" % b)
-        V(tt(W("a1"), W("u1s"), T["dm%d" % t][:], A.mult), "u1s dm%d" % t, "a1")
         V(tt(W("sm"), W("kk"), W("t6"), A.add), "kk t6", "sm")
-        V(ts(W("t7"), W("kk"), OWN - 192.0, 96.0, A.is_le, A.mult), "kk", "t7")
+        V(tt(W("a1"), W("u1s"), T["dm%d" % t][:], A.mult), "u1s dm%d" % t, "a1")
+        V(tt(W("gn"), W("sm"), W("t7"), A.add), "sm t7", "gn")
         V(tt(W("an"), W("a1"), W("jn"), A.add), "a1 jn", "an")
+        at("travel0")
         last = t == R - 1
-        at("travel")
         if last:
             V(ts(W("t1"), T.k0[:, q64], -512.0, 1.0, A.is_le, A.add), "k0", "t1")
             V(ts(W("t2"), W("kk"), 512.0, 2.0, A.is_ge, A.mult), "kk", "t2")
-        V(tt(W("gn"), W("sm"), W("t7"), A.add), "sm t7", "gn")
-        if last:
             V(tt(W("pp2"), W("t1"), W("u1s"), A.add), "t1 u1s", "pp2")
         V(tt(W("ff"), W("gn"), W("an"), A.max), "gn an", "ff")
+        at("travel1")
         if last:
             V(tt(W("pp3"), W("pp2"), W("t2"), A.add), "pp2 t2", "pp3")
         V(ts(T.off[:], W("ff"), -4.0, col(OFFC), A.mult, A.add), "ff offc", "off")
+        at("travel2")
         if last:
             V(lambda: g.vector.transpose(W("m21"), W("pp3")), "pp3", "m21")
             V(cp(T.wc16[:], W("m21", 0, 64, 4)), "m21", "wc16")
@@ -384,20 +413,22 @@ def rank_program(g, core, T, topo):
         if t == 1:
             quant("v", T.v0[:], 0, 128, "v0", "qv")
         r = "h0 h1 h2 h3 hz land"
-        V(cp(T.fg[:, 0:192], T.hh[:, 0:1040].indirect(T["land%d" % t][:, 0:12])), r, "g0")
-        act(T.fg[:, 192:384], T.hh[:, 0:1040].indirect(T["land%d" % t][:, 12:24]), r, "g1")
+        a = 12
+        V(cp(T.fg[:, 0:16 * a], T.hh[:, 0:1040].indirect(T["land%d" % t][:, 0:a])), r, "g0")
+        act(T.fg[:, 16 * a:384], T.hh[:, 0:1040].indirect(T["land%d" % t][:, a:24]), r, "g1")
         at("guests")
         r = " ".join(fs) + " g0 g1 off"
         for h in (0, 1):
             a, m, e = FILL[h]
             V(cp(T.z[:, 16 * a:16 * m], T.fg[:, 0:1408].indirect(T.off[:, a:m])), r, "zv%d" % h)
             act(T.z[:, 16 * m:16 * e], T.fg[:, 0:1408].indirect(T.off[:, m:e]), r, "za%d" % h)
-            at("fill%d" % h)
             if h:
                 scale_z(SCALE[:EARLY])
+            else:
+                V(cp(T.z[:, 512:16 * FILL[1][0]], T.fg[:, 0:1408].indirect(T.off[:, 32:FILL[1][0]])), r, "zw")
             quant("z", T.z[:, 512 * h:512 * h + 512], 128 * h, 128 * h + 128, "zv%d za%d" % (h, h), "qz%d" % h)
-            for b in range(4):
-                mm("bk"[h] + "%d" % b, "w", 128 * b, "z", 128 * h, 128 * h + 128, "qw sw qz%d" % h)
+            for b, k in (SUMS[FIRST:] if h else SUMS[:FIRST]):
+                mm("bk"[k] + "%d" % b, "w", 128 * b, "z", 128 * k, 128 * k + 128, "qw sw qz%d" % k)
         scale_z(SCALE[EARLY:])
         for b, h in SUMS:
             bank, a = "bk"[h] + "%d" % b, 512 * h + 128 * b
@@ -411,15 +442,15 @@ def rank_program(g, core, T, topo):
                     dma("S", T.oc[:, 512 * b:512 * b + 512], T.qx[:, 128 * b:128 * b + 128].bitcast(dt.uint8), "st", "qx%d" % b)
                     mm("k%d" % b, "v", 0, "x", 128 * b, 128 * b + 128, "qv qx%d" % b)
                 continue
-            src = T["tt%d" % b][:, 0:256].indirect(T["ls%d" % t][:, a:e])
-            out, r, w = T.xt[:, 64 * a + b:64 * e:4], "tt%d0 tt%d1" % (b, b) + lst, "xs%d%d" % (b, a)
+            src = T["tt%d" % b][:, 0:256].indirect(T["inv%d" % t][:, a:e])
+            out, r, w = T.xt[:, 64 * a + b:64 * e:4], "tt%d0 tt%d1 inv%d" % (b, b, t), "xs%d%d" % (b, a)
             if q == "V":
                 V(ts(out, src, 0.03125, None, A.mult), r, w)
             else:
                 act(out, src, r, w, scale=0.03125)
     for k in range(4):
-        dma("A", T.osc[4 * k:4 * k + 4, :], T.sx[32 * k:32 * k + 4, :], "st2", "qx0 qx1")
+        dma("AS"[k // 2], T.osc[4 * k:4 * k + 4, :], T.sx[32 * k:32 * k + 4, :], ("st2", "st")[k // 2], "qx0 qx1")
     store_y(1)
     g.wait_ge(T.sem.loc, 3 * R * neng)
-    for s in sorted(count):
+    for s in sorted(count, key=lambda n: n == "st"):
         g.wait_ge(T.sem[s], count[s])

@@ -10,6 +10,7 @@ SHARES = (("A", 0, 0, 16), ("A", 1, 0, 16), ("A", 2, 8, 16),
 SCALE = (("V", 2, 0), ("V", 1, 0), ("A", 0, 0), ("A", 0, 1), ("A", 2, 1), ("A", 1, 1), ("A", 3, 1), ("A", 3, 0))
 EARLY = 2
 LOOK = 16
+GUESTS = (8, 12)
 FIRST = 3
 UNPACK = ((0, 4, 7), (0, 4, 8))
 SUMS = ((2, 0), (1, 0), (0, 0), (0, 1), (2, 1), (1, 1), (3, 1), (3, 0))
@@ -32,7 +33,8 @@ def _scratch():
     sb("bfloat16", 1040, "hh")
     sb("bfloat16", 1024, "x0 z z32 xt tu")
     sb("bfloat16", 528, "eb zero")
-    sb("bfloat16", 512, "u0 v0 sl")
+    sb("bfloat16", 768, "sl")
+    sb("bfloat16", 512, "u0 v0")
     sb("bfloat16", 256, "far row lam i4 i16 pat wr4 wr16 iv mrow thr0 thr1 thr2 tt0 tt1 tt2 tt3")
     sb("bfloat16", 64, "d64 e0 wb0 wb1 wb quarter nl1 nl2")
     sb("uint16", 16, "ls0 ls1 ls2 inv0 inv1 inv2")
@@ -44,11 +46,11 @@ def _scratch():
     sb("int32", 16, "mi mq")
     sb("float32", 8, "i8 gsel")
     sb("float32", 16, "pc wc16")
-    sb("float32", 72, "nm")
+    sb("float32", 72, "nm behind")
     sb("float32", 64, "n16 n4x dm0 dm1 dm2")
     sb("float32", 64 * len(SMALL), "small")
     sb("float16", 96, "ws96")
-    sb("float32", 128, "dump pair least")
+    sb("float16", 128, "dump pair least")
     sb("float32", 256, "raw yb")
     for n in "k0 k1 k2 k3 b0 b1 b2 b3".split():
         s[n] = ("psum", [128, 512], "float32")
@@ -179,7 +181,7 @@ def rank_program(g, core, T, topo):
     V(ts(T.pi[:, 2:3], T.pi[:, 4:5], 3, None, A.bitwise_and), "pi4", "pi2")
     V(ts(T.pi[:, 3:4], T.pi[:, 4:5], 4, None, A.logical_shift_right), "pi4", "pi3")
     V(ts(T.e0[:], T.d64[:], 0.0, 0.25, A.is_equal, A.mult), "d64", "e0")
-    dma("S", T.x0[:, 0:512], T.x[:, 0:512], "ld_xa", "pi3", "x0a")
+    dma("S", T.x0[:, 0:512], T.x[:, 0:512], "ld_xa", "zero", "x0a")
     dma("S", T.x0[:, 512:1024], T.x[:, 512:1024], "ld_xb", "", "x0b")
     dma("S", T.qw[:].bitcast(dt.uint8), T.wc[:], "ld_wc", "x0a x0b", "qw")
     dma("S", T.sw[:], T.ws[:], "ld_ws", "", "sw")
@@ -211,19 +213,16 @@ def rank_program(g, core, T, topo):
     V(fill(T.tu[:, 0:256], 0.0), "", "tz")
     V(fill(T.nm[:, 0:1], 0.0), "", "nm0")
     V(ts(T.nm[:, 1:65], T.i4[:, 0:64], col(ELEM), -HUGE, A.not_equal, A.mult), "i40 i41 i42 i43 pc", "nm")
-    V(ts(T.wr4[:], T.pat[:], 1024.0, -256.0, A.add, A.max), "pat", "wr4")
-    V(tt(W("md"), T.nm[:, 0:64], T.nm[:, 1:65], A.subtract), "nm0 nm", "md")
+    quant("c", T.ct[:, 0:512], 0, 128, " ".join("c0%d" % k for k in range(8)), "qc0")
     V(cp(T.mo[:], T.mi[:]), "mi", "mo")
     V(ts(T.mq[:], T.mi[:], 2, None, A.logical_shift_right), "mi", "mq")
     act(T.thr0[:], T.pat[:, 0:256].indirect(T.mo[:, 0:16]), "pat mo", "thr0")
-    quant("c", T.ct[:, 0:512], 0, 128, " ".join("c0%d" % k for k in range(8)), "qc0")
-    V(cp(T.ls0[:], T.mq[:]), "mq", "ls0")
     quant_e(0)
-    quant_e(1)
+    V(cp(T.ls0[:], T.mq[:]), "mq", "ls0")
     turn("thr", "ld_thr", "thr0")
     turn("ls", "ld_ls", "ls0")
     quant("u", T.u0[:], 0, 128, "u0", "qu")
-    quant_e(2)
+    quant_e(1)
     V(cp(T.qu16[:, 0:128].bitcast(dt.uint32), T.qu[:, 0:128].bitcast(dt.uint32).indirect(T.pick8[:, 0:8])), "qu pick8", "qu16")
     quant_x(0, T.x0, "x0a")
     quant_x(1, T.x0, "x0b")
@@ -231,21 +230,24 @@ def rank_program(g, core, T, topo):
     act(col(CA), col(SUB), "pc", "ca", scale=-1.0, bias=1027.0)
     act(T.mrow[:], T.row[:, 0:256].indirect(T.mo[:, 0:16]), "row mo", "mrow")
     act(W("jn"), T.n4x[:], "n4x ca", "jn", IDENT, bias=col(CA))
+    quant_e(2)
     quant_e(3)
-    quant("c", T.ct[:, 512:1536], 128, 384, " ".join("c%d%d" % (j, k) for j in (1, 2) for k in range(8)), "qc1")
-
-    act(W("md4"), W("md"), "md", "md4", bias=4.0)
     act(col(INIT1), T.nm[:, 64:65], "nm ca", "init1", IDENT, scale=-1.0, bias=col(CA))
+
+    def sums():
+        quant("c", T.ct[:, 512:1536], 128, 384, " ".join("c%d%d" % (j, k) for j in (1, 2) for k in range(8)), "qc1")
+        V(ts(T.wr4[:], T.pat[:], 1024.0, -256.0, A.add, A.max), "pat", "wr4")
+
+    def steps():
+        V(tt(W("md"), T.nm[:, 0:64], T.nm[:, 1:65], A.subtract), "nm0 nm", "md")
+        act(W("md4"), W("md"), "md", "md4", bias=4.0)
 
     def masks():
         act(col(DUMP), col(RES), "pc", "cdump", bias=256.0 - OWN)
         act(col(CM), col(SUB), "pc", "cm", scale=256.0, bias=159.0)
         act(W("t2"), T.nm[:, 1:65], "nm cdump", "t2", IDENT, scale=2.0, bias=col(DUMP))
-        act(T.dump[:, 1:128:2], T.zero[:, 0:64], "zero", "dump1", bias=-HUGE)
-        V(tt(W("a1"), T.raw[:, 3:256:4], W("jn"), A.add), "raw0 raw1 jn", "a1")
-
-    def invert(h):
-        V(cp(T.iv[:, 0:256].indirect(T.mo[:, 8 * h:8 * h + 8]), T.row[:, 128 * h:128 * h + 128]), "row mo", "iv")
+        act(T.behind[:, 64:65], T.nm[:, 64:65], "nm", "end")
+        V(scan(T.raw[:], T.wr4[:], T.mrow[:], 0.0, A.add, A.min), "wr4 mrow", "raw0 raw1")
 
     def late_constants():
         act(col(S0), col(ELEM), "pc", "s0", bias=3072.0)
@@ -264,14 +266,16 @@ def rank_program(g, core, T, topo):
         dma("S", T.v0[:], T.v[:], "ld_v", "", "v0")
 
     once = {
-        "count": lambda: V(scan(T.raw[:], T.wr4[:], T.mrow[:], 0.0, A.add, A.min), "wr4 mrow", "raw0 raw1"),
+        "scored": lambda: V(ts(T.dump[:, 1:128:2], T.zero[:, 0:64], -HUGE, None, A.add), "zero", "dump1"),
+        "count": sums,
+        "looked": steps,
         "again": masks,
-        "waves": lambda: V(ts(T.dm0[:], W("a1"), -1.0, col(CM), A.mult, A.add), "a1 cm", "dm0"),
+        "waves": lambda: V(tt(W("a1"), T.raw[:, 3:256:4], W("jn"), A.add), "raw0 raw1 jn", "a1"),
+        "paired": lambda: V(ts(T.dm0[:], W("a1"), -1.0, col(CM), A.mult, A.add), "a1 cm", "dm0"),
         "counted": lambda: V(tt(T.dump[:, 0:128:2], W("t2"), T.n16[:], A.add), "t2 n16", "dump"),
         "order": late_constants,
-        "travel0": lambda: invert(0),
-        "travel1": lambda: invert(1),
-        "travel2": lambda: V(scan(T.raw[:], T.wr16[:], T.iv[:], 0.0, A.add, A.min), "wr16 iv", "raw0 raw1"),
+        "sent": lambda: V(cp(T.iv[:, 0:256].indirect(T.mo[:, 0:16]), T.row[:, 0:256]), "row mo", "iv"),
+        "travel": lambda: V(scan(T.raw[:], T.wr16[:], T.iv[:], 0.0, A.add, A.min), "wr16 iv", "raw0 raw1"),
         "guests": inverse,
     }
 
@@ -329,6 +333,7 @@ def rank_program(g, core, T, topo):
             V(tt(T.tu[:, 256 + 128 * h:384 + 128 * h], T["k%d" % h][:, 0:128], T["thr%d" % t][:, 128 * h:128 * h + 128], A.is_le),
               "k%d thr%d" % (h, t), "u1%d" % h)
         V(fill(T.sl[:, 0:96], 256.0), "", "sl")
+        at("scored")
         quant("1", T.tu[:, 0:512], 0, 128, "u10 u11 tz", "q1")
         mm("k2", "c", 0, "1", 0, 128, "qc0 q1")
         at("count")
@@ -343,6 +348,9 @@ def rank_program(g, core, T, topo):
         for part in parts[n2:]:
             unpack(*part)
         mm("k1", "c", 256, "1", 0, 128, "qc1 q1")
+        at("looked")
+        if t == R - 1:
+            quant("v", T.v0[:], 0, 128, "v0", "qv")
         quant("2", T.tu[:, 256:768], 0, 128, "u2", "q2")
         at("again")
         mm("k2", "c", 0, "2", 0, 128, "qc0 q2")
@@ -357,8 +365,9 @@ def rank_program(g, core, T, topo):
         send(T["sh%d" % t][:], T["sf%d" % t][:], "ah%d" % t, "qf")
         V(ts(T.nl2[:], T.k2[:, q64], -3.5, -1.0, A.is_gt, A.mult), "k2", "nl2")
         V(tt(W("x1"), T.k1[:, q64], W("cum1"), A.add), "k1 cum1", "x1")
+        V(ts(W("u1s"), T.k1[:, q64], -512.0, None, A.is_le), "k1", "u1s")
         look_up(t, "nl2", 512, "u2", "u3", A.min)
-        V(scan(W("cum2"), T.k3[:, q64], W("md"), T.nm[:, 64:65], A.add, A.add), "k3 md nm", "cum2")
+        V(scan(W("cum2"), T.k3[:, q64], W("md"), 0.0, A.add, A.add), "k3 md", "cum2")
         quant("3", T.tu[:, 512:1024], 0, 128, "u3", "q3")
         act(W("t1"), W("x1"), "x1 cum2", "t1", IDENT, scale=-1.0, bias=W("cum2", 63))
         mm("k2", "c", 128, "3", 0, 128, "q3")
@@ -366,57 +375,71 @@ def rank_program(g, core, T, topo):
         mm("b1", "c", 128, "3", 0, 128, "q3", False, True)
         mm("b2", "c", 256, "3", 0, 128, "q3", False, True)
         V(tt(W("pp2"), T.b0[:, q64], W("cum2"), A.add), "b0 cum2", "pp2")
+        def own_or_partner(k):
+            if k:
+                V(tt(W("an"), W("a1"), W("jn"), A.add), "a1 jn", "an")
+            else:
+                V(tt(W("a1"), W("u1s"), T["dm%d" % t][:], A.mult), "u1s dm%d" % t, "a1")
+        last = t == R - 1
+        if t:
+            own_or_partner(0)
         at("waves")
-        V(tt(W("m21"), W("pp2"), W("t1"), A.min), "pp2 t1", "m21")
-        V(scan(W("cum3"), T.k2[:, q64], W("md"), 0.0, A.add, A.add), "k2 md", "cum3")
+        V(tt(T.pair[:, 1:128:2], W("pp2"), W("t1"), A.min), "pp2 t1", "known")
+        V(scan(T.behind[:, 63::-1], T.k2[:, 127:63:-1], T.small[:, 63::-1], T.nm[:, 64:65], A.add, A.add), "k2 md nm", "behind")
+        if t:
+            own_or_partner(1)
+        at("paired")
         at("counted")
-        V(tt(T.pair[:, 0:128:2], T.k0[:, q64], W("cum3"), A.add), "k0 cum3", "pp3")
-        act(T.pair[:, 1:128:2], W("m21"), "m21 cum3", "known", IDENT, bias=W("cum3", 63))
+        V(tt(T.pair[:, 0:128:2], T.k0[:, q64], T.behind[:, 1:65], A.subtract), "k0 behind end", "pp3")
         at("order")
-        V(ts(W("u1s"), T.k1[:, q64], -512.0, None, A.is_le), "k1", "u1s")
-        V(scan(T.least[:], T.dump[:], T.pair[:], -HUGE, A.max, A.min), "dump dump1 pp3 known", "least")
         V(scan(W("cum1"), T.b1[:, q64], T.zero[:, 0:64], 0.0, A.add, A.add), "b1 zero", "cum1")
-        V(ts(T.pos[:], T.least[:, 7:128:8], OWN, None, A.add), "least", "pos")
+        if t == 0:
+            own_or_partner(0)
+        V(scan(T.least[:], T.dump[:], T.pair[:], -HUGE, A.max, A.min), "dump dump1 pp3 known", "least")
         V(tt(W("kk"), T.b2[:, q64], W("cum1"), A.add), "b2 cum1", "kk")
-        V(cp(T.sl[:, 0:512].indirect(T.pos[:, 0:16]), T.lam[:, 0:256]), "pos lam", "sl")
+        if t == 0:
+            own_or_partner(1)
+        if last:
+            V(ts(W("t1"), T.k0[:, q64], -512.0, 1.0, A.is_le, A.add), "k0", "t1")
+        V(ts(T.pos[:], T.least[:, 7:128:8], T.behind[:, 0:1], OWN, A.add, A.add), "least behind", "pos")
         V(ts(W("t6"), W("kk"), OWN - 96.0, 96.0, A.is_le, A.mult), "kk", "t6")
-        V(scan(T.ws96[:], T.wr4[:, 0:96], T.sl[:, 0:96], 0.0, A.add, A.min), "wr4 sl", "ws96")
         V(ts(W("t7"), W("kk"), OWN - 192.0, 96.0, A.is_le, A.mult), "kk", "t7")
+        V(cp(T.sl[:, 0:768].indirect(T.pos[:, 0:16]), T.lam[:, 0:256]), "pos lam", "sl")
+        V(tt(W("sm"), W("kk"), W("t6"), A.add), "kk t6", "sm")
+        V(scan(T.ws96[:], T.wr4[:, 0:96], T.sl[:, 0:96], 0.0, A.add, A.min), "wr4 sl", "ws96")
+        if t == 0:
+            V(tt(W("gn"), W("sm"), W("t7"), A.add), "sm t7", "gn")
+        if last:
+            V(tt(W("pp2"), W("t1"), W("u1s"), A.add), "t1 u1s", "pp2")
         V(ts(T["slot%d" % t][:], T.ws96[:, 3:96:4], 4.0, col(SLOTC), A.mult, A.add), "ws96 slotc", "slot")
         send(T["land%d" % t][:], T["slot%d" % t][:], "al%d" % t, "slot")
+        if t:
+            V(tt(W("gn"), W("sm"), W("t7"), A.add), "sm t7", "gn")
         writer["hq"] = ("ah%d" % t, 2 * neng, {})
         writer["land"] = ("al%d" % t, neng, {})
         for b, bank in enumerate(("b3", "k3", "b0", "k2")):
             mm(bank, "e", 128 * b, "h%d" % t, 0, 256, "hq")
             act(T.hh[:, b:1024:4], T[bank][:, 0:256], bank, "h%d" % b)
-        V(tt(W("sm"), W("kk"), W("t6"), A.add), "kk t6", "sm")
-        V(tt(W("a1"), W("u1s"), T["dm%d" % t][:], A.mult), "u1s dm%d" % t, "a1")
-        V(tt(W("gn"), W("sm"), W("t7"), A.add), "sm t7", "gn")
-        V(tt(W("an"), W("a1"), W("jn"), A.add), "a1 jn", "an")
-        at("travel0")
-        last = t == R - 1
+        at("sent")
         if last:
-            V(ts(W("t1"), T.k0[:, q64], -512.0, 1.0, A.is_le, A.add), "k0", "t1")
             V(ts(W("t2"), W("kk"), 512.0, 2.0, A.is_ge, A.mult), "kk", "t2")
-            V(tt(W("pp2"), W("t1"), W("u1s"), A.add), "t1 u1s", "pp2")
         V(tt(W("ff"), W("gn"), W("an"), A.max), "gn an", "ff")
-        at("travel1")
+        at("travel")
         if last:
             V(tt(W("pp3"), W("pp2"), W("t2"), A.add), "pp2 t2", "pp3")
         V(ts(T.off[:], W("ff"), -4.0, col(OFFC), A.mult, A.add), "ff offc", "off")
-        at("travel2")
         if last:
             V(lambda: g.vector.transpose(W("m21"), W("pp3")), "pp3", "m21")
+        r = "h0 h1 h2 h3 hz land"
+        a = GUESTS[min(t, 1)]
+        if a:
+            V(cp(T.fg[:, 0:16 * a], T.hh[:, 0:1040].indirect(T["land%d" % t][:, 0:a])), r, "g0")
+        act(T.fg[:, 16 * a:384], T.hh[:, 0:1040].indirect(T["land%d" % t][:, a:24]), r, "g1" if a else "g0 g1")
+        at("guests")
+        if last:
             V(cp(T.wc16[:], W("m21", 0, 64, 4)), "m21", "wc16")
             for k in range(4):
                 dma("S", T.wv[k % 2:8:2, 128 * (k // 2):128 * (k // 2) + 128], T.wc16[:, 4 * k:4 * k + 4], "st", "wc16")
-        if t == 1:
-            quant("v", T.v0[:], 0, 128, "v0", "qv")
-        r = "h0 h1 h2 h3 hz land"
-        a = 12
-        V(cp(T.fg[:, 0:16 * a], T.hh[:, 0:1040].indirect(T["land%d" % t][:, 0:a])), r, "g0")
-        act(T.fg[:, 16 * a:384], T.hh[:, 0:1040].indirect(T["land%d" % t][:, a:24]), r, "g1")
-        at("guests")
         r = " ".join(fs) + " g0 g1 off"
         for h in (0, 1):
             a, m, e = FILL[h]

@@ -1,20 +1,21 @@
 from concourse.mybir import dt, AluOpType, ActivationFunctionType
 
 R = 3
-HUGE = 4096.0
-OWN = 1023.0
-NEVER = -1e29
-SMALL = "md md4 jn cum1 cum2 cum3 x1 pp2 pp3 t1 t2 m21 kk u1s a1 an t6 t7 sm gn ff".split()
+GUEST = 544.0
+M = 1024.0
+MASK = 1536.0
+TINY = "l1 l2 l3 uc leg d2 dn e1 ee uu c2 dm far w1 w2".split()
 SHARES = (("A", 0, 0, 16), ("A", 1, 0, 16), ("A", 2, 8, 16),
           ("V", 2, 0, 8), ("V", 3, 0, 8), ("V", 3, 8, 16), ("Q", 0, 0, 8), ("Q", 1, 8, 16))
 SCALE = (("V", 2, 0), ("V", 1, 0), ("A", 0, 0), ("A", 0, 1), ("A", 2, 1), ("A", 1, 1), ("A", 3, 1), ("A", 3, 0))
 EARLY = 2
-LOOK = 16
-GUESTS = (8, 12)
+LOOK = (8, 8)
+GUESTS = (0, 12)
 FIRST = 3
-UNPACK = ((0, 4, 7), (0, 4, 8))
 SUMS = ((2, 0), (1, 0), (0, 0), (0, 1), (2, 1), (1, 1), (3, 1), (3, 0))
-FILL = ((0, 18, 32), (38, 42, 64))
+FILL = ((0, 16, 32), (38, 44, 64))
+ONCE = {"scored": "dm", "listing": "c2", "count": "s0 frames row", "behind": "high s1", "lifted": "behind", "paired": "s2 l2 anew",
+        "placed": "l3 s3 marks", "third": "list2", "least": "quarters", "pos": "mo even", "chosen": "iv0", "sent": "iv1", "travel": "iv2", "listed": "iv3", "half": "inv", "sums": "turn"}
 
 
 def _scratch():
@@ -24,42 +25,45 @@ def _scratch():
         for n in names.split():
             s[n] = ("sbuf", [128, w], d)
 
-    for w, names in ((128, "u u16 v 1 2 3"), (256, "x z f0 f1 f2 h0 h1 h2"), (384, "c"), (512, "w e")):
+    for w, names in ((128, "u u16 v 2"), (256, "x z 1 c f0 f1 f2 h0 h1 h2"), (512, "w e")):
         for n in names.split():
             s["q" + n] = ("sbuf", [128, w], "float8_e4m3fn_x4")
             s["s" + n] = ("sbuf", [128, w], "uint8")
-    sb("bfloat16", 1536, "ct")
     sb("bfloat16", 1408, "fg")
     sb("bfloat16", 1040, "hh")
-    sb("bfloat16", 1024, "x0 z z32 xt tu")
-    sb("bfloat16", 528, "eb zero")
+    sb("bfloat16", 1024, "x0 z z32 xt fl")
+    sb("bfloat16", 528, "eb ones")
     sb("bfloat16", 768, "sl")
-    sb("bfloat16", 512, "u0 v0")
-    sb("bfloat16", 256, "far row lam i4 i16 pat wr4 wr16 iv mrow thr0 thr1 thr2 tt0 tt1 tt2 tt3")
-    sb("bfloat16", 64, "d64 e0 wb0 wb1 wb quarter nl1 nl2")
-    sb("uint16", 16, "ls0 ls1 ls2 inv0 inv1 inv2")
-    sb("uint16", 16, "mo pos")
+    sb("bfloat16", 512, "u0 v0 f2 win pa fa fb tab0 tab1 tab2")
+    sb("bfloat16", 256, "row hold16 less16 own4 wr16 u4 f3 known unit su1s sy sn sk s4 tt0 tt1 tt2 tt3")
+    sb("bfloat16", 272, "y2")
+    sb("bfloat16", 192, "anew")
+    sb("bfloat16", 80, "i16 own16")
+    sb("bfloat16", 64, "edge i4")
+    sb("float16", 512, "pb least from4")
+    sb("float16", 256, "step raw")
+    sb("float16", 192, "three sums")
+    sb("float16", 96, "ws96")
+    sb("uint16", 16, "inv0 inv1 inv2 mo pos list1 list2")
     sb("uint16", 64, "off")
     sb("uint16", 24, "slot0 slot1 slot2 land0 land1 land2")
     sb("uint16", 8, "pick8")
     sb("int32", 8, "pick8i pi")
-    sb("int32", 16, "mi mq")
-    sb("float32", 8, "i8 gsel")
-    sb("float32", 16, "pc wc16")
-    sb("float32", 72, "nm behind")
-    sb("float32", 64, "n16 n4x dm0 dm1 dm2")
-    sb("float32", 64 * len(SMALL), "small")
-    sb("float16", 96, "ws96")
-    sb("float16", 128, "dump pair least")
-    sb("float32", 256, "raw yb")
+    sb("int32", 16, "mi")
+    sb("float32", 24, "pc")
+    sb("float32", 16, "n16 m20 m21 m22")
+    sb("float32", 32, "wave turned")
+    sb("float32", 16 * len(TINY), "tiny")
+    sb("float32", 256, "yb")
     for n in "k0 k1 k2 k3 b0 b1 b2 b3".split():
         s[n] = ("psum", [128, 512], "float32")
     return s
 
 
 SCRATCH = _scratch()
-LOADS = ["u", "xa", "xb", "v", "wc", "ws", "m", "thr", "ls", "inv", "dm"]
-SEMAPHORES = ["sV", "sT", "sA", "sG", "loc", "st", "st2"] + ["ld_" + n for n in LOADS] + ["ah0", "ah1", "ah2", "al0", "al1", "al2"]
+LOADS = ["u", "xa", "xb", "v", "wc", "ws", "m", "m2", "inv", "tab"]
+SEMAPHORES = (["sV", "sT", "sA", "sG", "loc", "st", "st2"] + ["ld_" + n for n in LOADS]
+              + ["ag0", "ag1", "ag2", "ah0", "ah1", "ah2", "al0", "al1", "al2"])
 
 
 def rank_program(g, core, T, topo):
@@ -68,6 +72,7 @@ def rank_program(g, core, T, topo):
         return
     A = AluOpType
     COPY, IDENT = ActivationFunctionType.Copy, ActivationFunctionType.Identity
+    SIGN, RELU, ABS = ActivationFunctionType.Sign, ActivationFunctionType.Relu, ActivationFunctionType.Abs
     nxt = T.cores[(rank + 1) % len(T.cores)]
     rid, pid = topo.addr(nxt)[0], topo.addr(nxt)[1]
     mask, neng = topo.mask(core, nxt), len(topo.engines(core, nxt))
@@ -90,10 +95,10 @@ def rank_program(g, core, T, topo):
                 known[q][k] = max(known[q].get(k, 0), c[k])
             known[q][s] = max(known[q].get(s, 0), v)
 
-    def op(q, fn, r=(), w=(), sem=None, inc=1, chain=False):
+    def op(q, fn, r=(), w=(), sem=None, inc=1):
         need = [writer[k] for k in r]
         for k in w:
-            if k in writer and not chain:
+            if k in writer:
                 need.append(writer[k])
             need += [e for qq, e in readers.get(k, {}).items() if qq != q]
         order(q, need)
@@ -133,12 +138,15 @@ def rank_program(g, core, T, topo):
     def scan(out, a, b, init, o0, o1):
         return lambda: g.vector.tensor_tensor_scan(out, a, b, init, o0, o1)
 
+    def keep(out, src):
+        return scan(out, T.pa[:, 0:512:2], src, 0.0, A.add, A.min)
+
     def quant(n, src, a, b, r, tok):
         V(lambda: g.vector.quantize_mx(T["q" + n][:, a:b], T["s" + n][:, a:b], src), r, tok)
 
-    def mm(bank, ln, la, rn, ra, rb, r, start=True, stop=True):
+    def mm(bank, ln, la, rn, ra, rb, r):
         op("T", lambda: g.tensor.matmul_mx(T[bank][:, 0:rb - ra], T["q" + ln][:, la:la + 128], T["s" + ln][:, la:la + 128],
-                                           T["q" + rn][:, ra:rb], T["s" + rn][:, ra:rb], start, stop), r.split(), [bank], chain=not start)
+                                           T["q" + rn][:, ra:rb], T["s" + rn][:, ra:rb], True, True), r.split(), [bank])
 
     def dma(q, out, in_, sem, r="", w=""):
         op(q, lambda: queues[q].dma_start(out, in_), r.split(), w.split(), sem, 16)
@@ -154,52 +162,19 @@ def rank_program(g, core, T, topo):
             dma("S", T[name + "%d" % t][128 - n:128, :], T[name + "0"][0:n, :], sem, r, name + "%d" % t)
         writer[name + "1"] = writer[name + "2"]
 
-    def W(name, a=0, b=64, step=1):
-        k = 64 * SMALL.index(name)
-        return T.small[:, k + a:k + b:step]
+    def Y(name):
+        k = 16 * TINY.index(name)
+        return T.tiny[:, k:k + 16]
 
     def col(k):
         return T.pc[:, k:k + 1]
-    RES, SUB, ELEM, GROUP, CA, INIT1, DUMP, OFFC, S0, SLOTC, CM, CI = range(12)
+    RES, SUB, ELEM, OFFC, S0, SLOTC, CI, CL, CD, CU, CN, N23, CF, CW, C0, C96, C192, C1, CG, N2, N3 = range(21)
 
-    dma("S", T.mi[:], T.m[:], "ld_m", "", "mi")
-    dma("A", T.u0[:], T.u[:], "ld_u", "", "u0")
+    def zeros(n):
+        return T.fl[:, 2:4 * n:4]
 
-    op("G", lambda: g.iota(T.pi[:, 4:5], [[0, 1]], 0, 1), [], ["pi4"])
-    iota("d64", [[-1, 4], [0, 4], [1, 4]], 0, 0)
-    iota("i8", [[1, 8]], 0, 0)
-    iota("pick8i", [[16, 8]], 0, 0)
-    V(fill(T.zero[:], 0.0), "", "zero")
-    op("G", lambda: g.affine_select(T.eb[:], T.zero[:], [[-1, 528]], A.not_equal, 1.0, 3, 4), ["zero"], ["eb"])
-    iota("row", [[1, 256]], 0, 0)
-    iota("n16", [[16, 16], [0, 4]], 0, 0)
-    iota("n4x", [[-4, 64]], -100, 0)
-    iota("lam", [[16, 16], [1, 4], [4, 4]], 0, 0)
-    iota("i16", [[0, 16], [1, 16]], 0, 0)
-    V(ts(T.pi[:, 0:1], T.pi[:, 4:5], 15, None, A.bitwise_and), "pi4", "pi0")
-    V(ts(T.pi[:, 1:2], T.pi[:, 4:5], 2, 3, A.logical_shift_right, A.bitwise_and), "pi4", "pi1")
-    V(ts(T.pi[:, 2:3], T.pi[:, 4:5], 3, None, A.bitwise_and), "pi4", "pi2")
-    V(ts(T.pi[:, 3:4], T.pi[:, 4:5], 4, None, A.logical_shift_right), "pi4", "pi3")
-    V(ts(T.e0[:], T.d64[:], 0.0, 0.25, A.is_equal, A.mult), "d64", "e0")
-    dma("S", T.x0[:, 0:512], T.x[:, 0:512], "ld_xa", "zero", "x0a")
-    dma("S", T.x0[:, 512:1024], T.x[:, 512:1024], "ld_xb", "", "x0b")
-    dma("S", T.qw[:].bitcast(dt.uint8), T.wc[:], "ld_wc", "x0a x0b", "qw")
-    dma("S", T.sw[:], T.ws[:], "ld_ws", "", "sw")
-    V(cp(T.pc[:, 0:4], T.pi[:, 0:4]), "pi0 pi1 pi2 pi3", "pc")
-    V(fill(T.quarter[:], 0.25), "", "quarter")
-    V(ts(T.wb0[:], T.d64[:], 0.0, -0.25, A.is_gt, A.mult), "d64", "wb0")
-    V(ts(T.gsel[:], T.i8[:], col(GROUP), None, A.is_equal), "i8 pc", "gsel")
-    V(ts(T.wb1[:], T.d64[:], 0.0, -256.0, A.is_equal, A.mult), "d64", "wb1")
-    for k in range(4):
-        V(fill(T.i4[:, k:256:4], float(k)), "", "i4%d" % k)
-    V(tt(T.wb[:], T.wb0[:], T.wb1[:], A.add), "wb0 wb1", "wb")
-    V(ts(T.pat[:], T.i4[:], col(SUB), NEVER, A.not_equal, A.mult), "i40 i41 i42 i43 pc", "pat")
-    V(cp(T.pick8[:], T.pick8i[:]), "pick8i", "pick8")
-
-    def tile_of_constants(j, src):
-        for k in range(8):
-            kw = {"scale": T.gsel[:, k:k + 1]} if j else {}
-            act(T.ct[:, 512 * j + 64 * k:512 * j + 64 * k + 64], T[src][:], src + (" gsel" if j else ""), "c%d%d" % (j, k), **kw)
+    def column(out, src, w, scale, bias, r="pc"):
+        act(col(out), col(src), r, w, scale=scale, bias=bias)
 
     def quant_e(b):
         quant("e", T.eb[:, 3 - b:515 - b], 128 * b, 128 * b + 128, "eb", "qe%d" % b)
@@ -207,95 +182,120 @@ def rank_program(g, core, T, topo):
     def quant_x(h, src, r):
         quant("x", src[:, 512 * h:512 * h + 512], 128 * h, 128 * h + 128, r, "qx%d" % h)
 
-    tile_of_constants(0, "e0")
-    tile_of_constants(1, "quarter")
-    tile_of_constants(2, "wb")
-    V(fill(T.tu[:, 0:256], 0.0), "", "tz")
-    V(fill(T.nm[:, 0:1], 0.0), "", "nm0")
-    V(ts(T.nm[:, 1:65], T.i4[:, 0:64], col(ELEM), -HUGE, A.not_equal, A.mult), "i40 i41 i42 i43 pc", "nm")
-    quant("c", T.ct[:, 0:512], 0, 128, " ".join("c0%d" % k for k in range(8)), "qc0")
-    V(cp(T.mo[:], T.mi[:]), "mi", "mo")
-    V(ts(T.mq[:], T.mi[:], 2, None, A.logical_shift_right), "mi", "mq")
-    act(T.thr0[:], T.pat[:, 0:256].indirect(T.mo[:, 0:16]), "pat mo", "thr0")
-    quant_e(0)
-    V(cp(T.ls0[:], T.mq[:]), "mq", "ls0")
-    turn("thr", "ld_thr", "thr0")
-    turn("ls", "ld_ls", "ls0")
+    def spread(name, src, func=COPY, step=1, **kw):
+        for k in range(4):
+            act(T[name][:, 64 * k * step:64 * (k + 1) * step:step], T[src][:, 0:64], src, name + "%d" % k, func, **kw)
+        writer[name] = writer[name + "3"]
+
+    def step(k):
+        V(ts(T.step[:, 64 * k:64 * k + 64], T.edge[:], MASK / M, -1.0, A.mult, A.add), "edge", "step%d" % k)
+
+    dma("S", T.mi[:], T.m[:], "ld_m", "", "mi")
+    dma("A", T.u0[:], T.u[:], "ld_u", "", "u0")
+    op("G", lambda: g.iota(T.pi[:, 4:5], [[0, 1]], 0, 1), [], ["pi4"])
+    iota("pick8i", [[16, 8]], 0, 0)
+    iota("i16", [[0, 5], [1, 16]], 0, 0)
+    V(fill(T.fl[:, 0:528], 0.0), "", "zero u10")
+    op("G", lambda: g.affine_select(T.eb[:], T.fl[:, 0:528], [[-1, 528]], A.not_equal, 1.0, 3, 4), ["zero", "u10"], ["eb"])
+    iota("n16", [[16, 16]], 0, 0)
+    iota("unit", [[0, 256]], 1, 0)
+    iota("i4", [[0, 16], [1, 4]], 0, 0)
+    V(ts(T.pi[:, 0:1], T.pi[:, 4:5], 15, None, A.bitwise_and), "pi4", "pi0")
+    V(ts(T.pi[:, 1:2], T.pi[:, 4:5], 2, 3, A.logical_shift_right, A.bitwise_and), "pi4", "pi1")
+    V(ts(T.pi[:, 2:3], T.pi[:, 4:5], 3, None, A.bitwise_and), "pi4", "pi2")
+    dma("S", T.x0[:, 0:512], T.x[:, 0:512], "ld_xa", "zero", "x0a")
+    dma("S", T.x0[:, 512:1024], T.x[:, 512:1024], "ld_xb", "", "x0b")
+    dma("S", T.qw[:].bitcast(dt.uint8), T.wc[:], "ld_wc", "x0a x0b", "qw")
+    dma("S", T.sw[:], T.ws[:], "ld_ws", "", "sw")
+    act(T.ones[:], T.fl[:, 0:528], "zero u10", "ones")
+    V(cp(T.pick8[:], T.pick8i[:]), "pick8i", "pick8")
+    V(cp(T.pc[:, 0:3], T.pi[:, 0:3]), "pi0 pi1 pi2", "pc")
+    V(fill(T.fl[:, 528:1024], 0.0), "", "zero2 u11")
+    V(ts(T.own16[:], T.i16[:], col(RES), M, A.is_equal, A.mult), "i16 pc", "own16")
     quant("u", T.u0[:], 0, 128, "u0", "qu")
-    quant_e(1)
+    V(fill(T.ones[:, 4:528:4], 1.0 / 64), "", "ones")
+    V(tt(T.edge[:], T.own16[:, 1:65], T.own16[:, 0:64], A.subtract), "own16", "edge")
+    column(CL, RES, "cl", 1.0, -14.0)
+    act(col(CN), T.own16[:, 0:1], "own16", "cn", scale=-MASK / M, bias=MASK)
+    column(C0, RES, "c0", -M, 15.0 * M)
     V(cp(T.qu16[:, 0:128].bitcast(dt.uint32), T.qu[:, 0:128].bitcast(dt.uint32).indirect(T.pick8[:, 0:8])), "qu pick8", "qu16")
-    quant_x(0, T.x0, "x0a")
-    quant_x(1, T.x0, "x0b")
     act(T.su16[:, 0:128], T.su[:, 0:128].indirect(T.pick8[:, 0:8]), "qu pick8", "su16")
-    act(col(CA), col(SUB), "pc", "ca", scale=-1.0, bias=1027.0)
-    act(T.mrow[:], T.row[:, 0:256].indirect(T.mo[:, 0:16]), "row mo", "mrow")
-    act(W("jn"), T.n4x[:], "n4x ca", "jn", IDENT, bias=col(CA))
-    quant_e(2)
-    quant_e(3)
-    act(col(INIT1), T.nm[:, 64:65], "nm ca", "init1", IDENT, scale=-1.0, bias=col(CA))
+    spread("hold16", "own16", bias=-1.0)
+    act(col(CD), col(CN), "cn c0", "cd", IDENT, scale=-1.0, bias=col(C0))
+    act(T.win[:, 1:512:2], zeros(256), "zero zero2", "wz")
+    quant_x(0, T.x0, "x0a")
+    quant("c", T.ones[:, 4:516], 0, 128, "ones", "qc0")
+    quant_x(1, T.x0, "x0b")
+    V(ts(T.m20[:], T.mi[:], 2.0, col(CL), A.mult, A.add), "mi cl", "m20")
+    turn("m2", "ld_m2", "m20")
+    for b in range(4):
+        quant_e(b)
+    spread("pa", "own16", step=2)
+    act(Y("leg"), T.n16[:], "n16 pc", "leg", IDENT, bias=col(RES))
+    act(T.f2[:, 1:512:2], zeros(256), "zero zero2", "fz")
+    column(CF, CN, "cf", -1.0, 256.0, "cn")
+    column(CW, RES, "cw", -1.0, 15.0)
+    act(Y("far"), Y("leg"), "leg cf", "far", IDENT, bias=col(CF))
 
-    def sums():
-        quant("c", T.ct[:, 512:1536], 128, 384, " ".join("c%d%d" % (j, k) for j in (1, 2) for k in range(8)), "qc1")
-        V(ts(T.wr4[:], T.pat[:], 1024.0, -256.0, A.add, A.max), "pat", "wr4")
+    def frames():
+        act(T.y2[:, 256:272], zeros(16), "zero", "end")
+        column(CU, CN, "cu", -1.0, M, "cn")
+        column(CG, CN, "cg", 1.0, 256.0, "cn")
+        spread("less16", "own16", scale=-1.0)
 
-    def steps():
-        V(tt(W("md"), T.nm[:, 0:64], T.nm[:, 1:65], A.subtract), "nm0 nm", "md")
-        act(W("md4"), W("md"), "md", "md4", bias=4.0)
+    def marks():
+        act(T.i4[:], T.i4[:], "i4 pc", "i4", ABS, scale=-1.0, bias=col(SUB))
+        spread("wr16", "i16", bias=-256.0)
+        spread("own4", "i4", RELU, scale=-GUEST, bias=GUEST)
 
-    def masks():
-        act(col(DUMP), col(RES), "pc", "cdump", bias=256.0 - OWN)
-        act(col(CM), col(SUB), "pc", "cm", scale=256.0, bias=159.0)
-        act(W("t2"), T.nm[:, 1:65], "nm cdump", "t2", IDENT, scale=2.0, bias=col(DUMP))
-        act(T.behind[:, 64:65], T.nm[:, 64:65], "nm", "end")
-        V(scan(T.raw[:], T.wr4[:], T.mrow[:], 0.0, A.add, A.min), "wr4 mrow", "raw0 raw1")
+    def behind():
+        act(T.i16[:, 0:64], T.edge[:], "edge", "i16", RELU, scale=-1.0, bias=256.0)
+        act(col(CI), T.own16[:, 0:1], "own16", "ci", scale=-0.25, bias=256.0)
 
-    def late_constants():
-        act(col(S0), col(ELEM), "pc", "s0", bias=3072.0)
-        act(T.wr16[:], T.i16[:], "i16 pc", "wr16", ActivationFunctionType.Abs, scale=-1.0, bias=col(RES))
+    def quarters():
+        act(T.fa[:, 0:512:2], T.own4[:], "own4", "wr4", scale=5.25, bias=-256.0)
+        column(S0, ELEM, "s0", 1.0, 3072.0)
+        column(C96, SUB, "c96", 256.0, 96.0 - GUEST - 768.0)
+        column(C192, SUB, "c192", 256.0, 192.0 - GUEST - 768.0)
         act(col(SLOTC), col(SUB), "pc s0", "slotc", IDENT, scale=-1024.0, bias=col(S0))
-        act(T.wr16[:], T.wr16[:], "wr16", "wr16", ActivationFunctionType.Relu, scale=-4352.0, bias=4352.0)
-        act(col(OFFC), col(ELEM), "pc", "offc", bias=4092.0)
-        act(T.wr16[:], T.wr16[:], "wr16", "wr16", bias=-256.0)
-        act(col(CI), col(RES), "pc", "ci", scale=-256.0, bias=3840.0)
-        act(T.hh[:, 1024:1040], T.zero[:, 0:16], "zero", "hz")
+        act(T.hh[:, 1024:1040], zeros(16), "zero", "hz")
+        column(C1, RES, "c1", -2.0, 31.0)
+        act(T.wave[:, 16:32], zeros(16), "zero", "wz2")
+        column(OFFC, SLOTC, "offc", 1.0, 4.0 * GUEST, "slotc")
 
     def inverse():
-        V(ts(T.inv0[:], T.raw[:, 15:256:16], col(CI), None, A.add), "raw0 raw1 ci", "inv0")
+        V(ts(T.inv0[:], T.raw[:, 0:256:16], col(CI), None, A.add), "raw ci", "inv0")
         turn("inv", "ld_inv", "inv0")
-        turn("dm", "ld_dm", "dm0")
+        turn("tab", "ld_tab", "iv")
         dma("S", T.v0[:], T.v[:], "ld_v", "", "v0")
 
     once = {
-        "scored": lambda: V(ts(T.dump[:, 1:128:2], T.zero[:, 0:64], -HUGE, None, A.add), "zero", "dump1"),
-        "count": sums,
-        "looked": steps,
-        "again": masks,
-        "waves": lambda: V(tt(W("a1"), T.raw[:, 3:256:4], W("jn"), A.add), "raw0 raw1 jn", "a1"),
-        "paired": lambda: V(ts(T.dm0[:], W("a1"), -1.0, col(CM), A.mult, A.add), "a1 cm", "dm0"),
-        "counted": lambda: V(tt(T.dump[:, 0:128:2], W("t2"), T.n16[:], A.add), "t2 n16", "dump"),
-        "order": late_constants,
-        "sent": lambda: V(cp(T.iv[:, 0:256].indirect(T.mo[:, 0:16]), T.row[:, 0:256]), "row mo", "iv"),
-        "travel": lambda: V(scan(T.raw[:], T.wr16[:], T.iv[:], 0.0, A.add, A.min), "wr16 iv", "raw0 raw1"),
-        "guests": inverse,
+        "c2": lambda: quant("c", T.ones[:, 2:514], 128, 256, "ones", "qc2"),
+        "high": lambda: V(ts(T.pb[:, 1:512:2], zeros(256), 2.0 * M, None, A.add), "zero zero2", "kk16"),
+        "row": lambda: iota("row", [[1, 256]], 0, 0),
+        "anew": lambda: op("G", lambda: g.affine_select(T.anew[:], T.unit[:, 0:192], [[0, 64], [1, 3]], A.is_gt, 0.0, 0, 0), ["unit"], ["anew"]),
+        "mo": lambda: V(ts(T.mo[:], T.mi[:], 2.0, 1.0, A.mult, A.add), "mi", "mo"),
+        "even": lambda: act(T.tab0[:, 0:512:2], T.row[:], "row", "iv"),
+        "inv": lambda: V(scan(T.raw[:, ::-1], T.wr16[:, ::-1], T.tab0[:, 511::-2], 0.0, A.add, A.min), "wr16 iv", "raw"),
+        "dm": lambda: V(tt(Y("dm"), T.mi[:], Y("leg"), A.subtract), "mi leg", "dm"),
+        "l2": lambda: V(tt(Y("l2"), Y("uc"), Y("dm"), A.mult), "uc dm", "l2"),
+        "l3": lambda: V(tt(Y("l3"), Y("l2"), Y("leg"), A.add), "l2 leg", "l3"),
+        "list2": lambda: V(cp(T.list2[:], Y("l3")), "l3", "list2"),
+        "frames": frames, "marks": marks, "behind": behind, "quarters": quarters, "turn": inverse,
     }
-
+    for k in range(4):
+        once["s%d" % k] = lambda k=k: step(k)
+        once["iv%d" % k] = lambda k=k: V(cp(T.tab0[:, 0:512].indirect(T.mo[:, 4 * k:4 * k + 4]), T.row[:, 64 * k:64 * k + 64]), "row mo", "iv")
     fs = ["f0%d f1%d f2%d f3%d" % (h, h, h, h) for h in (0, 1)]
-    q64 = slice(64, 128)
+    end16 = slice(15, 256, 16)
+    u1, u2 = T.fl[:, 0:1024:4], T.f2[:, 0:512:2]
 
-    def unpack(b, h, bank, half="TA"):
+    def unpack(b, h, half="TA"):
+        bank = "b%d" % b
         if "T" in half:
             mm(bank, "e", 128 * b, "x", 128 * h, 128 * h + 128, "qe%d qx%d" % (b, h))
         if "A" in half:
             act(T.fg[:, 384 + 512 * h + b:896 + 512 * h:4], T[bank][:, 0:128], bank, "f%d%d" % (b, h))
-
-    def look_up(t, win, a, r, w, keep):
-        n, lists = 16 * LOOK, T["ls%d" % t]
-        if LOOK == 16:
-            V(tt(T.tu[:, a + 256:a + 512], T[win][:, 0:64].indirect(lists[:, 0:16]), T.tu[:, a:a + 256], A.mult), win + " ls%d " % t + r, w)
-            return
-        act(T.far[:, n:256], T[win][:, 0:64].indirect(lists[:, LOOK:16]), win + " ls%d" % t, "far")
-        V(tt(T.tu[:, a + 256:a + 256 + n], T[win][:, 0:64].indirect(lists[:, 0:LOOK]), T.tu[:, a:a + n], A.mult), win + " ls%d " % t + r, w + "a")
-        V(scan(T.tu[:, a + 256 + n:a + 512], T.tu[:, a + n:a + 256], T.far[:, n:256], 0.0, keep, A.mult), "far " + r, w)
 
     def scale_z(parts):
         for q, b, h in parts:
@@ -317,129 +317,137 @@ def rank_program(g, core, T, topo):
         order("G", [writer[tok]])
         g.remote_dma(out, in_, T.sem[sem], T.sem.loc, pid, rid, mask)
 
+    def export(t, h):
+        a, b, sem = 128 * h, 128 * h + 128, ("ag%d", "ah%d")[h] % t
+        quant("f%d" % t, T.fg[:, 384 + 4 * a:384 + 4 * b], a, b, fs[h], "qf")
+        send(T["qh%d" % t][:, a:b].bitcast(dt.uint8), T["qf%d" % t][:, a:b].bitcast(dt.uint8), sem, "qf")
+        send(T["sh%d" % t][:, a:b], T["sf%d" % t][:, a:b], sem, "qf")
+        writer["hq%d" % h] = (sem, 2 * neng, {})
+
     for t in range(R):
         def at(place):
             if t == 0:
-                once[place]()
-        mm("k0", "u16", 0, "x", 0, 128, "qu16 su16 qx0")
-        parts = [(b, 0, "b%d" % b) for b in range(4)] + [(b, 1, ("k3", "b0", "b1", "b2")[b]) for b in range(4)]
-        n0, n1, n2 = UNPACK[min(t, 1)]
-        for part in parts[:n0]:
-            unpack(*part)
-        mm("k1", "u16", 0, "x", 128, 256, "qu16 su16 qx1")
-        for part in parts[n0:n1]:
-            unpack(*part)
-        for h in (0, 1):
-            V(tt(T.tu[:, 256 + 128 * h:384 + 128 * h], T["k%d" % h][:, 0:128], T["thr%d" % t][:, 128 * h:128 * h + 128], A.is_le),
-              "k%d thr%d" % (h, t), "u1%d" % h)
-        V(fill(T.sl[:, 0:96], 256.0), "", "sl")
-        at("scored")
-        quant("1", T.tu[:, 0:512], 0, 128, "u10 u11 tz", "q1")
-        mm("k2", "c", 0, "1", 0, 128, "qc0 q1")
-        at("count")
-        for part in parts[n1:n2]:
-            unpack(*part, half="T")
-        mm("k0", "c", 128, "1", 0, 128, "qc1 q1")
-        V(ts(T.nl1[:], T.k2[:, q64], 3.5, -1.0, A.is_ge, A.mult), "k2", "nl1")
-        quant("f%d" % t, T.fg[:, 384:896], 0, 128, fs[0], "qf")
-        look_up(t, "nl1", 256, "u10 u11", "u2", A.max)
-        for part in parts[n1:n2]:
-            unpack(*part, half="A")
-        for part in parts[n2:]:
-            unpack(*part)
-        mm("k1", "c", 256, "1", 0, 128, "qc1 q1")
-        at("looked")
-        if t == R - 1:
-            quant("v", T.v0[:], 0, 128, "v0", "qv")
-        quant("2", T.tu[:, 256:768], 0, 128, "u2", "q2")
-        at("again")
-        mm("k2", "c", 0, "2", 0, 128, "qc0 q2")
-        for bank, a in (("k3", 128), ("b0", 256)):
-            mm(bank, "c", a, "1", 0, 128, "q1", True, False)
-            mm(bank, "c", a, "2", 0, 128, "q2", False, True)
-        mm("b1", "c", 128, "2", 0, 128, "q2", True, False)
-        mm("b2", "c", 256, "2", 0, 128, "q2", True, False)
-        V(scan(W("cum1"), T.k0[:, q64], W("md4"), col(INIT1), A.add, A.subtract), "k0 md4 init1", "cum1")
-        quant("f%d" % t, T.fg[:, 896:1408], 128, 256, fs[1], "qf")
-        send(T["qh%d" % t][:].bitcast(dt.uint8), T["qf%d" % t][:].bitcast(dt.uint8), "ah%d" % t, "qf")
-        send(T["sh%d" % t][:], T["sf%d" % t][:], "ah%d" % t, "qf")
-        V(ts(T.nl2[:], T.k2[:, q64], -3.5, -1.0, A.is_gt, A.mult), "k2", "nl2")
-        V(tt(W("x1"), T.k1[:, q64], W("cum1"), A.add), "k1 cum1", "x1")
-        V(ts(W("u1s"), T.k1[:, q64], -512.0, None, A.is_le), "k1", "u1s")
-        look_up(t, "nl2", 512, "u2", "u3", A.min)
-        V(scan(W("cum2"), T.k3[:, q64], W("md"), 0.0, A.add, A.add), "k3 md", "cum2")
-        quant("3", T.tu[:, 512:1024], 0, 128, "u3", "q3")
-        act(W("t1"), W("x1"), "x1 cum2", "t1", IDENT, scale=-1.0, bias=W("cum2", 63))
-        mm("k2", "c", 128, "3", 0, 128, "q3")
-        mm("k0", "c", 256, "3", 0, 128, "q3")
-        mm("b1", "c", 128, "3", 0, 128, "q3", False, True)
-        mm("b2", "c", 256, "3", 0, 128, "q3", False, True)
-        V(tt(W("pp2"), T.b0[:, q64], W("cum2"), A.add), "b0 cum2", "pp2")
-        def own_or_partner(k):
-            if k:
-                V(tt(W("an"), W("a1"), W("jn"), A.add), "a1 jn", "an")
-            else:
-                V(tt(W("a1"), W("u1s"), T["dm%d" % t][:], A.mult), "u1s dm%d" % t, "a1")
+                for n in ONCE.get(place, "").split():
+                    once[n]()
         last = t == R - 1
-        if t:
-            own_or_partner(0)
-        at("waves")
-        V(tt(T.pair[:, 1:128:2], W("pp2"), W("t1"), A.min), "pp2 t1", "known")
-        V(scan(T.behind[:, 63::-1], T.k2[:, 127:63:-1], T.small[:, 63::-1], T.nm[:, 64:65], A.add, A.add), "k2 md nm", "behind")
-        if t:
-            own_or_partner(1)
+        for h in (0, 1):
+            mm("k%d" % h, "u16", 0, "x", 128 * h, 128 * h + 128, "qu16 su16 qx%d" % h)
+        for b in range(3):
+            unpack(b, 0)
+        for h in (0, 1):
+            V(ts(T.fl[:, 512 * h:512 * h + 512:4], T["k%d" % h][:, 0:128], 0.0, None, A.is_le), "k%d" % h, "u1%d" % h)
+        quant("1", T.fl[:, 0:512], 0, 128, "u10 zero", "q10")
+        mm("k2", "c", 0, "1", 0, 128, "qc0 q10")
+        quant("1", T.fl[:, 512:1024], 128, 256, "u11 zero", "q11")
+        mm("k3", "c", 0, "1", 128, 256, "qc0 q11")
+        unpack(3, 0, "T")
+        V(scan(T.su1s[:], T.hold16[:], u1, 0.0, A.add, A.min), "hold16 u10 u11", "su1")
+        at("scored")
+        V(scan(T.known[:], T.unit[:], u1, -1.0, A.add, A.subtract), "unit u10 u11", "known")
+        V(tt(Y("l1"), T["m2%d" % t][:], T.su1s[:, end16], A.subtract), "m2%d su1" % t, "l1")
+        at("listing")
+        act(Y("d2"), T.su1s[:, end16], "su1 cd", "d2", IDENT, scale=M, bias=col(CD))
+        act(T.win[:, 0:256:2], T.k2[:, 0:128], "k2", "wa", SIGN, bias=-0.875)
+        act(T.win[:, 256:512:2], T.k3[:, 0:128], "k3", "wb", SIGN, bias=-0.875)
+        unpack(3, 0, "A")
+        V(keep(T.sk[:], T.known[:]), "pa known", "sk")
+        V(cp(T.list1[:], Y("l1")), "l1", "list1")
+        V(tt(Y("e1"), T.sk[:, end16], Y("d2"), A.add), "sk d2", "e1")
+        for b in range(3):
+            unpack(b, 1, "T")
+        n = LOOK[0]
+        act(T.f2[:, 0:32 * n:2], T.win[:, 0:512].indirect(T.list1[:, 0:n]), "wa wb wz list1", "u2a", RELU)
+        V(ts(T.f2[:, 32 * n:512:2], T.win[:, 0:512].indirect(T.list1[:, n:16]), 0.0, None, A.max), "wa wb wz list1", "u2b")
+        unpack(3, 1, "T")
+        for b in range(4):
+            unpack(b, 1, "A")
+        if not t:
+            act(Y("uc"), T.su1s[:, end16], "su1 cw", "uc", IDENT, bias=col(CW))
+        if last:
+            act(Y("uc"), T.su1s[:, end16], "su1 c1", "uc", IDENT, scale=2.0, bias=col(C1))
+        export(t, 0)
+        at("count")
+        quant("2", T.f2[:], 0, 128, "u2a u2b fz", "q2")
+        mm("k0", "c", 0, "2", 0, 128, "q2")
+        mm("k1", "c", 128, "2", 0, 128, "qc2 q2")
+        V(scan(T.y2[:, 255::-1], T.f2[:, 510::-2], T.fl[:, 1020::-4], 0.0, A.add, A.subtract), "u2a u2b u10 u11", "y2")
+        V(tt(Y("ee"), Y("e1"), Y("far"), A.min), "e1 far", "ee")
+        at("behind")
+        V(keep(T.sy[:], T.y2[:, 0:256]), "pa y2", "sy")
+        V(keep(T.sn[:], T.y2[:, 1:257]), "pa y2 end", "sn")
+        at("looked")
+        act(col(N2), T.y2[:, 0:1], "y2 cg", "n2", IDENT, scale=-1.0, bias=col(CG))
+        act(Y("uu"), T.sy[:, end16], "sy cu", "uu", IDENT, scale=M + 1.0, bias=col(CU))
+        act(Y("dn"), T.sn[:, end16], "sn", "dn", scale=-M)
+        at("lifted")
+        V(tt(T.win[:, 0:512:4], T.k0[:, 0:128], T.win[:, 0:512:4], A.is_lt), "k0 wa wb", "wa")
+        V(tt(T.win[:, 2:512:4], T.k1[:, 0:128], T.win[:, 2:512:4], A.is_lt), "k1 wb", "wb")
+        export(t, 1)
         at("paired")
-        at("counted")
-        V(tt(T.pair[:, 0:128:2], T.k0[:, q64], T.behind[:, 1:65], A.subtract), "k0 behind end", "pp3")
-        at("order")
-        V(scan(W("cum1"), T.b1[:, q64], T.zero[:, 0:64], 0.0, A.add, A.add), "b1 zero", "cum1")
-        if t == 0:
-            own_or_partner(0)
-        V(scan(T.least[:], T.dump[:], T.pair[:], -HUGE, A.max, A.min), "dump dump1 pp3 known", "least")
-        V(tt(W("kk"), T.b2[:, q64], W("cum1"), A.add), "b2 cum1", "kk")
-        if t == 0:
-            own_or_partner(1)
+        n = LOOK[1]
+        act(T.f3[:, 0:16 * n], T.win[:, 0:512].indirect(T.list1[:, 0:n]), "wa wb list1", "f3a", bias=-1.0)
+        V(ts(T.f3[:, 16 * n:256], T.win[:, 0:512].indirect(T.list1[:, n:16]), -1.0, None, A.add), "wa wb list1", "f3b")
+        V(tt(Y("c2"), Y("uu"), Y("dn"), A.add), "uu dn", "c2")
+        at("placed")
         if last:
-            V(ts(W("t1"), T.k0[:, q64], -512.0, 1.0, A.is_le, A.add), "k0", "t1")
-        V(ts(T.pos[:], T.least[:, 7:128:8], T.behind[:, 0:1], OWN, A.add, A.add), "least behind", "pos")
-        V(ts(W("t6"), W("kk"), OWN - 96.0, 96.0, A.is_le, A.mult), "kk", "t6")
-        V(ts(W("t7"), W("kk"), OWN - 192.0, 96.0, A.is_le, A.mult), "kk", "t7")
-        V(cp(T.sl[:, 0:768].indirect(T.pos[:, 0:16]), T.lam[:, 0:256]), "pos lam", "sl")
-        V(tt(W("sm"), W("kk"), W("t6"), A.add), "kk t6", "sm")
-        V(scan(T.ws96[:], T.wr4[:, 0:96], T.sl[:, 0:96], 0.0, A.add, A.min), "wr4 sl", "ws96")
-        if t == 0:
-            V(tt(W("gn"), W("sm"), W("t7"), A.add), "sm t7", "gn")
-        if last:
-            V(tt(W("pp2"), W("t1"), W("u1s"), A.add), "t1 u1s", "pp2")
+            V(tt(Y("w1"), T.sy[:, end16], T.sn[:, end16], A.subtract), "sy sn", "w1")
+        V(scan(T.pb[:, 510::-2], T.step[:, ::-1], T.f3[:, ::-1], T.y2[:, 0:1], A.add, A.subtract), "step0 step1 step2 step3 f3a f3b y2", "y3")
+        V(tt(T.pb[:, 31:512:32], Y("ee"), Y("c2"), A.min), "ee c2", "kk16")
+        V(scan(T.pa[:, 1:512:2], T.less16[:], T.f3[:], 0.0, A.min, A.mult), "less16 f3a f3b", "n3")
+        act(T.sl[:, 0:96], zeros(96), "zero", "sl", bias=256.0)
+        act(T.s4[:], T.f3[:], "f3a f3b", "s4 n3s", accum_out=col(N3))
+        act(col(N23), col(N3), "n3s n2", "n23", IDENT, bias=col(N2))
+        V(scan(T.u4[:], u2, T.f3[:], 0.0, A.max, A.mult), "u2a u2b f3a f3b", "u4")
+        at("third")
+        V(scan(T.least[:], T.pa[:], T.pb[:], 0.0, A.add, A.min), "pa n3 y3 kk16", "least")
+        at("least")
+        V(scan(T.fb[:, 0:512:2], zeros(256), T.u4[:], -1.0, A.add, A.subtract), "zero zero2 u4", "k4")
+        if t:
+            act(T.fb[:, 1:512:2], T["tab%d" % t][:, 0:512].indirect(T.list1[:, 0:16]), "tab%d list1" % t, "src", bias=-256.0)
+        else:
+            act(T.fb[:, 1:512:2], T.row[:, 0:256].indirect(T.list2[:, 0:16]), "row list2", "src", bias=-256.0)
+        V(ts(T.pos[:], T.least[:, 31:512:32], col(N23), None, A.add), "least n23", "pos")
+        V(scan(T.fa[:, 1:512:2], T.own4[:], T.u4[:], 0.0, A.max, A.mult), "own4 u4", "n4")
+        at("pos")
+        V(cp(T.sl[:, 0:768].indirect(T.pos[:, 0:16]), T.row[:, 0:256]), "pos row", "sl")
+        V(scan(T.from4[:, 0:256], T.fa[:, 0:256], T.fb[:, 0:256], 0.0, A.add, A.min), "wr4 n4 k4 src", "from0")
+        V(scan(T.ws96[:], T.fa[:, 0:192:2], T.sl[:, 0:96], 0.0, A.add, A.min), "wr4 sl", "ws96")
+        V(scan(T.from4[:, 256:512], T.fa[:, 256:512], T.fb[:, 256:512], 0.0, A.add, A.min), "wr4 n4 k4 src", "from1")
         V(ts(T["slot%d" % t][:], T.ws96[:, 3:96:4], 4.0, col(SLOTC), A.mult, A.add), "ws96 slotc", "slot")
         send(T["land%d" % t][:], T["slot%d" % t][:], "al%d" % t, "slot")
-        if t:
-            V(tt(W("gn"), W("sm"), W("t7"), A.add), "sm t7", "gn")
-        writer["hq"] = ("ah%d" % t, 2 * neng, {})
         writer["land"] = ("al%d" % t, neng, {})
-        for b, bank in enumerate(("b3", "k3", "b0", "k2")):
-            mm(bank, "e", 128 * b, "h%d" % t, 0, 256, "hq")
-            act(T.hh[:, b:1024:4], T[bank][:, 0:256], bank, "h%d" % b)
+        for h in (0, 1):
+            for b in range(4):
+                bank = "bk"[h] + "%d" % b
+                mm(bank, "e", 128 * b, "h%d" % t, 128 * h, 128 * h + 128, "hq%d" % h)
+                act(T.hh[:, 512 * h + b:512 * h + 512:4], T[bank][:, 0:128], bank, "h%d%d" % (b, h))
+        src = T.from4[:, 7:512:8]
+        at("chosen")
+        V(cp(T.three[:, 0:192:3], src), "from0 from1", "t5")
+        V(ts(T.three[:, 1:192:3], src, col(C96), -96.0, A.is_ge, A.mult), "from0 from1 c96", "t6")
+        V(ts(T.three[:, 2:192:3], src, col(C192), -96.0, A.is_ge, A.mult), "from0 from1 c192", "t7")
         at("sent")
+        if t == R - 2:
+            quant("v", T.v0[:], 0, 128, "v0", "qv")
         if last:
-            V(ts(W("t2"), W("kk"), 512.0, 2.0, A.is_ge, A.mult), "kk", "t2")
-        V(tt(W("ff"), W("gn"), W("an"), A.max), "gn an", "ff")
+            V(ts(Y("l3"), T.least[:, 31:512:32], col(CF), None, A.is_ge), "least cf", "l3")
+            V(tt(Y("w2"), Y("w1"), Y("uc"), A.add), "w1 uc", "w2")
+        V(scan(T.sums[:], T.anew[:], T.three[:], 0.0, A.mult, A.add), "anew t5 t6 t7", "gn")
         at("travel")
         if last:
-            V(tt(W("pp3"), W("pp2"), W("t2"), A.add), "pp2 t2", "pp3")
-        V(ts(T.off[:], W("ff"), -4.0, col(OFFC), A.mult, A.add), "ff offc", "off")
-        if last:
-            V(lambda: g.vector.transpose(W("m21"), W("pp3")), "pp3", "m21")
-        r = "h0 h1 h2 h3 hz land"
+            V(tt(T.wave[:, 0:16], Y("w2"), Y("l3"), A.add), "w2 l3", "wave")
+        V(ts(T.off[:], T.sums[:, 2:192:3], 4.0, col(OFFC), A.mult, A.add), "gn offc", "off")
+        at("listed")
+        r = "h00 h10 h20 h30 h01 h11 h21 h31 hz land"
         a = GUESTS[min(t, 1)]
         if a:
             V(cp(T.fg[:, 0:16 * a], T.hh[:, 0:1040].indirect(T["land%d" % t][:, 0:a])), r, "g0")
         act(T.fg[:, 16 * a:384], T.hh[:, 0:1040].indirect(T["land%d" % t][:, a:24]), r, "g1" if a else "g0 g1")
         at("guests")
         if last:
-            V(cp(T.wc16[:], W("m21", 0, 64, 4)), "m21", "wc16")
-            for k in range(4):
-                dma("S", T.wv[k % 2:8:2, 128 * (k // 2):128 * (k // 2) + 128], T.wc16[:, 4 * k:4 * k + 4], "st", "wc16")
+            V(lambda: g.vector.transpose(T.turned[:], T.wave[:]), "wave wz2", "turned")
+            for k in range(8):
+                dma("S", T.wv[k, :], T.turned[32 * (k // 2):32 * (k // 2) + 16, 16 * (k % 2):16 * (k % 2) + 16], "st", "turned")
         r = " ".join(fs) + " g0 g1 off"
         for h in (0, 1):
             a, m, e = FILL[h]
@@ -449,10 +457,12 @@ def rank_program(g, core, T, topo):
                 scale_z(SCALE[:EARLY])
             else:
                 V(cp(T.z[:, 512:16 * FILL[1][0]], T.fg[:, 0:1408].indirect(T.off[:, 32:FILL[1][0]])), r, "zw")
+                at("half")
             quant("z", T.z[:, 512 * h:512 * h + 512], 128 * h, 128 * h + 128, "zv%d za%d" % (h, h), "qz%d" % h)
             for b, k in (SUMS[FIRST:] if h else SUMS[:FIRST]):
                 mm("bk"[k] + "%d" % b, "w", 128 * b, "z", 128 * k, 128 * k + 128, "qw sw qz%d" % k)
         scale_z(SCALE[EARLY:])
+        at("sums")
         for b, h in SUMS:
             bank, a = "bk"[h] + "%d" % b, 512 * h + 128 * b
             V(tt(T["tt%d" % b][:, 128 * h:128 * h + 128], T[bank][:, 0:128], T.z32[:, a:a + 128], A.add), bank + " y%d%d" % (b, h), "tt%d%d" % (b, h))
@@ -474,6 +484,6 @@ def rank_program(g, core, T, topo):
     for k in range(4):
         dma("AS"[k // 2], T.osc[4 * k:4 * k + 4, :], T.sx[32 * k:32 * k + 4, :], ("st2", "st")[k // 2], "qx0 qx1")
     store_y(1)
-    g.wait_ge(T.sem.loc, 3 * R * neng)
+    g.wait_ge(T.sem.loc, 5 * R * neng)
     for s in sorted(count, key=lambda n: n == "st"):
         g.wait_ge(T.sem[s], count[s])

from concourse.mybir import dt, AluOpType, ActivationFunctionType

R = 3
GUEST = 544.0
M = 1024.0
MASK = 1536.0
TINY = "l1 l2 l3 uc leg d2 dn e1 ee uu c2 dm far w1 w2".split()
SHARES = (("A", 0, 0, 16), ("A", 1, 0, 16), ("A", 2, 8, 16),
          ("V", 2, 0, 8), ("V", 3, 0, 8), ("V", 3, 8, 16), ("Q", 0, 0, 8), ("Q", 1, 8, 16))
SCALE = (("V", 2, 0), ("V", 1, 0), ("A", 0, 0), ("A", 0, 1), ("A", 2, 1), ("A", 1, 1), ("A", 3, 1), ("A", 3, 0))
EARLY = 2
LOOK = (8, 8)
GUESTS = (0, 12)
FIRST = 3
SUMS = ((2, 0), (1, 0), (0, 0), (0, 1), (2, 1), (1, 1), (3, 1), (3, 0))
FILL = ((0, 16, 32), (38, 44, 64))
ONCE = {"scored": "dm", "listing": "c2", "count": "s0 frames row", "behind": "high s1", "lifted": "behind", "paired": "s2 l2 anew",
        "placed": "l3 s3 marks", "third": "list2", "least": "quarters", "pos": "mo even", "chosen": "iv0", "sent": "iv1", "travel": "iv2", "listed": "iv3", "half": "inv", "sums": "turn"}


def _scratch():
    s = {}

    def sb(d, w, names):
        for n in names.split():
            s[n] = ("sbuf", [128, w], d)

    for w, names in ((128, "u u16 v 2"), (256, "x z 1 c f0 f1 f2 h0 h1 h2"), (512, "w e")):
        for n in names.split():
            s["q" + n] = ("sbuf", [128, w], "float8_e4m3fn_x4")
            s["s" + n] = ("sbuf", [128, w], "uint8")
    sb("bfloat16", 1408, "fg")
    sb("bfloat16", 1040, "hh")
    sb("bfloat16", 1024, "x0 z z32 xt fl")
    sb("bfloat16", 528, "eb ones")
    sb("bfloat16", 768, "sl")
    sb("bfloat16", 512, "u0 v0 f2 win pa fa fb tab0 tab1 tab2")
    sb("bfloat16", 256, "row hold16 less16 own4 wr16 u4 f3 known unit su1s sy sn sk s4 tt0 tt1 tt2 tt3")
    sb("bfloat16", 272, "y2")
    sb("bfloat16", 192, "anew")
    sb("bfloat16", 80, "i16 own16")
    sb("bfloat16", 64, "edge i4")
    sb("float16", 512, "pb least from4")
    sb("float16", 256, "step raw")
    sb("float16", 192, "three sums")
    sb("float16", 96, "ws96")
    sb("uint16", 16, "inv0 inv1 inv2 mo pos list1 list2")
    sb("uint16", 64, "off")
    sb("uint16", 24, "slot0 slot1 slot2 land0 land1 land2")
    sb("uint16", 8, "pick8")
    sb("int32", 8, "pick8i pi")
    sb("int32", 16, "mi")
    sb("float32", 24, "pc")
    sb("float32", 16, "n16 m20 m21 m22")
    sb("float32", 32, "wave turned")
    sb("float32", 16 * len(TINY), "tiny")
    sb("float32", 256, "yb")
    for n in "k0 k1 k2 k3 b0 b1 b2 b3".split():
        s[n] = ("psum", [128, 512], "float32")
    return s


SCRATCH = _scratch()
LOADS = ["u", "xa", "xb", "v", "wc", "ws", "m", "m2", "inv", "tab"]
SEMAPHORES = (["sV", "sT", "sA", "sG", "loc", "st", "st2"] + ["ld_" + n for n in LOADS]
              + ["ag0", "ag1", "ag2", "ah0", "ah1", "ah2", "al0", "al1", "al2"])


def rank_program(g, core, T, topo):
    rank = T.rank_of(core)
    if rank is None:
        return
    A = AluOpType
    COPY, IDENT = ActivationFunctionType.Copy, ActivationFunctionType.Identity
    SIGN, RELU, ABS = ActivationFunctionType.Sign, ActivationFunctionType.Relu, ActivationFunctionType.Abs
    nxt = T.cores[(rank + 1) % len(T.cores)]
    rid, pid = topo.addr(nxt)[0], topo.addr(nxt)[1]
    mask, neng = topo.mask(core, nxt), len(topo.engines(core, nxt))
    queues = {"V": g.vector, "T": g.tensor, "A": g.scalar, "G": g, "S": g.sync}
    known = {q: {} for q in queues}
    count, writer, readers = {}, {}, {}

    def order(q, need):
        best = {}
        for e in need:
            if known[q].get(e[0], 0) < e[1] and (e[0] not in best or best[e[0]][1] < e[1]):
                best[e[0]] = e
        for s in list(best):
            if any(o != s and best[o][2].get(s, 0) >= best[s][1] for o in best):
                del best[s]
        for s in best:
            _, v, c = best[s]
            queues[q].wait_ge(T.sem[s], v)
            for k in c:
                known[q][k] = max(known[q].get(k, 0), c[k])
            known[q][s] = max(known[q].get(s, 0), v)

    def op(q, fn, r=(), w=(), sem=None, inc=1):
        need = [writer[k] for k in r]
        for k in w:
            if k in writer:
                need.append(writer[k])
            need += [e for qq, e in readers.get(k, {}).items() if qq != q]
        order(q, need)
        i = fn()
        s = sem or "s" + q
        i.then_inc(T.sem[s], inc)
        count[s] = count.get(s, 0) + inc
        c = dict(known[q])
        c[s] = count[s]
        e = (s, count[s], c)
        for k in r:
            readers.setdefault(k, {})[q] = e
        for k in w:
            writer[k] = e
            readers[k] = {}

    def V(fn, r="", w=""):
        op("V", fn, r.split(), w.split())

    def act(out, in_, r, w, func=COPY, **kw):
        op("A", lambda: g.scalar.activation(out, in_, func, **kw), r.split(), w.split())

    def ts(out, in0, s1, s2, op0, op1=None):
        if op1 is None:
            return lambda: g.vector.tensor_scalar(out, in0, s1, None, op0)
        return lambda: g.vector.tensor_scalar(out, in0, s1, s2, op0, op1)

    def tt(out, a, b, o):
        return lambda: g.vector.tensor_tensor(out, a, b, o)

    def cp(out, a):
        return lambda: g.vector.tensor_copy(out, a)

    def fill(ap, v):
        return lambda: g.vector.memset(ap, v)

    def scan(out, a, b, init, o0, o1):
        return lambda: g.vector.tensor_tensor_scan(out, a, b, init, o0, o1)

    def keep(out, src):
        return scan(out, T.pa[:, 0:512:2], src, 0.0, A.add, A.min)

    def quant(n, src, a, b, r, tok):
        V(lambda: g.vector.quantize_mx(T["q" + n][:, a:b], T["s" + n][:, a:b], src), r, tok)

    def mm(bank, ln, la, rn, ra, rb, r):
        op("T", lambda: g.tensor.matmul_mx(T[bank][:, 0:rb - ra], T["q" + ln][:, la:la + 128], T["s" + ln][:, la:la + 128],
                                           T["q" + rn][:, ra:rb], T["s" + rn][:, ra:rb], True, True), r.split(), [bank])

    def dma(q, out, in_, sem, r="", w=""):
        op(q, lambda: queues[q].dma_start(out, in_), r.split(), w.split(), sem, 16)

    def iota(name, pat, base, ch):
        small = SCRATCH[name][2] != "int32"
        op("G", lambda: g.iota(T[name][:], pat, base, ch, allow_small_or_imprecise_dtypes=small), [], [name])

    def turn(name, sem, r):
        for t in (1, 2):
            n = 16 * t
            dma("S", T[name + "%d" % t][0:128 - n, :], T[name + "0"][n:128, :], sem, r, name + "%da" % t)
            dma("S", T[name + "%d" % t][128 - n:128, :], T[name + "0"][0:n, :], sem, r, name + "%d" % t)
        writer[name + "1"] = writer[name + "2"]

    def Y(name):
        k = 16 * TINY.index(name)
        return T.tiny[:, k:k + 16]

    def col(k):
        return T.pc[:, k:k + 1]
    RES, SUB, ELEM, OFFC, S0, SLOTC, CI, CL, CD, CU, CN, N23, CF, CW, C0, C96, C192, C1, CG, N2, N3 = range(21)

    def zeros(n):
        return T.fl[:, 2:4 * n:4]

    def column(out, src, w, scale, bias, r="pc"):
        act(col(out), col(src), r, w, scale=scale, bias=bias)

    def quant_e(b):
        quant("e", T.eb[:, 3 - b:515 - b], 128 * b, 128 * b + 128, "eb", "qe%d" % b)

    def quant_x(h, src, r):
        quant("x", src[:, 512 * h:512 * h + 512], 128 * h, 128 * h + 128, r, "qx%d" % h)

    def spread(name, src, func=COPY, step=1, **kw):
        for k in range(4):
            act(T[name][:, 64 * k * step:64 * (k + 1) * step:step], T[src][:, 0:64], src, name + "%d" % k, func, **kw)
        writer[name] = writer[name + "3"]

    def step(k):
        V(ts(T.step[:, 64 * k:64 * k + 64], T.edge[:], MASK / M, -1.0, A.mult, A.add), "edge", "step%d" % k)

    dma("S", T.mi[:], T.m[:], "ld_m", "", "mi")
    dma("A", T.u0[:], T.u[:], "ld_u", "", "u0")
    op("G", lambda: g.iota(T.pi[:, 4:5], [[0, 1]], 0, 1), [], ["pi4"])
    iota("pick8i", [[16, 8]], 0, 0)
    iota("i16", [[0, 5], [1, 16]], 0, 0)
    V(fill(T.fl[:, 0:528], 0.0), "", "zero u10")
    op("G", lambda: g.affine_select(T.eb[:], T.fl[:, 0:528], [[-1, 528]], A.not_equal, 1.0, 3, 4), ["zero", "u10"], ["eb"])
    iota("n16", [[16, 16]], 0, 0)
    iota("unit", [[0, 256]], 1, 0)
    iota("i4", [[0, 16], [1, 4]], 0, 0)
    V(ts(T.pi[:, 0:1], T.pi[:, 4:5], 15, None, A.bitwise_and), "pi4", "pi0")
    V(ts(T.pi[:, 1:2], T.pi[:, 4:5], 2, 3, A.logical_shift_right, A.bitwise_and), "pi4", "pi1")
    V(ts(T.pi[:, 2:3], T.pi[:, 4:5], 3, None, A.bitwise_and), "pi4", "pi2")
    dma("S", T.x0[:, 0:512], T.x[:, 0:512], "ld_xa", "zero", "x0a")
    dma("S", T.x0[:, 512:1024], T.x[:, 512:1024], "ld_xb", "", "x0b")
    dma("S", T.qw[:].bitcast(dt.uint8), T.wc[:], "ld_wc", "x0a x0b", "qw")
    dma("S", T.sw[:], T.ws[:], "ld_ws", "", "sw")
    act(T.ones[:], T.fl[:, 0:528], "zero u10", "ones")
    V(cp(T.pick8[:], T.pick8i[:]), "pick8i", "pick8")
    V(cp(T.pc[:, 0:3], T.pi[:, 0:3]), "pi0 pi1 pi2", "pc")
    V(fill(T.fl[:, 528:1024], 0.0), "", "zero2 u11")
    V(ts(T.own16[:], T.i16[:], col(RES), M, A.is_equal, A.mult), "i16 pc", "own16")
    quant("u", T.u0[:], 0, 128, "u0", "qu")
    V(fill(T.ones[:, 4:528:4], 1.0 / 64), "", "ones")
    V(tt(T.edge[:], T.own16[:, 1:65], T.own16[:, 0:64], A.subtract), "own16", "edge")
    column(CL, RES, "cl", 1.0, -14.0)
    act(col(CN), T.own16[:, 0:1], "own16", "cn", scale=-MASK / M, bias=MASK)
    column(C0, RES, "c0", -M, 15.0 * M)
    V(cp(T.qu16[:, 0:128].bitcast(dt.uint32), T.qu[:, 0:128].bitcast(dt.uint32).indirect(T.pick8[:, 0:8])), "qu pick8", "qu16")
    act(T.su16[:, 0:128], T.su[:, 0:128].indirect(T.pick8[:, 0:8]), "qu pick8", "su16")
    spread("hold16", "own16", bias=-1.0)
    act(col(CD), col(CN), "cn c0", "cd", IDENT, scale=-1.0, bias=col(C0))
    act(T.win[:, 1:512:2], zeros(256), "zero zero2", "wz")
    quant_x(0, T.x0, "x0a")
    quant("c", T.ones[:, 4:516], 0, 128, "ones", "qc0")
    quant_x(1, T.x0, "x0b")
    V(ts(T.m20[:], T.mi[:], 2.0, col(CL), A.mult, A.add), "mi cl", "m20")
    turn("m2", "ld_m2", "m20")
    for b in range(4):
        quant_e(b)
    spread("pa", "own16", step=2)
    act(Y("leg"), T.n16[:], "n16 pc", "leg", IDENT, bias=col(RES))
    act(T.f2[:, 1:512:2], zeros(256), "zero zero2", "fz")
    column(CF, CN, "cf", -1.0, 256.0, "cn")
    column(CW, RES, "cw", -1.0, 15.0)
    act(Y("far"), Y("leg"), "leg cf", "far", IDENT, bias=col(CF))

    def frames():
        act(T.y2[:, 256:272], zeros(16), "zero", "end")
        column(CU, CN, "cu", -1.0, M, "cn")
        column(CG, CN, "cg", 1.0, 256.0, "cn")
        spread("less16", "own16", scale=-1.0)

    def marks():
        act(T.i4[:], T.i4[:], "i4 pc", "i4", ABS, scale=-1.0, bias=col(SUB))
        spread("wr16", "i16", bias=-256.0)
        spread("own4", "i4", RELU, scale=-GUEST, bias=GUEST)

    def behind():
        act(T.i16[:, 0:64], T.edge[:], "edge", "i16", RELU, scale=-1.0, bias=256.0)
        act(col(CI), T.own16[:, 0:1], "own16", "ci", scale=-0.25, bias=256.0)

    def quarters():
        act(T.fa[:, 0:512:2], T.own4[:], "own4", "wr4", scale=5.25, bias=-256.0)
        column(S0, ELEM, "s0", 1.0, 3072.0)
        column(C96, SUB, "c96", 256.0, 96.0 - GUEST - 768.0)
        column(C192, SUB, "c192", 256.0, 192.0 - GUEST - 768.0)
        act(col(SLOTC), col(SUB), "pc s0", "slotc", IDENT, scale=-1024.0, bias=col(S0))
        act(T.hh[:, 1024:1040], zeros(16), "zero", "hz")
        column(C1, RES, "c1", -2.0, 31.0)
        act(T.wave[:, 16:32], zeros(16), "zero", "wz2")
        column(OFFC, SLOTC, "offc", 1.0, 4.0 * GUEST, "slotc")

    def inverse():
        V(ts(T.inv0[:], T.raw[:, 0:256:16], col(CI), None, A.add), "raw ci", "inv0")
        turn("inv", "ld_inv", "inv0")
        turn("tab", "ld_tab", "iv")
        dma("S", T.v0[:], T.v[:], "ld_v", "", "v0")

    once = {
        "c2": lambda: quant("c", T.ones[:, 2:514], 128, 256, "ones", "qc2"),
        "high": lambda: V(ts(T.pb[:, 1:512:2], zeros(256), 2.0 * M, None, A.add), "zero zero2", "kk16"),
        "row": lambda: iota("row", [[1, 256]], 0, 0),
        "anew": lambda: op("G", lambda: g.affine_select(T.anew[:], T.unit[:, 0:192], [[0, 64], [1, 3]], A.is_gt, 0.0, 0, 0), ["unit"], ["anew"]),
        "mo": lambda: V(ts(T.mo[:], T.mi[:], 2.0, 1.0, A.mult, A.add), "mi", "mo"),
        "even": lambda: act(T.tab0[:, 0:512:2], T.row[:], "row", "iv"),
        "inv": lambda: V(scan(T.raw[:, ::-1], T.wr16[:, ::-1], T.tab0[:, 511::-2], 0.0, A.add, A.min), "wr16 iv", "raw"),
        "dm": lambda: V(tt(Y("dm"), T.mi[:], Y("leg"), A.subtract), "mi leg", "dm"),
        "l2": lambda: V(tt(Y("l2"), Y("uc"), Y("dm"), A.mult), "uc dm", "l2"),
        "l3": lambda: V(tt(Y("l3"), Y("l2"), Y("leg"), A.add), "l2 leg", "l3"),
        "list2": lambda: V(cp(T.list2[:], Y("l3")), "l3", "list2"),
        "frames": frames, "marks": marks, "behind": behind, "quarters": quarters, "turn": inverse,
    }
    for k in range(4):
        once["s%d" % k] = lambda k=k: step(k)
        once["iv%d" % k] = lambda k=k: V(cp(T.tab0[:, 0:512].indirect(T.mo[:, 4 * k:4 * k + 4]), T.row[:, 64 * k:64 * k + 64]), "row mo", "iv")
    fs = ["f0%d f1%d f2%d f3%d" % (h, h, h, h) for h in (0, 1)]
    end16 = slice(15, 256, 16)
    u1, u2 = T.fl[:, 0:1024:4], T.f2[:, 0:512:2]

    def unpack(b, h, half="TA"):
        bank = "b%d" % b
        if "T" in half:
            mm(bank, "e", 128 * b, "x", 128 * h, 128 * h + 128, "qe%d qx%d" % (b, h))
        if "A" in half:
            act(T.fg[:, 384 + 512 * h + b:896 + 512 * h:4], T[bank][:, 0:128], bank, "f%d%d" % (b, h))

    def scale_z(parts):
        for q, b, h in parts:
            a = 512 * h + 128 * b
            out, src, r, w = T.z32[:, a:a + 128], T.z[:, 512 * h + b:512 * h + 512:4], "zv%d za%d" % (h, h), "y%d%d" % (b, h)
            if q == "V":
                V(ts(out, src, 32.0, None, A.mult), r, w)
            else:
                act(out, src, r, w, scale=32.0)

    def store_y(h):
        if h:
            V(cp(T.yb[:, 128:256], T.k1[:, 0:128]), "k1", "yb1")
        else:
            act(T.yb[:, 0:128], T.k0[:, 0:128], "k0", "yb0")
        dma("AS"[h], T.y[:, 128 * h:128 * h + 128], T.yb[:, 128 * h:128 * h + 128], ("st2", "st")[h], "yb%d" % h)

    def send(out, in_, sem, tok):
        order("G", [writer[tok]])
        g.remote_dma(out, in_, T.sem[sem], T.sem.loc, pid, rid, mask)

    def export(t, h):
        a, b, sem = 128 * h, 128 * h + 128, ("ag%d", "ah%d")[h] % t
        quant("f%d" % t, T.fg[:, 384 + 4 * a:384 + 4 * b], a, b, fs[h], "qf")
        send(T["qh%d" % t][:, a:b].bitcast(dt.uint8), T["qf%d" % t][:, a:b].bitcast(dt.uint8), sem, "qf")
        send(T["sh%d" % t][:, a:b], T["sf%d" % t][:, a:b], sem, "qf")
        writer["hq%d" % h] = (sem, 2 * neng, {})

    for t in range(R):
        def at(place):
            if t == 0:
                for n in ONCE.get(place, "").split():
                    once[n]()
        last = t == R - 1
        for h in (0, 1):
            mm("k%d" % h, "u16", 0, "x", 128 * h, 128 * h + 128, "qu16 su16 qx%d" % h)
        for b in range(3):
            unpack(b, 0)
        for h in (0, 1):
            V(ts(T.fl[:, 512 * h:512 * h + 512:4], T["k%d" % h][:, 0:128], 0.0, None, A.is_le), "k%d" % h, "u1%d" % h)
        quant("1", T.fl[:, 0:512], 0, 128, "u10 zero", "q10")
        mm("k2", "c", 0, "1", 0, 128, "qc0 q10")
        quant("1", T.fl[:, 512:1024], 128, 256, "u11 zero", "q11")
        mm("k3", "c", 0, "1", 128, 256, "qc0 q11")
        unpack(3, 0, "T")
        V(scan(T.su1s[:], T.hold16[:], u1, 0.0, A.add, A.min), "hold16 u10 u11", "su1")
        at("scored")
        V(scan(T.known[:], T.unit[:], u1, -1.0, A.add, A.subtract), "unit u10 u11", "known")
        V(tt(Y("l1"), T["m2%d" % t][:], T.su1s[:, end16], A.subtract), "m2%d su1" % t, "l1")
        at("listing")
        act(Y("d2"), T.su1s[:, end16], "su1 cd", "d2", IDENT, scale=M, bias=col(CD))
        act(T.win[:, 0:256:2], T.k2[:, 0:128], "k2", "wa", SIGN, bias=-0.875)
        act(T.win[:, 256:512:2], T.k3[:, 0:128], "k3", "wb", SIGN, bias=-0.875)
        unpack(3, 0, "A")
        V(keep(T.sk[:], T.known[:]), "pa known", "sk")
        V(cp(T.list1[:], Y("l1")), "l1", "list1")
        V(tt(Y("e1"), T.sk[:, end16], Y("d2"), A.add), "sk d2", "e1")
        for b in range(3):
            unpack(b, 1, "T")
        n = LOOK[0]
        act(T.f2[:, 0:32 * n:2], T.win[:, 0:512].indirect(T.list1[:, 0:n]), "wa wb wz list1", "u2a", RELU)
        V(ts(T.f2[:, 32 * n:512:2], T.win[:, 0:512].indirect(T.list1[:, n:16]), 0.0, None, A.max), "wa wb wz list1", "u2b")
        unpack(3, 1, "T")
        for b in range(4):
            unpack(b, 1, "A")
        if not t:
            act(Y("uc"), T.su1s[:, end16], "su1 cw", "uc", IDENT, bias=col(CW))
        if last:
            act(Y("uc"), T.su1s[:, end16], "su1 c1", "uc", IDENT, scale=2.0, bias=col(C1))
        export(t, 0)
        at("count")
        quant("2", T.f2[:], 0, 128, "u2a u2b fz", "q2")
        mm("k0", "c", 0, "2", 0, 128, "q2")
        mm("k1", "c", 128, "2", 0, 128, "qc2 q2")
        V(scan(T.y2[:, 255::-1], T.f2[:, 510::-2], T.fl[:, 1020::-4], 0.0, A.add, A.subtract), "u2a u2b u10 u11", "y2")
        V(tt(Y("ee"), Y("e1"), Y("far"), A.min), "e1 far", "ee")
        at("behind")
        V(keep(T.sy[:], T.y2[:, 0:256]), "pa y2", "sy")
        V(keep(T.sn[:], T.y2[:, 1:257]), "pa y2 end", "sn")
        at("looked")
        act(col(N2), T.y2[:, 0:1], "y2 cg", "n2", IDENT, scale=-1.0, bias=col(CG))
        act(Y("uu"), T.sy[:, end16], "sy cu", "uu", IDENT, scale=M + 1.0, bias=col(CU))
        act(Y("dn"), T.sn[:, end16], "sn", "dn", scale=-M)
        at("lifted")
        V(tt(T.win[:, 0:512:4], T.k0[:, 0:128], T.win[:, 0:512:4], A.is_lt), "k0 wa wb", "wa")
        V(tt(T.win[:, 2:512:4], T.k1[:, 0:128], T.win[:, 2:512:4], A.is_lt), "k1 wb", "wb")
        export(t, 1)
        at("paired")
        n = LOOK[1]
        act(T.f3[:, 0:16 * n], T.win[:, 0:512].indirect(T.list1[:, 0:n]), "wa wb list1", "f3a", bias=-1.0)
        V(ts(T.f3[:, 16 * n:256], T.win[:, 0:512].indirect(T.list1[:, n:16]), -1.0, None, A.add), "wa wb list1", "f3b")
        V(tt(Y("c2"), Y("uu"), Y("dn"), A.add), "uu dn", "c2")
        at("placed")
        if last:
            V(tt(Y("w1"), T.sy[:, end16], T.sn[:, end16], A.subtract), "sy sn", "w1")
        V(scan(T.pb[:, 510::-2], T.step[:, ::-1], T.f3[:, ::-1], T.y2[:, 0:1], A.add, A.subtract), "step0 step1 step2 step3 f3a f3b y2", "y3")
        V(tt(T.pb[:, 31:512:32], Y("ee"), Y("c2"), A.min), "ee c2", "kk16")
        V(scan(T.pa[:, 1:512:2], T.less16[:], T.f3[:], 0.0, A.min, A.mult), "less16 f3a f3b", "n3")
        act(T.sl[:, 0:96], zeros(96), "zero", "sl", bias=256.0)
        act(T.s4[:], T.f3[:], "f3a f3b", "s4 n3s", accum_out=col(N3))
        act(col(N23), col(N3), "n3s n2", "n23", IDENT, bias=col(N2))
        V(scan(T.u4[:], u2, T.f3[:], 0.0, A.max, A.mult), "u2a u2b f3a f3b", "u4")
        at("third")
        V(scan(T.least[:], T.pa[:], T.pb[:], 0.0, A.add, A.min), "pa n3 y3 kk16", "least")
        at("least")
        V(scan(T.fb[:, 0:512:2], zeros(256), T.u4[:], -1.0, A.add, A.subtract), "zero zero2 u4", "k4")
        if t:
            act(T.fb[:, 1:512:2], T["tab%d" % t][:, 0:512].indirect(T.list1[:, 0:16]), "tab%d list1" % t, "src", bias=-256.0)
        else:
            act(T.fb[:, 1:512:2], T.row[:, 0:256].indirect(T.list2[:, 0:16]), "row list2", "src", bias=-256.0)
        V(ts(T.pos[:], T.least[:, 31:512:32], col(N23), None, A.add), "least n23", "pos")
        V(scan(T.fa[:, 1:512:2], T.own4[:], T.u4[:], 0.0, A.max, A.mult), "own4 u4", "n4")
        at("pos")
        V(cp(T.sl[:, 0:768].indirect(T.pos[:, 0:16]), T.row[:, 0:256]), "pos row", "sl")
        V(scan(T.from4[:, 0:256], T.fa[:, 0:256], T.fb[:, 0:256], 0.0, A.add, A.min), "wr4 n4 k4 src", "from0")
        V(scan(T.ws96[:], T.fa[:, 0:192:2], T.sl[:, 0:96], 0.0, A.add, A.min), "wr4 sl", "ws96")
        V(scan(T.from4[:, 256:512], T.fa[:, 256:512], T.fb[:, 256:512], 0.0, A.add, A.min), "wr4 n4 k4 src", "from1")
        V(ts(T["slot%d" % t][:], T.ws96[:, 3:96:4], 4.0, col(SLOTC), A.mult, A.add), "ws96 slotc", "slot")
        send(T["land%d" % t][:], T["slot%d" % t][:], "al%d" % t, "slot")
        writer["land"] = ("al%d" % t, neng, {})
        for h in (0, 1):
            for b in range(4):
                bank = "bk"[h] + "%d" % b
                mm(bank, "e", 128 * b, "h%d" % t, 128 * h, 128 * h + 128, "hq%d" % h)
                act(T.hh[:, 512 * h + b:512 * h + 512:4], T[bank][:, 0:128], bank, "h%d%d" % (b, h))
        src = T.from4[:, 7:512:8]
        at("chosen")
        V(cp(T.three[:, 0:192:3], src), "from0 from1", "t5")
        V(ts(T.three[:, 1:192:3], src, col(C96), -96.0, A.is_ge, A.mult), "from0 from1 c96", "t6")
        V(ts(T.three[:, 2:192:3], src, col(C192), -96.0, A.is_ge, A.mult), "from0 from1 c192", "t7")
        at("sent")
        if t == R - 2:
            quant("v", T.v0[:], 0, 128, "v0", "qv")
        if last:
            V(ts(Y("l3"), T.least[:, 31:512:32], col(CF), None, A.is_ge), "least cf", "l3")
            V(tt(Y("w2"), Y("w1"), Y("uc"), A.add), "w1 uc", "w2")
        V(scan(T.sums[:], T.anew[:], T.three[:], 0.0, A.mult, A.add), "anew t5 t6 t7", "gn")
        at("travel")
        if last:
            V(tt(T.wave[:, 0:16], Y("w2"), Y("l3"), A.add), "w2 l3", "wave")
        V(ts(T.off[:], T.sums[:, 2:192:3], 4.0, col(OFFC), A.mult, A.add), "gn offc", "off")
        at("listed")
        r = "h00 h10 h20 h30 h01 h11 h21 h31 hz land"
        a = GUESTS[min(t, 1)]
        if a:
            V(cp(T.fg[:, 0:16 * a], T.hh[:, 0:1040].indirect(T["land%d" % t][:, 0:a])), r, "g0")
        act(T.fg[:, 16 * a:384], T.hh[:, 0:1040].indirect(T["land%d" % t][:, a:24]), r, "g1" if a else "g0 g1")
        at("guests")
        if last:
            V(lambda: g.vector.transpose(T.turned[:], T.wave[:]), "wave wz2", "turned")
            for k in range(8):
                dma("S", T.wv[k, :], T.turned[32 * (k // 2):32 * (k // 2) + 16, 16 * (k % 2):16 * (k % 2) + 16], "st", "turned")
        r = " ".join(fs) + " g0 g1 off"
        for h in (0, 1):
            a, m, e = FILL[h]
            V(cp(T.z[:, 16 * a:16 * m], T.fg[:, 0:1408].indirect(T.off[:, a:m])), r, "zv%d" % h)
            act(T.z[:, 16 * m:16 * e], T.fg[:, 0:1408].indirect(T.off[:, m:e]), r, "za%d" % h)
            if h:
                scale_z(SCALE[:EARLY])
            else:
                V(cp(T.z[:, 512:16 * FILL[1][0]], T.fg[:, 0:1408].indirect(T.off[:, 32:FILL[1][0]])), r, "zw")
                at("half")
            quant("z", T.z[:, 512 * h:512 * h + 512], 128 * h, 128 * h + 128, "zv%d za%d" % (h, h), "qz%d" % h)
            for b, k in (SUMS[FIRST:] if h else SUMS[:FIRST]):
                mm("bk"[k] + "%d" % b, "w", 128 * b, "z", 128 * k, 128 * k + 128, "qw sw qz%d" % k)
        scale_z(SCALE[EARLY:])
        at("sums")
        for b, h in SUMS:
            bank, a = "bk"[h] + "%d" % b, 512 * h + 128 * b
            V(tt(T["tt%d" % b][:, 128 * h:128 * h + 128], T[bank][:, 0:128], T.z32[:, a:a + 128], A.add), bank + " y%d%d" % (b, h), "tt%d%d" % (b, h))
        for q, b, a, e in SHARES:
            if q == "Q":
                if last and b:
                    store_y(0)
                quant_x(b, T.xt, " ".join("xs%d%d" % (k[1], k[2]) for k in SHARES if k[0] != "Q" and k[2] < e and k[3] > a))
                if last:
                    dma("S", T.oc[:, 512 * b:512 * b + 512], T.qx[:, 128 * b:128 * b + 128].bitcast(dt.uint8), "st", "qx%d" % b)
                    mm("k%d" % b, "v", 0, "x", 128 * b, 128 * b + 128, "qv qx%d" % b)
                continue
            src = T["tt%d" % b][:, 0:256].indirect(T["inv%d" % t][:, a:e])
            out, r, w = T.xt[:, 64 * a + b:64 * e:4], "tt%d0 tt%d1 inv%d" % (b, b, t), "xs%d%d" % (b, a)
            if q == "V":
                V(ts(out, src, 0.03125, None, A.mult), r, w)
            else:
                act(out, src, r, w, scale=0.03125)
    for k in range(4):
        dma("AS"[k // 2], T.osc[4 * k:4 * k + 4, :], T.sx[32 * k:32 * k + 4, :], ("st2", "st")[k // 2], "qx0 qx1")
    store_y(1)
    g.wait_ge(T.sem.loc, 5 * R * neng)
    for s in sorted(count, key=lambda n: n == "st"):
        g.wait_ge(T.sem[s], count[s])
